import numpy as np
import ml_dtypes


def mxq(x, axis, fmt="e4m3"):
    dtype, down = {"e4m3": (ml_dtypes.float8_e4m3fn, 7), "e5m2": (ml_dtypes.float8_e5m2, 14)}[fmt]
    v = np.moveaxis(np.asarray(x, np.float32).astype(ml_dtypes.bfloat16).astype(np.float64), axis, -1)
    blocks = v.reshape(v.shape[:-1] + (-1, 32))
    amax = np.abs(blocks).max(-1, keepdims=True)
    byte = np.maximum(np.where(amax > 0, np.frexp(amax)[1] - 1 + 127, 0) - down, 1)
    scale = np.exp2(byte - 127.0)
    codes = (blocks / scale).astype(np.float32).astype(dtype).astype(np.float64)
    return np.moveaxis((codes * scale).reshape(v.shape), -1, axis)


WIDE = False


def mx_kscale(k):
    if not WIDE:
        return np.ones(k)
    levels = np.array([10, -10, 5, -5, 0])
    if k % 512:
        return np.exp2(np.random.permutation(np.resize(levels, k // 32))).repeat(32)
    a = np.empty((k // 512, 16))
    for p in range(k // 512):
        a[p, :8] = np.random.permutation(np.resize(levels, 8))
        for g in range(8):
            far = levels[np.abs(levels - a[p, g]) >= 10]
            a[p, g + 8] = far[np.random.randint(len(far))]
    return np.exp2(a.ravel()).repeat(32)


def f64(x):
    return np.asarray(x).astype(np.float64)


def striped(idx):
    return np.tile(idx.reshape(-1, 16).T, (8, 1)).astype(np.uint16)


def unstriped(offs):
    return offs[:16].T.reshape(-1).astype(np.int64)


E2M1 = np.array([0.0, 0.5, 1.0, 1.5, 2.0, 3.0, 4.0, 6.0, -0.0, -0.5, -1.0, -1.5, -2.0, -3.0, -4.0, -6.0])


def pack_weight(w, fmt):
    k, n = w.shape
    w = f64(np.asarray(w, np.float32).astype(ml_dtypes.bfloat16)).reshape(k // 32, 32, n)
    amax = np.abs(w).max(1)
    if fmt == "e4m3":
        byte = np.frexp(amax)[1] - 1 + 127 - 7
    else:
        mant, ex = np.frexp(amax / 6.0)
        byte = np.where(mant > 0.5, ex, ex - 1) + 127
    byte = np.clip(np.where(amax > 0, byte, 1), 1, 254)
    scaled = (w * np.exp2(127.0 - byte)[:, None, :]).reshape(k, n).astype(np.float32)
    by_word = np.ascontiguousarray(scaled.reshape(k // 512, 128, 4, n).transpose(0, 1, 3, 2))
    if fmt == "e4m3":
        words = by_word.astype(ml_dtypes.float8_e4m3fn).view(np.uint8)
    else:
        c = by_word.astype(ml_dtypes.float4_e2m1fn).view(np.uint8) & 0xF
        words = (c[..., 0::2] | (c[..., 1::2] << 4)).reshape(k // 512, 128, 2 * n)
    return np.ascontiguousarray(words), np.ascontiguousarray(byte.astype(np.uint8).reshape(k // 512, 16, n))


def unpack_weight(words, scales, fmt):
    g, _, n = scales.shape
    words = np.ascontiguousarray(words).reshape(g, 128, n, -1)
    if fmt == "e4m3":
        vals = words.view(ml_dtypes.float8_e4m3fn).astype(np.float64)
    else:
        nib = np.empty((g, 128, n, 4), np.uint8)
        nib[..., 0::2] = words & 0xF
        nib[..., 1::2] = words >> 4
        vals = E2M1[nib]
    vals = vals * np.repeat(np.exp2(scales.astype(np.float64) - 127.0), 8, axis=1)[..., None]
    return vals.transpose(0, 1, 3, 2).reshape(g * 512, n)


def d_relu2(v):
    return 2.0 * np.maximum(v, 0.0)


K, T, E, C, H, N = 256, 1024, 4, 256, 512, 1536


def by_expert(wq, xq):
    return np.concatenate([wq[e].T @ xq[:, e * C:(e + 1) * C] for e in range(E)], axis=1)


def setup_inputs():
    n = np.random.standard_normal
    v = mx_kscale(N)
    u = mx_kscale(H)
    slot_token = np.random.permutation(T)[:E * C]
    w_slot = np.random.uniform(0.2, 1.0, E * C)
    dy = pack_weight(n((N, T)) * v[:, None], "e4m3")
    wt = pack_weight(n((N, K)) / np.sqrt(N) / v[:, None], "e2m1")
    return {
        "dy_words": dy[0],
        "dy_scales": dy[1],
        "wt_words": wt[0],
        "wt_scales": wt[1],
        "wbt": (n((E, N, H)) / np.sqrt(N) / v[None, :, None] * u).astype(np.float32),
        "wat": (n((E, H, K)) / np.sqrt(H) / u[None, :, None]).astype(np.float32),
        "a": (n((H, E * C))).astype(np.float32),
        "gate": (np.tile(w_slot, (128, 1))).astype(np.float32),
        "offs": striped(slot_token),
    }


def reference(dy_words, dy_scales, wt_words, wt_scales, wbt, wat, a, gate, offs):
    wt = unpack_weight(wt_words, wt_scales, "e2m1")
    wbtq = mxq(f64(wbt), 1, "e4m3")
    watq = mxq(f64(wat), 1, "e4m3")
    idx = unstriped(offs)
    dy = unpack_weight(dy_words, dy_scales, "e4m3")
    base = wt.T @ dy
    dh = f64(gate[:1]) * by_expert(wbtq, dy[:, idx]) * d_relu2(f64(a))
    dx = by_expert(watq, mxq(dh, 0, "e4m3"))
    c = np.zeros((K, T))
    c[:, idx] = dx
    return base + c

@@ -1,0 +1,260 @@
+from contextlib import ExitStack
+
+import concourse.mybir as mybir
+
+K, T, E, C, H, N = 256, 1024, 4, 256, 512, 1536
+FLOPS = 2 * N * K * T + 2 * E * C * (N * H + H * K)
+
+F32 = mybir.dt.float32
+BF16 = mybir.dt.bfloat16
+I32 = mybir.dt.int32
+U32 = mybir.dt.uint32
+U16 = mybir.dt.uint16
+U8 = mybir.dt.uint8
+FP8X4 = mybir.dt.float8_e4m3fn_x4
+FP4X4 = mybir.dt.float4_e2m1fn_x4
+ALU = mybir.AluOpType
+
+P = 128
+PACK = 4
+PASS = P * PACK
+PASSES = N // PASS
+BANK = 512
+LIST_COLS = C // 16
+
+
+def tile_moe_adb_relu2_kernel(
+    tc, dy_words, dy_scales, wt_words, wt_scales, wbt, wat, a, gate, offs, out
+):
+    nc = tc.nc
+    with ExitStack() as ctx:
+        held = ctx.enter_context(tc.tile_pool(name="held", bufs=1))
+        ring = ctx.enter_context(tc.tile_pool(name="ring", bufs=2))
+        psum = ctx.enter_context(tc.psum_pool(name="psum", bufs=2))
+
+        def keep(name, shape, dtype):
+            return held.tile(shape, dtype, name=name, align_bytes=64)
+
+        offsets = held.tile([P, T // 16], U16, name="offsets")
+        dy = [keep("dy%d" % s, [P, T], I32) for s in range(PASSES)]
+        dy_packed = keep("dy_packed", [P, T], U8)
+        dy_plane = keep("dy_plane", [P, PASSES, T], U8)
+        wt_codes = keep("wt_codes", [P, PASSES, 2 * K], U8)
+        wt_plane = keep("wt_plane", [P, PASSES, K], U8)
+        slot_words = [keep("slot_words%d" % s, [P, E * C], I32) for s in range(PASSES)]
+        slot_scales = keep("slot_scales", [P, E * C], U8)
+        window = [keep("window%d" % kt, [P, T], F32) for kt in range(K // P)]
+
+        nc.vector.memset(dy_packed[:].bitcast(I32), 0)
+        nc.vector.memset(dy_plane[:].rearrange("p s t -> p (s t)").bitcast(I32), 0)
+        nc.vector.memset(wt_plane[:].rearrange("p s k -> p (s k)").bitcast(I32), 0)
+
+        wb_raw = {}
+        a_sb, gate_sb, wa_raw = {}, {}, {}
+
+        def load_wb(e, s, pieces):
+            width = H // pieces
+            rows = wbt[e, s * PASS : (s + 1) * PASS, :].rearrange("(p j) c -> p j c", j=PACK)
+            wb_raw[e, s] = []
+            for q in range(pieces):
+                raw = keep("wb_raw%d_%d_%d" % (e, s, q), [P, PACK, width], F32)
+                nc.sync.dma_start(out=raw[:], in_=rows[:, :, q * width : (q + 1) * width])
+                wb_raw[e, s].append(raw)
+
+        def load_dy(s):
+            nc.sync.dma_start(out=dy[s][:], in_=dy_words[s].rearrange("p t d -> p (t d)").bitcast(I32))
+
+        def load_a(e):
+            a_sb[e] = keep("a%d" % e, [P, PACK, C], F32)
+            nc.sync.dma_start(
+                out=a_sb[e][:], in_=a.rearrange("(p t) j -> p t j", t=PACK)[:, :, e * C : (e + 1) * C]
+            )
+
+        def load_gate(e):
+            gate_sb[e] = keep("gate%d" % e, [P, C], F32)
+            nc.sync.dma_start(out=gate_sb[e][:], in_=gate[:, e * C : (e + 1) * C])
+
+        def load_wa(e):
+            wa_raw[e] = keep("wa_raw%d" % e, [P, PACK, K], F32)
+            nc.sync.dma_start(out=wa_raw[e][:], in_=wat[e].rearrange("(p j) k -> p j k", j=PACK))
+
+        load_wb(0, 0, 2)
+        nc.sync.dma_start(offsets[:], offs)
+        load_dy(0)
+        for quad in range(4):
+            nc.sync.dma_start(
+                out=dy_packed[32 * quad : 32 * quad + 4 * PASSES, :].bitcast(I32),
+                in_=dy_scales[:, 4 * quad : 4 * quad + 4, :].bitcast(I32),
+            )
+        load_wb(0, 1, 1)
+        load_dy(1)
+        load_wb(0, 2, 1)
+        load_dy(2)
+        load_gate(0)
+        load_a(0)
+        for e in range(1, E):
+            load_wb(e, 0, 1)
+            load_wa(e - 1)
+            load_gate(e)
+            load_wb(e, 1, 1)
+            if e < E - 1:
+                load_a(e)
+                load_wb(e, 2, 1)
+            else:
+                load_wb(e, 2, 2)
+                load_a(e)
+                load_wa(e)
+        for quad in range(4):
+            nc.sync.dma_start(
+                out=dy_plane[32 * quad : 32 * quad + 4, :, :].bitcast(I32),
+                in_=dy_scales[:, 4 * quad : 4 * quad + 4, :].rearrange("s r t -> r s t").bitcast(I32),
+            )
+            nc.sync.dma_start(
+                out=wt_plane[32 * quad : 32 * quad + 4, :, :].bitcast(I32),
+                in_=wt_scales[:, 4 * quad : 4 * quad + 4, :].rearrange("s r k -> r s k").bitcast(I32),
+            )
+        nc.sync.dma_start(out=wt_codes[:].bitcast(I32), in_=wt_words.rearrange("s p b -> p s b").bitcast(I32))
+
+        wb_codes, wb_plane, wa_codes, wa_plane, factor, dh = {}, {}, {}, {}, {}, {}
+
+        def expert_offsets(e):
+            return offsets[:, e * LIST_COLS : (e + 1) * LIST_COLS]
+
+        def gather(e):
+            slots = slice(e * C, (e + 1) * C)
+            for s in range(PASSES):
+                nc.vector.tensor_copy(
+                    slot_words[s][:, slots].bitcast(U32), dy[s][:].bitcast(U32).indirect(expert_offsets(e))
+                )
+            nc.vector.tensor_copy(slot_scales[:, slots], dy_packed[:].indirect(expert_offsets(e)))
+
+        def quantize_wb(e, s):
+            grouped = ring.tile([P, PACK, P, PACK], BF16, name="wb_grouped", align_bytes=64, bufs=3)
+            pieces = wb_raw[e, s]
+            span = P // len(pieces)
+            for q, raw in enumerate(pieces):
+                nc.scalar.copy(
+                    out=grouped[:, :, q * span : (q + 1) * span, :].rearrange("p t m j -> p m j t"),
+                    in_=raw[:].rearrange("p j (m t) -> p m j t", t=PACK),
+                )
+            wb_codes[e, s] = ring.tile([P, H], U32, name="wb_codes", align_bytes=64, bufs=2 * PASSES)
+            wb_plane[e, s] = ring.tile([P, H], U8, name="wb_plane", align_bytes=64, bufs=2 * PASSES)
+            nc.vector.quantize_mx(
+                out=wb_codes[e, s][:].bitcast(FP8X4),
+                scales=wb_plane[e, s][:],
+                in_=grouped[:].rearrange("p t m j -> p (t m j)"),
+            )
+
+        def quantize_wa(e):
+            grouped = ring.tile([P, K, PACK], BF16, name="wa_grouped", align_bytes=64)
+            nc.scalar.copy(
+                out=grouped[:].rearrange("p (c i) j -> p c j i", i=4),
+                in_=wa_raw[e][:].rearrange("p j (c i) -> p c j i", i=4),
+            )
+            wa_codes[e] = keep("wa_codes%d" % e, [P, K], U32)
+            wa_plane[e] = keep("wa_plane%d" % e, [P, K], U8)
+            nc.vector.quantize_mx(
+                out=wa_codes[e][:].bitcast(FP8X4),
+                scales=wa_plane[e][:],
+                in_=grouped[:].rearrange("p k j -> p (k j)"),
+            )
+
+        def make_factor(e):
+            gate2 = keep("gate2_%d" % e, [P, C], F32)
+            nc.gpsimd.tensor_scalar(
+                out=gate2[:], in0=gate_sb[e][:], scalar1=2.0, scalar2=0.0, op0=ALU.mult, op1=ALU.add
+            )
+            factor[e] = ring.tile([P, PACK, C], F32, name="factor", align_bytes=64)
+            nc.vector.scalar_tensor_tensor(
+                out=factor[e][:],
+                in0=a_sb[e][:],
+                scalar=0.0,
+                in1=gate2[:].unsqueeze(1).to_broadcast([P, PACK, C]),
+                op0=ALU.max,
+                op1=ALU.mult,
+            )
+
+        def first_product(e):
+            dh[e] = ring.tile([P, C, PACK], BF16, name="dh", align_bytes=64)
+            for half in range(C // P):
+                sums = psum.tile([P, PACK, P], F32, name="sums")
+                cols = slice(e * C + half * P, e * C + (half + 1) * P)
+                for t in range(PACK):
+                    for s in range(PASSES):
+                        nc.tensor.matmul_mx(
+                            out=sums[:, t, :],
+                            lhsT=wb_codes[e, s][:, t * P : (t + 1) * P].bitcast(FP8X4),
+                            lhsT_scale=wb_plane[e, s][:, t * P : (t + 1) * P],
+                            rhs=slot_words[s][:, cols].bitcast(FP8X4),
+                            rhs_scale=slot_scales[4 * s :, cols],
+                            start=(s == 0),
+                            stop=(s == PASSES - 1),
+                        )
+                nc.vector.tensor_tensor(
+                    out=dh[e][:, half * P : (half + 1) * P, :].rearrange("p (c i) t -> p c t i", i=4),
+                    in0=sums[:].rearrange("p t (c i) -> p c t i", i=4),
+                    in1=factor[e][:, :, half * P : (half + 1) * P].rearrange("p t (c i) -> p c t i", i=4),
+                    op=ALU.mult,
+                )
+
+        def second_product(e):
+            dh_codes = ring.tile([P, C], U32, name="dh_codes", align_bytes=64)
+            dh_plane = ring.tile([P, C], U8, name="dh_plane", align_bytes=64)
+            nc.vector.quantize_mx(
+                out=dh_codes[:].bitcast(FP8X4), scales=dh_plane[:], in_=dh[e][:].rearrange("p c t -> p (c t)")
+            )
+            for kt in range(K // P):
+                acc = psum.tile([P, BANK], F32, name="acc")
+                nc.tensor.matmul_mx(
+                    out=acc[:, :C],
+                    lhsT=wa_codes[e][:, kt * P : (kt + 1) * P].bitcast(FP8X4),
+                    lhsT_scale=wa_plane[e][:, kt * P : (kt + 1) * P],
+                    rhs=dh_codes[:].bitcast(FP8X4),
+                    rhs_scale=dh_plane[:],
+                    start=True,
+                    stop=True,
+                )
+                dx = ring.tile([P, C], F32, name="dx%d" % kt, align_bytes=64)
+                nc.scalar.copy(out=dx[:], in_=acc[:, :C])
+                dxs[e, kt] = dx
+
+        dxs = {}
+
+        def scatter(e, kt):
+            nc.vector.tensor_copy(window[kt][:].indirect(expert_offsets(e)), dxs[e, kt][:])
+
+        def finish(kt):
+            for h in range(T // BANK):
+                cols = slice(h * BANK, (h + 1) * BANK)
+                acc = psum.tile([P, BANK], F32, name="acc")
+                for s in range(PASSES):
+                    nc.tensor.matmul_mx(
+                        out=acc[:],
+                        lhsT=wt_codes[:, s, 2 * kt * P : 2 * (kt + 1) * P].bitcast(FP4X4),
+                        lhsT_scale=wt_plane[:, s, kt * P : (kt + 1) * P],
+                        rhs=dy[s][:, cols].bitcast(FP8X4),
+                        rhs_scale=dy_plane[:, s, cols],
+                        start=(s == 0),
+                        stop=(s == PASSES - 1),
+                    )
+                nc.vector.tensor_tensor(out=window[kt][:, cols], in0=acc[:], in1=window[kt][:, cols], op=ALU.add)
+                nc.sync.dma_start(out=out[kt * P : (kt + 1) * P, cols], in_=window[kt][:, cols])
+
+        for e in range(E):
+            quantize_wb(e, 0)
+            if e > 0:
+                quantize_wa(e - 1)
+                second_product(e - 1)
+            gather(e)
+            quantize_wb(e, 1)
+            if e > 0:
+                for kt in range(K // P):
+                    scatter(e - 1, kt)
+            quantize_wb(e, 2)
+            make_factor(e)
+            first_product(e)
+        quantize_wa(E - 1)
+        second_product(E - 1)
+        for kt in range(K // P):
+            scatter(E - 1, kt)
+            finish(kt)

@@ -1,3 +1,4 @@
+import math
 from contextlib import ExitStack
 
 import concourse.mybir as mybir
@@ -21,6 +22,16 @@ PASS = P * PACK
 PASSES = N // PASS
 BANK = 512
 LIST_COLS = C // 16
+STAGES = 4
+EVAC_V = True
+F_POOL = 0
+WA_POOL = 0
+TAILV = False
+EARLY2 = True
+HEAD = "d0 w0 d1 s w1 d2 g w2 a A".split()
+HEADV = "d0 q0 d1 s q1 d2 q2".split()
+GATHER = 512
+EVAC_AFTER = 0
 
 
 def tile_moe_adb_relu2_kernel(
@@ -46,8 +57,6 @@ def tile_moe_adb_relu2_kernel(
         window = [keep("window%d" % kt, [P, T], F32) for kt in range(K // P)]
 
         nc.vector.memset(dy_packed[:].bitcast(I32), 0)
-        nc.vector.memset(dy_plane[:].rearrange("p s t -> p (s t)").bitcast(I32), 0)
-        nc.vector.memset(wt_plane[:].rearrange("p s k -> p (s k)").bitcast(I32), 0)
 
         wb_raw = {}
         a_sb, gate_sb, wa_raw = {}, {}, {}
@@ -78,32 +87,45 @@ def tile_moe_adb_relu2_kernel(
             wa_raw[e] = keep("wa_raw%d" % e, [P, PACK, K], F32)
             nc.sync.dma_start(out=wa_raw[e][:], in_=wat[e].rearrange("(p j) k -> p j k", j=PACK))
 
-        load_wb(0, 0, 2)
+        def load_packed_scales():
+            for quad in range(4):
+                nc.sync.dma_start(
+                    out=dy_packed[32 * quad : 32 * quad + 4 * PASSES, :].bitcast(I32),
+                    in_=dy_scales[:, 4 * quad : 4 * quad + 4, :].bitcast(I32),
+                )
+
+        nc.gpsimd.memset(dy_plane[:].rearrange("p s t -> p (s t)").bitcast(I32), 0)
+        nc.gpsimd.memset(wt_plane[:].rearrange("p s k -> p (s k)").bitcast(I32), 0)
         nc.sync.dma_start(offsets[:], offs)
-        load_dy(0)
-        for quad in range(4):
-            nc.sync.dma_start(
-                out=dy_packed[32 * quad : 32 * quad + 4 * PASSES, :].bitcast(I32),
-                in_=dy_scales[:, 4 * quad : 4 * quad + 4, :].bitcast(I32),
-            )
-        load_wb(0, 1, 1)
-        load_dy(1)
-        load_wb(0, 2, 1)
-        load_dy(2)
-        load_gate(0)
-        load_a(0)
+        for item in HEAD:
+            if item[0] == "d":
+                load_dy(int(item[1]))
+            elif item[0] == "w":
+                load_wb(0, int(item[1]), 2 if item[1] == "0" else 1)
+            elif item == "s":
+                load_packed_scales()
+            elif item == "g":
+                load_gate(0)
+            elif item == "a":
+                load_a(0)
+            elif item == "A":
+                load_wa(0)
         for e in range(1, E):
+            if e < F_POOL:
+                load_gate(e)
+                load_a(e)
             load_wb(e, 0, 1)
-            load_wa(e - 1)
-            load_gate(e)
-            load_wb(e, 1, 1)
-            if e < E - 1:
-                load_a(e)
-                load_wb(e, 2, 1)
-            else:
-                load_wb(e, 2, 2)
-                load_a(e)
+            if e < WA_POOL:
                 load_wa(e)
+            load_wb(e, 1, 1)
+            if e >= F_POOL:
+                load_gate(e)
+            load_wb(e, 2, 2 if e == E - 1 else 1)
+            if e >= F_POOL:
+                load_a(e)
+            if e >= WA_POOL:
+                load_wa(e)
+        nc.sync.dma_start(out=wt_codes[:].bitcast(I32), in_=wt_words.rearrange("s p b -> p s b").bitcast(I32))
         for quad in range(4):
             nc.sync.dma_start(
                 out=dy_plane[32 * quad : 32 * quad + 4, :, :].bitcast(I32),
@@ -113,27 +135,28 @@ def tile_moe_adb_relu2_kernel(
                 out=wt_plane[32 * quad : 32 * quad + 4, :, :].bitcast(I32),
                 in_=wt_scales[:, 4 * quad : 4 * quad + 4, :].rearrange("s r k -> r s k").bitcast(I32),
             )
-        nc.sync.dma_start(out=wt_codes[:].bitcast(I32), in_=wt_words.rearrange("s p b -> p s b").bitcast(I32))
 
         wb_codes, wb_plane, wa_codes, wa_plane, factor, dh = {}, {}, {}, {}, {}, {}
 
         def expert_offsets(e):
             return offsets[:, e * LIST_COLS : (e + 1) * LIST_COLS]
 
-        def gather(e):
-            slots = slice(e * C, (e + 1) * C)
-            for s in range(PASSES):
+        def gather(into, source):
+            for g in range(0, E * C, GATHER):
                 nc.vector.tensor_copy(
-                    slot_words[s][:, slots].bitcast(U32), dy[s][:].bitcast(U32).indirect(expert_offsets(e))
+                    into[:, g : g + GATHER], source.indirect(offsets[:, g // 16 : (g + GATHER) // 16])
                 )
-            nc.vector.tensor_copy(slot_scales[:, slots], dy_packed[:].indirect(expert_offsets(e)))
+
+        staged = [keep("staged%d" % b, [P, PACK * H], BF16) for b in range(STAGES)]
 
         def quantize_wb(e, s):
-            grouped = ring.tile([P, PACK, P, PACK], BF16, name="wb_grouped", align_bytes=64, bufs=3)
+            flat = staged[(PASSES * e + s) % STAGES]
+            grouped = flat[:].rearrange("p (t m j) -> p t m j", t=PACK, j=PACK)
             pieces = wb_raw[e, s]
             span = P // len(pieces)
             for q, raw in enumerate(pieces):
-                nc.scalar.copy(
+                copy = nc.vector.tensor_copy if TAILV and (e, s, q) == (E - 1, PASSES - 1, 1) else nc.scalar.copy
+                copy(
                     out=grouped[:, :, q * span : (q + 1) * span, :].rearrange("p t m j -> p m j t"),
                     in_=raw[:].rearrange("p j (m t) -> p m j t", t=PACK),
                 )
@@ -142,21 +165,30 @@ def tile_moe_adb_relu2_kernel(
             nc.vector.quantize_mx(
                 out=wb_codes[e, s][:].bitcast(FP8X4),
                 scales=wb_plane[e, s][:],
-                in_=grouped[:].rearrange("p t m j -> p (t m j)"),
+                in_=flat[:],
             )
 
         def quantize_wa(e):
-            grouped = ring.tile([P, K, PACK], BF16, name="wa_grouped", align_bytes=64)
-            nc.scalar.copy(
-                out=grouped[:].rearrange("p (c i) j -> p c j i", i=4),
-                in_=wa_raw[e][:].rearrange("p j (c i) -> p c j i", i=4),
-            )
+            if e < WA_POOL:
+                flat = keep("wa_staged%d" % e, [P, PACK * K], BF16)[:]
+                nc.gpsimd.tensor_scalar(
+                    out=flat.rearrange("p (k j) -> p k j", j=PACK),
+                    in0=wa_raw[e][:].rearrange("p j k -> p k j"),
+                    scalar1=1.0, scalar2=0.0, op0=ALU.mult, op1=ALU.add,
+                )
+            else:
+                spent = wb_raw[e, PASSES - 1][-1][:].rearrange("p j c -> p (j c)")
+                flat = spent[:, spent.shape[1] - PACK * K // 2 :].bitcast(BF16)
+                nc.scalar.copy(
+                    out=flat.rearrange("p (c i j) -> p c j i", i=4, j=PACK),
+                    in_=wa_raw[e][:].rearrange("p j (c i) -> p c j i", i=4),
+                )
             wa_codes[e] = keep("wa_codes%d" % e, [P, K], U32)
             wa_plane[e] = keep("wa_plane%d" % e, [P, K], U8)
             nc.vector.quantize_mx(
                 out=wa_codes[e][:].bitcast(FP8X4),
                 scales=wa_plane[e][:],
-                in_=grouped[:].rearrange("p k j -> p (k j)"),
+                in_=flat,
             )
 
         def make_factor(e):
@@ -164,9 +196,18 @@ def tile_moe_adb_relu2_kernel(
             nc.gpsimd.tensor_scalar(
                 out=gate2[:], in0=gate_sb[e][:], scalar1=2.0, scalar2=0.0, op0=ALU.mult, op1=ALU.add
             )
-            factor[e] = ring.tile([P, PACK, C], F32, name="factor", align_bytes=64)
+            if e < F_POOL:
+                factor[e] = a_sb[e][:]
+                for t in range(PACK):
+                    nc.gpsimd.tensor_scalar(
+                        out=a_sb[e][:, t, :], in0=a_sb[e][:, t, :], scalar1=math.inf, scalar2=0.0, op0=ALU.min, op1=ALU.max
+                    )
+                    nc.gpsimd.tensor_tensor(out=a_sb[e][:, t, :], in0=a_sb[e][:, t, :], in1=gate2[:], op=ALU.mult)
+                return
+            spent = wb_raw[e, PASSES - 1][0][:].rearrange("p j c -> p (j c)")
+            factor[e] = spent[:, : PACK * C].rearrange("p (t j) -> p t j", t=PACK)
             nc.vector.scalar_tensor_tensor(
-                out=factor[e][:],
+                out=factor[e],
                 in0=a_sb[e][:],
                 scalar=0.0,
                 in1=gate2[:].unsqueeze(1).to_broadcast([P, PACK, C]),
@@ -214,14 +255,18 @@ def tile_moe_adb_relu2_kernel(
                     start=True,
                     stop=True,
                 )
-                dx = ring.tile([P, C], F32, name="dx%d" % kt, align_bytes=64)
-                nc.scalar.copy(out=dx[:], in_=acc[:, :C])
+                dx = wb_raw[min(e + 1, E - 1), EVAC_AFTER][0][:, kt, :C]
+                if EVAC_V and e < E - 1:
+                    dx = ring.tile([P, C], F32, name="dx%d" % kt, align_bytes=64)[:]
+                    nc.vector.tensor_copy(out=dx, in_=acc[:, :C])
+                else:
+                    nc.scalar.copy(out=dx, in_=acc[:, :C])
                 dxs[e, kt] = dx
 
         dxs = {}
 
         def scatter(e, kt):
-            nc.vector.tensor_copy(window[kt][:].indirect(expert_offsets(e)), dxs[e, kt][:])
+            nc.vector.tensor_copy(window[kt][:].indirect(expert_offsets(e)), dxs[e, kt])
 
         def finish(kt):
             for h in range(T // BANK):
@@ -240,20 +285,27 @@ def tile_moe_adb_relu2_kernel(
                 nc.vector.tensor_tensor(out=window[kt][:, cols], in0=acc[:], in1=window[kt][:, cols], op=ALU.add)
                 nc.sync.dma_start(out=out[kt * P : (kt + 1) * P, cols], in_=window[kt][:, cols])
 
+        for item in HEADV:
+            if item[0] == "d":
+                gather(slot_words[int(item[1])][:].bitcast(U32), dy[int(item[1])][:].bitcast(U32))
+            elif item == "s":
+                gather(slot_scales[:], dy_packed[:])
+            else:
+                quantize_wb(0, int(item[1]))
         for e in range(E):
-            quantize_wb(e, 0)
             if e > 0:
-                quantize_wa(e - 1)
-                second_product(e - 1)
-            gather(e)
-            quantize_wb(e, 1)
-            if e > 0:
+                if EARLY2:
+                    second_product(e - 1)
+                quantize_wb(e, 0)
+                if not EARLY2:
+                    second_product(e - 1)
                 for kt in range(K // P):
                     scatter(e - 1, kt)
-            quantize_wb(e, 2)
+                quantize_wb(e, 1)
+                quantize_wb(e, 2)
             make_factor(e)
             first_product(e)
-        quantize_wa(E - 1)
+            quantize_wa(e)
         second_product(E - 1)
         for kt in range(K // P):
             scatter(E - 1, kt)

@@ -22,16 +22,19 @@ PASS = P * PACK
 PASSES = N // PASS
 BANK = 512
 LIST_COLS = C // 16
-STAGES = 4
+SPLIT_DX = False
 EVAC_V = True
 F_POOL = 0
 WA_POOL = 0
 TAILV = False
 EARLY2 = True
-HEAD = "d0 w0 d1 s w1 d2 g w2 a A".split()
-HEADV = "d0 q0 d1 s q1 d2 q2".split()
+HEAD = "d0 w0 s d1 w1 d2 g w2 a A".split()
+HEADV = "d0 s q0 d1 q1 d2 q2".split()
 GATHER = 512
-EVAC_AFTER = 0
+STAGES = 6
+EVAC_AFTER = [-1, 1, 1]
+HALVES = [3]
+CODES2 = 1
 
 
 def tile_moe_adb_relu2_kernel(
@@ -41,7 +44,7 @@ def tile_moe_adb_relu2_kernel(
     with ExitStack() as ctx:
         held = ctx.enter_context(tc.tile_pool(name="held", bufs=1))
         ring = ctx.enter_context(tc.tile_pool(name="ring", bufs=2))
-        psum = ctx.enter_context(tc.psum_pool(name="psum", bufs=2))
+        psum = ctx.enter_context(tc.psum_pool(name="psum", bufs=1))
 
         def keep(name, shape, dtype):
             return held.tile(shape, dtype, name=name, align_bytes=64)
@@ -58,17 +61,17 @@ def tile_moe_adb_relu2_kernel(
 
         nc.vector.memset(dy_packed[:].bitcast(I32), 0)
 
-        wb_raw = {}
+        wb_raw, wb_pieces = {}, {}
         a_sb, gate_sb, wa_raw = {}, {}, {}
 
         def load_wb(e, s, pieces):
             width = H // pieces
             rows = wbt[e, s * PASS : (s + 1) * PASS, :].rearrange("(p j) c -> p j c", j=PACK)
-            wb_raw[e, s] = []
+            wb_raw[e, s] = keep("wb_raw%d_%d" % (e, s), [P, PACK, H], F32)
+            wb_pieces[e, s] = pieces
             for q in range(pieces):
-                raw = keep("wb_raw%d_%d_%d" % (e, s, q), [P, PACK, width], F32)
-                nc.sync.dma_start(out=raw[:], in_=rows[:, :, q * width : (q + 1) * width])
-                wb_raw[e, s].append(raw)
+                cols = slice(q * width, (q + 1) * width)
+                nc.sync.dma_start(out=wb_raw[e, s][:, :, cols], in_=rows[:, :, cols])
 
         def load_dy(s):
             nc.sync.dma_start(out=dy[s][:], in_=dy_words[s].rearrange("p t d -> p (t d)").bitcast(I32))
@@ -120,7 +123,7 @@ def tile_moe_adb_relu2_kernel(
             load_wb(e, 1, 1)
             if e >= F_POOL:
                 load_gate(e)
-            load_wb(e, 2, 2 if e == E - 1 else 1)
+            load_wb(e, 2, 2 if e in HALVES else 1)
             if e >= F_POOL:
                 load_a(e)
             if e >= WA_POOL:
@@ -136,10 +139,15 @@ def tile_moe_adb_relu2_kernel(
                 in_=wt_scales[:, 4 * quad : 4 * quad + 4, :].rearrange("s r k -> r s k").bitcast(I32),
             )
 
-        wb_codes, wb_plane, wa_codes, wa_plane, factor, dh = {}, {}, {}, {}, {}, {}
+        wb_codes = [keep("wb_codes%d" % s, [P, H], U32) for s in range(PASSES)]
+        wb_plane = [keep("wb_plane%d" % s, [P, H], U8) for s in range(PASSES)]
+        wa_codes, wa_plane, factor, dh = {}, {}, {}, {}
+        staged = [keep("staged%d" % b, [P, PACK * H], BF16) for b in range(STAGES)]
+        sums = [psum.tile([P, PACK, P], F32, name="sums%d" % h) for h in range(C // P)]
+        acc = [psum.tile([P, BANK], F32, name="acc%d" % b) for b in range(4)]
 
-        def expert_offsets(e):
-            return offsets[:, e * LIST_COLS : (e + 1) * LIST_COLS]
+        def as_row(tile):
+            return tile[:].rearrange("p j c -> p (j c)")
 
         def gather(into, source):
             for g in range(0, E * C, GATHER):
@@ -147,65 +155,34 @@ def tile_moe_adb_relu2_kernel(
                     into[:, g : g + GATHER], source.indirect(offsets[:, g // 16 : (g + GATHER) // 16])
                 )
 
-        staged = [keep("staged%d" % b, [P, PACK * H], BF16) for b in range(STAGES)]
-
         def quantize_wb(e, s):
-            flat = staged[(PASSES * e + s) % STAGES]
-            grouped = flat[:].rearrange("p (t m j) -> p t m j", t=PACK, j=PACK)
-            pieces = wb_raw[e, s]
-            span = P // len(pieces)
-            for q, raw in enumerate(pieces):
-                copy = nc.vector.tensor_copy if TAILV and (e, s, q) == (E - 1, PASSES - 1, 1) else nc.scalar.copy
-                copy(
-                    out=grouped[:, :, q * span : (q + 1) * span, :].rearrange("p t m j -> p m j t"),
-                    in_=raw[:].rearrange("p j (m t) -> p m j t", t=PACK),
-                )
-            wb_codes[e, s] = ring.tile([P, H], U32, name="wb_codes", align_bytes=64, bufs=2 * PASSES)
-            wb_plane[e, s] = ring.tile([P, H], U8, name="wb_plane", align_bytes=64, bufs=2 * PASSES)
-            nc.vector.quantize_mx(
-                out=wb_codes[e, s][:].bitcast(FP8X4),
-                scales=wb_plane[e, s][:],
-                in_=flat[:],
-            )
+            if e in HALVES and s == PASSES - 1:
+                flat = as_row(wb_raw[e, s - 1])[:, : PACK * H // 2].bitcast(BF16)
+            else:
+                flat = staged[(PASSES * e + s) % STAGES][:]
+            grouped = flat.rearrange("p (t m j) -> p m j t", t=PACK, j=PACK)
+            raw = wb_raw[e, s][:].rearrange("p j (m t) -> p m j t", t=PACK)
+            span = P // wb_pieces[e, s]
+            for m in range(0, P, span):
+                nc.scalar.copy(out=grouped[:, m : m + span], in_=raw[:, m : m + span])
+            nc.vector.quantize_mx(out=wb_codes[s][:].bitcast(FP8X4), scales=wb_plane[s][:], in_=flat)
 
         def quantize_wa(e):
-            if e < WA_POOL:
-                flat = keep("wa_staged%d" % e, [P, PACK * K], BF16)[:]
-                nc.gpsimd.tensor_scalar(
-                    out=flat.rearrange("p (k j) -> p k j", j=PACK),
-                    in0=wa_raw[e][:].rearrange("p j k -> p k j"),
-                    scalar1=1.0, scalar2=0.0, op0=ALU.mult, op1=ALU.add,
-                )
-            else:
-                spent = wb_raw[e, PASSES - 1][-1][:].rearrange("p j c -> p (j c)")
-                flat = spent[:, spent.shape[1] - PACK * K // 2 :].bitcast(BF16)
-                nc.scalar.copy(
-                    out=flat.rearrange("p (c i j) -> p c j i", i=4, j=PACK),
-                    in_=wa_raw[e][:].rearrange("p j (c i) -> p c j i", i=4),
-                )
-            wa_codes[e] = keep("wa_codes%d" % e, [P, K], U32)
-            wa_plane[e] = keep("wa_plane%d" % e, [P, K], U8)
-            nc.vector.quantize_mx(
-                out=wa_codes[e][:].bitcast(FP8X4),
-                scales=wa_plane[e][:],
-                in_=flat,
+            flat = as_row(wb_raw[e, PASSES - 1])[:, PACK * C : PACK * C + PACK * K // 2].bitcast(BF16)
+            nc.scalar.copy(
+                out=flat.rearrange("p (c i j) -> p c j i", i=4, j=PACK),
+                in_=wa_raw[e][:].rearrange("p j (c i) -> p c j i", i=4),
             )
+            wa_codes[e] = ring.tile([P, K], U32, name="wa_codes", align_bytes=64)
+            wa_plane[e] = ring.tile([P, K], U8, name="wa_plane", align_bytes=64)
+            nc.vector.quantize_mx(out=wa_codes[e][:].bitcast(FP8X4), scales=wa_plane[e][:], in_=flat)
 
         def make_factor(e):
             gate2 = keep("gate2_%d" % e, [P, C], F32)
             nc.gpsimd.tensor_scalar(
                 out=gate2[:], in0=gate_sb[e][:], scalar1=2.0, scalar2=0.0, op0=ALU.mult, op1=ALU.add
             )
-            if e < F_POOL:
-                factor[e] = a_sb[e][:]
-                for t in range(PACK):
-                    nc.gpsimd.tensor_scalar(
-                        out=a_sb[e][:, t, :], in0=a_sb[e][:, t, :], scalar1=math.inf, scalar2=0.0, op0=ALU.min, op1=ALU.max
-                    )
-                    nc.gpsimd.tensor_tensor(out=a_sb[e][:, t, :], in0=a_sb[e][:, t, :], in1=gate2[:], op=ALU.mult)
-                return
-            spent = wb_raw[e, PASSES - 1][0][:].rearrange("p j c -> p (j c)")
-            factor[e] = spent[:, : PACK * C].rearrange("p (t j) -> p t j", t=PACK)
+            factor[e] = as_row(wb_raw[e, PASSES - 1])[:, : PACK * C].rearrange("p (t j) -> p t j", t=PACK)
             nc.vector.scalar_tensor_tensor(
                 out=factor[e],
                 in0=a_sb[e][:],
@@ -215,75 +192,62 @@ def tile_moe_adb_relu2_kernel(
                 op1=ALU.mult,
             )
 
-        def first_product(e):
-            dh[e] = ring.tile([P, C, PACK], BF16, name="dh", align_bytes=64)
-            for half in range(C // P):
-                sums = psum.tile([P, PACK, P], F32, name="sums")
-                cols = slice(e * C + half * P, e * C + (half + 1) * P)
-                for t in range(PACK):
-                    for s in range(PASSES):
-                        nc.tensor.matmul_mx(
-                            out=sums[:, t, :],
-                            lhsT=wb_codes[e, s][:, t * P : (t + 1) * P].bitcast(FP8X4),
-                            lhsT_scale=wb_plane[e, s][:, t * P : (t + 1) * P],
-                            rhs=slot_words[s][:, cols].bitcast(FP8X4),
-                            rhs_scale=slot_scales[4 * s :, cols],
-                            start=(s == 0),
-                            stop=(s == PASSES - 1),
-                        )
-                nc.vector.tensor_tensor(
-                    out=dh[e][:, half * P : (half + 1) * P, :].rearrange("p (c i) t -> p c t i", i=4),
-                    in0=sums[:].rearrange("p t (c i) -> p c t i", i=4),
-                    in1=factor[e][:, :, half * P : (half + 1) * P].rearrange("p t (c i) -> p c t i", i=4),
-                    op=ALU.mult,
-                )
-
-        def second_product(e):
-            dh_codes = ring.tile([P, C], U32, name="dh_codes", align_bytes=64)
-            dh_plane = ring.tile([P, C], U8, name="dh_plane", align_bytes=64)
-            nc.vector.quantize_mx(
-                out=dh_codes[:].bitcast(FP8X4), scales=dh_plane[:], in_=dh[e][:].rearrange("p c t -> p (c t)")
-            )
-            for kt in range(K // P):
-                acc = psum.tile([P, BANK], F32, name="acc")
-                nc.tensor.matmul_mx(
-                    out=acc[:, :C],
-                    lhsT=wa_codes[e][:, kt * P : (kt + 1) * P].bitcast(FP8X4),
-                    lhsT_scale=wa_plane[e][:, kt * P : (kt + 1) * P],
-                    rhs=dh_codes[:].bitcast(FP8X4),
-                    rhs_scale=dh_plane[:],
-                    start=True,
-                    stop=True,
-                )
-                dx = wb_raw[min(e + 1, E - 1), EVAC_AFTER][0][:, kt, :C]
-                if EVAC_V and e < E - 1:
-                    dx = ring.tile([P, C], F32, name="dx%d" % kt, align_bytes=64)[:]
-                    nc.vector.tensor_copy(out=dx, in_=acc[:, :C])
-                else:
-                    nc.scalar.copy(out=dx, in_=acc[:, :C])
-                dxs[e, kt] = dx
-
-        dxs = {}
-
-        def scatter(e, kt):
-            nc.vector.tensor_copy(window[kt][:].indirect(expert_offsets(e)), dxs[e, kt])
-
-        def finish(kt):
-            for h in range(T // BANK):
-                cols = slice(h * BANK, (h + 1) * BANK)
-                acc = psum.tile([P, BANK], F32, name="acc")
+        def first_product(e, half):
+            if half == 0:
+                dh[e] = ring.tile([P, C, PACK], BF16, name="dh", align_bytes=64)
+            cols = slice(e * C + half * P, e * C + (half + 1) * P)
+            for t in range(PACK):
                 for s in range(PASSES):
                     nc.tensor.matmul_mx(
-                        out=acc[:],
-                        lhsT=wt_codes[:, s, 2 * kt * P : 2 * (kt + 1) * P].bitcast(FP4X4),
-                        lhsT_scale=wt_plane[:, s, kt * P : (kt + 1) * P],
-                        rhs=dy[s][:, cols].bitcast(FP8X4),
-                        rhs_scale=dy_plane[:, s, cols],
+                        out=sums[half][:, t, :],
+                        lhsT=wb_codes[s][:, t * P : (t + 1) * P].bitcast(FP8X4),
+                        lhsT_scale=wb_plane[s][:, t * P : (t + 1) * P],
+                        rhs=slot_words[s][:, cols].bitcast(FP8X4),
+                        rhs_scale=slot_scales[4 * s :, cols],
                         start=(s == 0),
                         stop=(s == PASSES - 1),
                     )
-                nc.vector.tensor_tensor(out=window[kt][:, cols], in0=acc[:], in1=window[kt][:, cols], op=ALU.add)
-                nc.sync.dma_start(out=out[kt * P : (kt + 1) * P, cols], in_=window[kt][:, cols])
+            nc.vector.tensor_tensor(
+                out=dh[e][:, half * P : (half + 1) * P, :].rearrange("p (c i) t -> p c t i", i=4),
+                in0=sums[half][:].rearrange("p t (c i) -> p c t i", i=4),
+                in1=factor[e][:, :, half * P : (half + 1) * P].rearrange("p t (c i) -> p c t i", i=4),
+                op=ALU.mult,
+            )
+
+        def second_product(e, slots, dh_codes, dh_plane, into):
+            nc.vector.quantize_mx(
+                out=dh_codes.bitcast(FP8X4), scales=dh_plane, in_=dh[e][:, slots, :].rearrange("p c t -> p (c t)")
+            )
+            for kt in range(K // P):
+                nc.tensor.matmul_mx(
+                    out=into[kt],
+                    lhsT=wa_codes[e][:, kt * P : (kt + 1) * P].bitcast(FP8X4),
+                    lhsT_scale=wa_plane[e][:, kt * P : (kt + 1) * P],
+                    rhs=dh_codes.bitcast(FP8X4),
+                    rhs_scale=dh_plane,
+                    start=True,
+                    stop=True,
+                )
+
+        def scatter(kt, first, values):
+            count = values.shape[1]
+            nc.vector.tensor_copy(window[kt][:].indirect(offsets[:, first // 16 : (first + count) // 16]), values)
+
+        def finish(kt, h):
+            cols = slice(h * BANK, (h + 1) * BANK)
+            bank = acc[2 * kt + h]
+            for s in range(PASSES):
+                nc.tensor.matmul_mx(
+                    out=bank[:],
+                    lhsT=wt_codes[:, s, 2 * kt * P : 2 * (kt + 1) * P].bitcast(FP4X4),
+                    lhsT_scale=wt_plane[:, s, kt * P : (kt + 1) * P],
+                    rhs=dy[s][:, cols].bitcast(FP8X4),
+                    rhs_scale=dy_plane[:, s, cols],
+                    start=(s == 0),
+                    stop=(s == PASSES - 1),
+                )
+            nc.vector.tensor_tensor(out=window[kt][:, cols], in0=bank[:], in1=window[kt][:, cols], op=ALU.add)
+            nc.sync.dma_start(out=out[kt * P : (kt + 1) * P, cols], in_=window[kt][:, cols])
 
         for item in HEADV:
             if item[0] == "d":
@@ -292,21 +256,46 @@ def tile_moe_adb_relu2_kernel(
                 gather(slot_scales[:], dy_packed[:])
             else:
                 quantize_wb(0, int(item[1]))
-        for e in range(E):
-            if e > 0:
-                if EARLY2:
-                    second_product(e - 1)
-                quantize_wb(e, 0)
-                if not EARLY2:
-                    second_product(e - 1)
-                for kt in range(K // P):
-                    scatter(e - 1, kt)
-                quantize_wb(e, 1)
-                quantize_wb(e, 2)
+        for e in range(E - 1):
             make_factor(e)
-            first_product(e)
+            first_product(e, 0)
             quantize_wa(e)
-        second_product(E - 1)
+            first_product(e, 1)
+            second_product(
+                e, slice(0, C), wb_codes[CODES2][:, :C], wb_plane[CODES2][:, :C], [acc[0][:, :C], acc[0][:, C:]]
+            )
+            quantize_wb(e + 1, 0)
+            after = EVAC_AFTER[e]
+            if after == 1:
+                quantize_wb(e + 1, 1)
+            if after < 0:
+                dx = ring.tile([P, 2 * C], F32, name="dx", align_bytes=64)[:]
+                nc.vector.tensor_copy(out=dx, in_=acc[0][:])
+            else:
+                dx = as_row(wb_raw[e + 1, after])[:, PACK * H - 2 * C :]
+                nc.scalar.copy(out=dx, in_=acc[0][:])
+            for kt in range(K // P):
+                scatter(kt, e * C, dx[:, kt * C : (kt + 1) * C])
+            if after != 1:
+                quantize_wb(e + 1, 1)
+            quantize_wb(e + 1, 2)
+
+        last = E - 1
+        make_factor(last)
+        dx = ring.tile([P, 2 * C], F32, name="dx", align_bytes=64)
+        dh_codes = keep("dh_codes", [P, C], U32)
+        dh_plane = keep("dh_plane", [P, C], U8)
+        for half in range(C // P):
+            slots = slice(half * P, (half + 1) * P)
+            first_product(last, half)
+            if half == 0:
+                quantize_wa(last)
+            banks = [acc[2 * kt + half][:, :P] for kt in range(K // P)]
+            second_product(last, slots, dh_codes[:, slots], dh_plane[:, slots], banks)
+            for kt in range(K // P):
+                nc.scalar.copy(out=dx[:, kt * C + half * P : kt * C + (half + 1) * P], in_=banks[kt])
         for kt in range(K // P):
-            scatter(E - 1, kt)
-            finish(kt)
+            for half in range(C // P):
+                scatter(kt, last * C + half * P, dx[:, kt * C + half * P : kt * C + (half + 1) * P])
+            for h in range(T // BANK):
+                finish(kt, h)

@@ -2,6 +2,7 @@ import math
 from contextlib import ExitStack
 
 import concourse.mybir as mybir
+from concourse.masks import make_identity
 
 K, T, E, C, H, N = 256, 1024, 4, 256, 512, 1536
 FLOPS = 2 * N * K * T + 2 * E * C * (N * H + H * K)
@@ -28,9 +29,11 @@ F_POOL = 0
 WA_POOL = 0
 TAILV = False
 EARLY2 = True
-HEAD = "d0 w0 s d1 w1 d2 g w2 a A".split()
-HEADV = "d0 s q0 d1 q1 d2 q2".split()
+HEAD = "d0 w0 s d1 g w1 d2 w2 a A".split()
+HEADV = "d0 s q0 g d1 q1 d2 q2".split()
 GATHER = 512
+A_COUNT = [1, 1, 1, 1]
+FIRST_PIECES = 2
 STAGES = 6
 EVAC_AFTER = [-1, 1, 1]
 HALVES = [3]
@@ -62,7 +65,7 @@ def tile_moe_adb_relu2_kernel(
         nc.vector.memset(dy_packed[:].bitcast(I32), 0)
 
         wb_raw, wb_pieces = {}, {}
-        a_sb, gate_sb, wa_raw = {}, {}, {}
+        a_sb, wa_raw = {}, {}
 
         def load_wb(e, s, pieces):
             width = H // pieces
@@ -77,14 +80,21 @@ def tile_moe_adb_relu2_kernel(
             nc.sync.dma_start(out=dy[s][:], in_=dy_words[s].rearrange("p t d -> p (t d)").bitcast(I32))
 
         def load_a(e):
-            a_sb[e] = keep("a%d" % e, [P, PACK, C], F32)
+            count = A_COUNT[e]
+            both = keep("a%d" % e, [P, PACK, count * C], F32)
             nc.sync.dma_start(
-                out=a_sb[e][:], in_=a.rearrange("(p t) j -> p t j", t=PACK)[:, :, e * C : (e + 1) * C]
+                out=both[:], in_=a.rearrange("(p t) j -> p t j", t=PACK)[:, :, e * C : (e + count) * C]
             )
+            for u in range(count):
+                a_sb[e + u] = both[:, :, u * C : (u + 1) * C]
 
-        def load_gate(e):
-            gate_sb[e] = keep("gate%d" % e, [P, C], F32)
-            nc.sync.dma_start(out=gate_sb[e][:], in_=gate[:, e * C : (e + 1) * C])
+        gate_rows = keep("gate_rows", [P, P], F32)
+        identity = keep("identity", [P, P], F32)
+        nc.gpsimd.memset(gate_rows[:], 0.0)
+        make_identity(nc, identity[:])
+
+        def load_gate():
+            nc.sync.dma_start(out=gate_rows[: T // P, :], in_=gate[0, :].rearrange("(m p) -> m p", p=P))
 
         def load_wa(e):
             wa_raw[e] = keep("wa_raw%d" % e, [P, PACK, K], F32)
@@ -104,27 +114,22 @@ def tile_moe_adb_relu2_kernel(
             if item[0] == "d":
                 load_dy(int(item[1]))
             elif item[0] == "w":
-                load_wb(0, int(item[1]), 2 if item[1] == "0" else 1)
+                load_wb(0, int(item[1]), FIRST_PIECES if item[1] == "0" else 1)
             elif item == "s":
                 load_packed_scales()
             elif item == "g":
-                load_gate(0)
+                load_gate()
             elif item == "a":
                 load_a(0)
             elif item == "A":
                 load_wa(0)
         for e in range(1, E):
-            if e < F_POOL:
-                load_gate(e)
-                load_a(e)
             load_wb(e, 0, 1)
             if e < WA_POOL:
                 load_wa(e)
             load_wb(e, 1, 1)
-            if e >= F_POOL:
-                load_gate(e)
             load_wb(e, 2, 2 if e in HALVES else 1)
-            if e >= F_POOL:
+            if e not in a_sb:
                 load_a(e)
             if e >= WA_POOL:
                 load_wa(e)
@@ -173,24 +178,24 @@ def tile_moe_adb_relu2_kernel(
                 out=flat.rearrange("p (c i j) -> p c j i", i=4, j=PACK),
                 in_=wa_raw[e][:].rearrange("p j (c i) -> p c j i", i=4),
             )
-            wa_codes[e] = ring.tile([P, K], U32, name="wa_codes", align_bytes=64)
-            wa_plane[e] = ring.tile([P, K], U8, name="wa_plane", align_bytes=64)
-            nc.vector.quantize_mx(out=wa_codes[e][:].bitcast(FP8X4), scales=wa_plane[e][:], in_=flat)
+            if e < E - 1:
+                wa_codes[e], wa_plane[e] = wb_codes[2][:, :K], wb_plane[2][:, :K]
+            else:
+                wa_codes[e], wa_plane[e] = keep("wa_codes", [P, K], U32)[:], keep("wa_plane", [P, K], U8)[:]
+            nc.vector.quantize_mx(out=wa_codes[e].bitcast(FP8X4), scales=wa_plane[e], in_=flat)
 
         def make_factor(e):
-            gate2 = keep("gate2_%d" % e, [P, C], F32)
-            nc.gpsimd.tensor_scalar(
-                out=gate2[:], in0=gate_sb[e][:], scalar1=2.0, scalar2=0.0, op0=ALU.mult, op1=ALU.add
-            )
-            factor[e] = as_row(wb_raw[e, PASSES - 1])[:, : PACK * C].rearrange("p (t j) -> p t j", t=PACK)
-            nc.vector.scalar_tensor_tensor(
-                out=factor[e],
-                in0=a_sb[e][:],
-                scalar=0.0,
-                in1=gate2[:].unsqueeze(1).to_broadcast([P, PACK, C]),
-                op0=ALU.max,
-                op1=ALU.mult,
-            )
+            factor[e] = as_row(wb_raw[e, PASSES - 1])[:, : PACK * C].rearrange("p (j t) -> p j t", t=PACK)
+            for half in range(C // P):
+                slots = slice(half * P, (half + 1) * P)
+                nc.vector.scalar_tensor_tensor(
+                    out=factor[e][:, slots, :],
+                    in0=a_sb[e][:, :, slots].rearrange("p t j -> p j t"),
+                    scalar=0.0,
+                    in1=gate_sb[:, e * C + half * P : e * C + (half + 1) * P].unsqueeze(2).to_broadcast([P, P, PACK]),
+                    op0=ALU.max,
+                    op1=ALU.mult,
+                )
 
         def first_product(e, half):
             if half == 0:
@@ -207,11 +212,13 @@ def tile_moe_adb_relu2_kernel(
                         start=(s == 0),
                         stop=(s == PASSES - 1),
                     )
-            nc.vector.tensor_tensor(
-                out=dh[e][:, half * P : (half + 1) * P, :].rearrange("p (c i) t -> p c t i", i=4),
-                in0=sums[half][:].rearrange("p t (c i) -> p c t i", i=4),
-                in1=factor[e][:, :, half * P : (half + 1) * P].rearrange("p t (c i) -> p c t i", i=4),
-                op=ALU.mult,
+            nc.vector.scalar_tensor_tensor(
+                out=dh[e][:, half * P : (half + 1) * P, :],
+                in0=sums[half][:].rearrange("p t j -> p j t"),
+                scalar=2.0,
+                in1=factor[e][:, half * P : (half + 1) * P, :],
+                op0=ALU.mult,
+                op1=ALU.mult,
             )
 
         def second_product(e, slots, dh_codes, dh_plane, into):
@@ -249,8 +256,26 @@ def tile_moe_adb_relu2_kernel(
             nc.vector.tensor_tensor(out=window[kt][:, cols], in0=bank[:], in1=window[kt][:, cols], op=ALU.add)
             nc.sync.dma_start(out=out[kt * P : (kt + 1) * P, cols], in_=window[kt][:, cols])
 
+        gate_sb = keep("gate_sb", [P, T], F32)
+
+        def spread_gate():
+            gate_cols = keep("gate_cols", [P, T // P], F32)
+            nc.tensor.transpose(acc[0][:, :P], gate_rows[:], identity[:])
+            nc.scalar.copy(out=gate_cols[:], in_=acc[0][:, : T // P])
+            for h in range(T // BANK):
+                for m in range(BANK // P):
+                    column = h * (BANK // P) + m
+                    nc.tensor.transpose(
+                        acc[1 + h][:, m * P : (m + 1) * P],
+                        gate_cols[:, column : column + 1].to_broadcast([P, P]),
+                        identity[:],
+                    )
+                nc.scalar.copy(out=gate_sb[:, h * BANK : (h + 1) * BANK], in_=acc[1 + h][:])
+
         for item in HEADV:
-            if item[0] == "d":
+            if item == "g":
+                spread_gate()
+            elif item[0] == "d":
                 gather(slot_words[int(item[1])][:].bitcast(U32), dy[int(item[1])][:].bitcast(U32))
             elif item == "s":
                 gather(slot_scales[:], dy_packed[:])
@@ -259,8 +284,8 @@ def tile_moe_adb_relu2_kernel(
         for e in range(E - 1):
             make_factor(e)
             first_product(e, 0)
-            quantize_wa(e)
             first_product(e, 1)
+            quantize_wa(e)
             second_product(
                 e, slice(0, C), wb_codes[CODES2][:, :C], wb_plane[CODES2][:, :C], [acc[0][:, :C], acc[0][:, C:]]
             )
@@ -294,8 +319,10 @@ def tile_moe_adb_relu2_kernel(
             second_product(last, slots, dh_codes[:, slots], dh_plane[:, slots], banks)
             for kt in range(K // P):
                 nc.scalar.copy(out=dx[:, kt * C + half * P : kt * C + (half + 1) * P], in_=banks[kt])
-        for kt in range(K // P):
-            for half in range(C // P):
-                scatter(kt, last * C + half * P, dx[:, kt * C + half * P : kt * C + (half + 1) * P])
-            for h in range(T // BANK):
-                finish(kt, h)
+        for kt, half in [(0, 0), (0, 1), (1, 0)]:
+            scatter(kt, last * C + half * P, dx[:, kt * C + half * P : kt * C + (half + 1) * P])
+        finish(0, 0)
+        scatter(1, last * C + P, dx[:, C + P :])
+        finish(0, 1)
+        finish(1, 0)
+        finish(1, 1)

@@ -1,4 +1,3 @@
-import math
 from contextlib import ExitStack
 
 import concourse.mybir as mybir
@@ -6,6 +5,7 @@ from concourse.masks import make_identity
 
 K, T, E, C, H, N = 256, 1024, 4, 256, 512, 1536
 FLOPS = 2 * N * K * T + 2 * E * C * (N * H + H * K)
+BYTES = N * T + N * T // 32 + N * K // 2 + N * K // 32 + 4 * (E * N * H + E * H * K + H * T + T + K * T) + 2 * 8 * T
 
 F32 = mybir.dt.float32
 BF16 = mybir.dt.bfloat16
@@ -19,25 +19,16 @@ ALU = mybir.AluOpType
 
 P = 128
 PACK = 4
+RUN = 4
 PASS = P * PACK
 PASSES = N // PASS
 BANK = 512
-LIST_COLS = C // 16
-SPLIT_DX = False
-EVAC_V = True
-F_POOL = 0
-WA_POOL = 0
-TAILV = False
-EARLY2 = True
-HEAD = "d0 w0 s d1 g w1 d2 w2 a A".split()
-HEADV = "d0 s q0 g d1 q1 d2 q2".split()
-GATHER = 512
-A_COUNT = [1, 1, 1, 1]
-FIRST_PIECES = 2
-STAGES = 6
-EVAC_AFTER = [-1, 1, 1]
-HALVES = [3]
-CODES2 = 1
+K_TILES = K // P
+HALVES = C // P
+QUADS = P // 32
+GATHER = T // 2
+STAGES = 2 * PASSES
+LAST = E - 1
 
 
 def tile_moe_adb_relu2_kernel(
@@ -52,6 +43,12 @@ def tile_moe_adb_relu2_kernel(
         def keep(name, shape, dtype):
             return held.tile(shape, dtype, name=name, align_bytes=64)
 
+        def as_row(tile):
+            return tile[:].rearrange("p j c -> p (j c)")
+
+        def list_slice(first, count):
+            return offsets[:, first // 16 : (first + count) // 16]
+
         offsets = held.tile([P, T // 16], U16, name="offsets")
         dy = [keep("dy%d" % s, [P, T], I32) for s in range(PASSES)]
         dy_packed = keep("dy_packed", [P, T], U8)
@@ -60,147 +57,136 @@ def tile_moe_adb_relu2_kernel(
         wt_plane = keep("wt_plane", [P, PASSES, K], U8)
         slot_words = [keep("slot_words%d" % s, [P, E * C], I32) for s in range(PASSES)]
         slot_scales = keep("slot_scales", [P, E * C], U8)
-        window = [keep("window%d" % kt, [P, T], F32) for kt in range(K // P)]
+        window = [keep("window%d" % kt, [P, T], F32) for kt in range(K_TILES)]
+        gate_rows = keep("gate_rows", [P, P], F32)
+        identity = keep("identity", [P, P], F32)
 
         nc.vector.memset(dy_packed[:].bitcast(I32), 0)
+        nc.vector.memset(gate_rows[:], 0.0)
+        make_identity(nc, identity[:])
+        nc.gpsimd.memset(dy_plane[:].rearrange("p s t -> p (s t)").bitcast(I32), 0)
+        nc.gpsimd.memset(wt_plane[:].rearrange("p s k -> p (s k)").bitcast(I32), 0)
 
-        wb_raw, wb_pieces = {}, {}
-        a_sb, wa_raw = {}, {}
-
-        def load_wb(e, s, pieces):
-            width = H // pieces
-            rows = wbt[e, s * PASS : (s + 1) * PASS, :].rearrange("(p j) c -> p j c", j=PACK)
-            wb_raw[e, s] = keep("wb_raw%d_%d" % (e, s), [P, PACK, H], F32)
-            wb_pieces[e, s] = pieces
-            for q in range(pieces):
-                cols = slice(q * width, (q + 1) * width)
-                nc.sync.dma_start(out=wb_raw[e, s][:, :, cols], in_=rows[:, :, cols])
+        wb_raw, wa_raw, a_sb = {}, {}, {}
 
         def load_dy(s):
             nc.sync.dma_start(out=dy[s][:], in_=dy_words[s].rearrange("p t d -> p (t d)").bitcast(I32))
 
-        def load_a(e):
-            count = A_COUNT[e]
-            both = keep("a%d" % e, [P, PACK, count * C], F32)
-            nc.sync.dma_start(
-                out=both[:], in_=a.rearrange("(p t) j -> p t j", t=PACK)[:, :, e * C : (e + count) * C]
-            )
+        def load_wb(e, s):
+            wb_raw[e, s] = keep("wb_raw%d_%d" % (e, s), [P, PACK, H], F32)
+            rows = wbt[e, s * PASS : (s + 1) * PASS, :].rearrange("(p d) i -> p d i", d=PACK)
+            nc.sync.dma_start(out=wb_raw[e, s][:], in_=rows)
+
+        def load_a(e, count):
+            tile = keep("a%d" % e, [P, PACK, count * C], F32)
+            rows = a.rearrange("(c t r) j -> t c r j", t=PACK, r=RUN)
+            for t in range(PACK):
+                nc.sync.dma_start(out=tile[:, t, :], in_=rows[t, :, :, e * C : (e + count) * C])
             for u in range(count):
-                a_sb[e + u] = both[:, :, u * C : (u + 1) * C]
-
-        gate_rows = keep("gate_rows", [P, P], F32)
-        identity = keep("identity", [P, P], F32)
-        nc.gpsimd.memset(gate_rows[:], 0.0)
-        make_identity(nc, identity[:])
-
-        def load_gate():
-            nc.sync.dma_start(out=gate_rows[: T // P, :], in_=gate[0, :].rearrange("(m p) -> m p", p=P))
+                a_sb[e + u] = tile[:, :, u * C : (u + 1) * C]
 
         def load_wa(e):
             wa_raw[e] = keep("wa_raw%d" % e, [P, PACK, K], F32)
-            nc.sync.dma_start(out=wa_raw[e][:], in_=wat[e].rearrange("(p j) k -> p j k", j=PACK))
+            rows = wat[e].rearrange("(c t r) k -> t c r k", t=PACK, r=RUN)
+            for t in range(PACK):
+                nc.sync.dma_start(out=wa_raw[e][:, t, :], in_=rows[t])
 
-        def load_packed_scales():
-            for quad in range(4):
-                nc.sync.dma_start(
-                    out=dy_packed[32 * quad : 32 * quad + 4 * PASSES, :].bitcast(I32),
-                    in_=dy_scales[:, 4 * quad : 4 * quad + 4, :].bitcast(I32),
-                )
-
-        nc.gpsimd.memset(dy_plane[:].rearrange("p s t -> p (s t)").bitcast(I32), 0)
-        nc.gpsimd.memset(wt_plane[:].rearrange("p s k -> p (s k)").bitcast(I32), 0)
         nc.sync.dma_start(offsets[:], offs)
-        for item in HEAD:
-            if item[0] == "d":
-                load_dy(int(item[1]))
-            elif item[0] == "w":
-                load_wb(0, int(item[1]), FIRST_PIECES if item[1] == "0" else 1)
-            elif item == "s":
-                load_packed_scales()
-            elif item == "g":
-                load_gate()
-            elif item == "a":
-                load_a(0)
-            elif item == "A":
-                load_wa(0)
-        for e in range(1, E):
-            load_wb(e, 0, 1)
-            if e < WA_POOL:
-                load_wa(e)
-            load_wb(e, 1, 1)
-            load_wb(e, 2, 2 if e in HALVES else 1)
+        load_dy(0)
+        nc.sync.dma_start(out=gate_rows[: T // P, :], in_=gate[0, :].rearrange("(m p) -> m p", p=P))
+        load_wb(0, 0)
+        load_dy(1)
+        for quad in range(QUADS):
+            nc.sync.dma_start(
+                out=dy_packed[32 * quad : 32 * quad + 4 * PASSES, :].bitcast(I32),
+                in_=dy_scales[:, 4 * quad : 4 * quad + 4, :].bitcast(I32),
+            )
+        load_wb(0, 1)
+        load_dy(2)
+        load_wb(0, 2)
+        load_a(0, 2)
+        load_wa(0)
+        for e in range(1, LAST):
+            for s in range(PASSES):
+                load_wb(e, s)
             if e not in a_sb:
-                load_a(e)
-            if e >= WA_POOL:
-                load_wa(e)
+                load_a(e, 1)
+            load_wa(e)
+        for s in range(PASSES):
+            load_wb(LAST, s)
+        load_wa(LAST)
+        load_a(LAST, 1)
         nc.sync.dma_start(out=wt_codes[:].bitcast(I32), in_=wt_words.rearrange("s p b -> p s b").bitcast(I32))
-        for quad in range(4):
+        for quad in range(QUADS):
             nc.sync.dma_start(
                 out=dy_plane[32 * quad : 32 * quad + 4, :, :].bitcast(I32),
-                in_=dy_scales[:, 4 * quad : 4 * quad + 4, :].rearrange("s r t -> r s t").bitcast(I32),
+                in_=dy_scales[:, 4 * quad : 4 * quad + 4, :].rearrange("s b t -> b s t").bitcast(I32),
             )
             nc.sync.dma_start(
                 out=wt_plane[32 * quad : 32 * quad + 4, :, :].bitcast(I32),
-                in_=wt_scales[:, 4 * quad : 4 * quad + 4, :].rearrange("s r k -> r s k").bitcast(I32),
+                in_=wt_scales[:, 4 * quad : 4 * quad + 4, :].rearrange("s b k -> b s k").bitcast(I32),
             )
 
+        staged = [keep("staged%d" % b, [P, PACK * H], BF16) for b in range(STAGES)]
         wb_codes = [keep("wb_codes%d" % s, [P, H], U32) for s in range(PASSES)]
         wb_plane = [keep("wb_plane%d" % s, [P, H], U8) for s in range(PASSES)]
-        wa_codes, wa_plane, factor, dh = {}, {}, {}, {}
-        staged = [keep("staged%d" % b, [P, PACK * H], BF16) for b in range(STAGES)]
-        sums = [psum.tile([P, PACK, P], F32, name="sums%d" % h) for h in range(C // P)]
-        acc = [psum.tile([P, BANK], F32, name="acc%d" % b) for b in range(4)]
+        gate2 = keep("gate2", [P, T], F32)
+        sums = [psum.tile([P, PACK, P], F32, name="sums%d" % half) for half in range(HALVES)]
+        base = [psum.tile([P, BANK], F32, name="base%d" % b) for b in range(K_TILES * T // BANK)]
+        spare = psum.tile([P, BANK], F32, name="spare")
 
-        def as_row(tile):
-            return tile[:].rearrange("p j c -> p (j c)")
+        def spread_gate():
+            gate_cols = keep("gate_cols", [P, T // P], F32)
+            nc.tensor.transpose(base[0][:, :P], gate_rows[:], identity[:])
+            nc.scalar.mul(gate_cols[:], base[0][:, : T // P], 2.0)
+            for h in range(T // BANK):
+                for m in range(BANK // P):
+                    column = h * (BANK // P) + m
+                    nc.tensor.transpose(
+                        base[1 + h][:, m * P : (m + 1) * P],
+                        gate_cols[:, column : column + 1].to_broadcast([P, P]),
+                        identity[:],
+                    )
+                nc.scalar.copy(out=gate2[:, h * BANK : (h + 1) * BANK], in_=base[1 + h][:])
 
         def gather(into, source):
-            for g in range(0, E * C, GATHER):
-                nc.vector.tensor_copy(
-                    into[:, g : g + GATHER], source.indirect(offsets[:, g // 16 : (g + GATHER) // 16])
-                )
+            for first in range(0, E * C, GATHER):
+                nc.vector.tensor_copy(into[:, first : first + GATHER], source.indirect(list_slice(first, GATHER)))
 
         def quantize_wb(e, s):
-            if e in HALVES and s == PASSES - 1:
-                flat = as_row(wb_raw[e, s - 1])[:, : PACK * H // 2].bitcast(BF16)
-            else:
-                flat = staged[(PASSES * e + s) % STAGES][:]
-            grouped = flat.rearrange("p (t m j) -> p m j t", t=PACK, j=PACK)
-            raw = wb_raw[e, s][:].rearrange("p j (m t) -> p m j t", t=PACK)
-            span = P // wb_pieces[e, s]
-            for m in range(0, P, span):
-                nc.scalar.copy(out=grouped[:, m : m + span], in_=raw[:, m : m + span])
-            nc.vector.quantize_mx(out=wb_codes[s][:].bitcast(FP8X4), scales=wb_plane[s][:], in_=flat)
-
-        def quantize_wa(e):
-            flat = as_row(wb_raw[e, PASSES - 1])[:, PACK * C : PACK * C + PACK * K // 2].bitcast(BF16)
+            rounded = staged[(PASSES * e + s) % STAGES][:]
             nc.scalar.copy(
-                out=flat.rearrange("p (c i j) -> p c j i", i=4, j=PACK),
-                in_=wa_raw[e][:].rearrange("p j (c i) -> p c j i", i=4),
+                out=rounded.rearrange("p (t c r d) -> p c t d r", t=PACK, r=RUN, d=PACK),
+                in_=wb_raw[e, s][:].rearrange("p d (c t r) -> p c t d r", t=PACK, r=RUN),
             )
-            if e < E - 1:
-                wa_codes[e], wa_plane[e] = wb_codes[2][:, :K], wb_plane[2][:, :K]
-            else:
-                wa_codes[e], wa_plane[e] = keep("wa_codes", [P, K], U32)[:], keep("wa_plane", [P, K], U8)[:]
-            nc.vector.quantize_mx(out=wa_codes[e].bitcast(FP8X4), scales=wa_plane[e], in_=flat)
+            nc.vector.quantize_mx(out=wb_codes[s][:].bitcast(FP8X4), scales=wb_plane[s][:], in_=rounded)
+
+        def spent(e):
+            return as_row(wb_raw[e, PASSES - 1])
+
+        def quantize_wa(e, codes, plane):
+            rounded = spent(e)[:, PACK * C : PACK * C + PACK * K // 2].bitcast(BF16)
+            nc.scalar.copy(
+                out=rounded.rearrange("p (c r t) -> p c t r", r=RUN, t=PACK),
+                in_=wa_raw[e][:].rearrange("p t (c r) -> p c t r", r=RUN),
+            )
+            nc.vector.quantize_mx(out=codes.bitcast(FP8X4), scales=plane, in_=rounded)
 
         def make_factor(e):
-            factor[e] = as_row(wb_raw[e, PASSES - 1])[:, : PACK * C].rearrange("p (j t) -> p j t", t=PACK)
-            for half in range(C // P):
-                slots = slice(half * P, (half + 1) * P)
-                nc.vector.scalar_tensor_tensor(
-                    out=factor[e][:, slots, :],
-                    in0=a_sb[e][:, :, slots].rearrange("p t j -> p j t"),
-                    scalar=0.0,
-                    in1=gate_sb[:, e * C + half * P : e * C + (half + 1) * P].unsqueeze(2).to_broadcast([P, P, PACK]),
-                    op0=ALU.max,
-                    op1=ALU.mult,
-                )
+            factor = spent(e)[:, : PACK * C].rearrange("p (t j) -> p t j", t=PACK)
+            nc.vector.scalar_tensor_tensor(
+                out=factor,
+                in0=a_sb[e],
+                scalar=0.0,
+                in1=gate2[:, e * C : (e + 1) * C].unsqueeze(1).to_broadcast([P, PACK, C]),
+                op0=ALU.max,
+                op1=ALU.mult,
+            )
+            return factor
 
-        def first_product(e, half):
-            if half == 0:
-                dh[e] = ring.tile([P, C, PACK], BF16, name="dh", align_bytes=64)
+        def first_product(e, half, factor, dh):
             cols = slice(e * C + half * P, e * C + (half + 1) * P)
+            slots = slice(half * P, (half + 1) * P)
             for t in range(PACK):
                 for s in range(PASSES):
                     nc.tensor.matmul_mx(
@@ -212,24 +198,22 @@ def tile_moe_adb_relu2_kernel(
                         start=(s == 0),
                         stop=(s == PASSES - 1),
                     )
-            nc.vector.scalar_tensor_tensor(
-                out=dh[e][:, half * P : (half + 1) * P, :],
-                in0=sums[half][:].rearrange("p t j -> p j t"),
-                scalar=2.0,
-                in1=factor[e][:, half * P : (half + 1) * P, :],
-                op0=ALU.mult,
-                op1=ALU.mult,
+            nc.vector.tensor_tensor(
+                out=dh[:, slots, :].rearrange("p (c r) t -> p c t r", r=RUN),
+                in0=sums[half][:].rearrange("p t (c r) -> p c t r", r=RUN),
+                in1=factor[:, :, slots].rearrange("p t (c r) -> p c t r", r=RUN),
+                op=ALU.mult,
             )
 
-        def second_product(e, slots, dh_codes, dh_plane, into):
+        def second_product(dh_slots, dh_codes, dh_plane, wa_codes, wa_plane, banks):
             nc.vector.quantize_mx(
-                out=dh_codes.bitcast(FP8X4), scales=dh_plane, in_=dh[e][:, slots, :].rearrange("p c t -> p (c t)")
+                out=dh_codes.bitcast(FP8X4), scales=dh_plane, in_=dh_slots.rearrange("p j t -> p (j t)")
             )
-            for kt in range(K // P):
+            for kt in range(K_TILES):
                 nc.tensor.matmul_mx(
-                    out=into[kt],
-                    lhsT=wa_codes[e][:, kt * P : (kt + 1) * P].bitcast(FP8X4),
-                    lhsT_scale=wa_plane[e][:, kt * P : (kt + 1) * P],
+                    out=banks[kt],
+                    lhsT=wa_codes[:, kt * P : (kt + 1) * P].bitcast(FP8X4),
+                    lhsT_scale=wa_plane[:, kt * P : (kt + 1) * P],
                     rhs=dh_codes.bitcast(FP8X4),
                     rhs_scale=dh_plane,
                     start=True,
@@ -237,12 +221,59 @@ def tile_moe_adb_relu2_kernel(
                 )
 
         def scatter(kt, first, values):
-            count = values.shape[1]
-            nc.vector.tensor_copy(window[kt][:].indirect(offsets[:, first // 16 : (first + count) // 16]), values)
+            nc.vector.tensor_copy(window[kt][:].indirect(list_slice(first, values.shape[1])), values)
 
-        def finish(kt, h):
-            cols = slice(h * BANK, (h + 1) * BANK)
-            bank = acc[2 * kt + h]
+        spread_gate()
+        for s in range(PASSES):
+            gather(slot_words[s][:].bitcast(U32), dy[s][:].bitcast(U32))
+            if s == 0:
+                gather(slot_scales[:], dy_packed[:])
+            quantize_wb(0, s)
+
+        held_back = None
+        for e in range(LAST):
+            factor = make_factor(e)
+            if held_back is not None:
+                scatter(1, (e - 1) * C, held_back)
+            dh = ring.tile([P, C, PACK], BF16, name="dh", align_bytes=64)
+            for half in range(HALVES):
+                first_product(e, half, factor, dh)
+            wa_codes, wa_plane = wb_codes[2][:, :K], wb_plane[2][:, :K]
+            quantize_wa(e, wa_codes, wa_plane)
+            banks = [base[1][:, :C], spare[:, :C]]
+            second_product(dh[:], wb_codes[1][:, :C], wb_plane[1][:, :C], wa_codes, wa_plane, banks)
+            quantize_wb(e + 1, 0)
+            tiles_now = K_TILES if e == 0 else 1
+            dx = ring.tile([P, K_TILES, C], F32, name="dx", align_bytes=64)
+            for kt in range(tiles_now):
+                nc.vector.tensor_copy(out=dx[:, kt, :], in_=banks[kt])
+            for kt in range(tiles_now):
+                scatter(kt, e * C, dx[:, kt, :])
+            quantize_wb(e + 1, 1)
+            quantize_wb(e + 1, 2)
+            if e > 0:
+                held_back = spent(e + 1)[:, PACK * H - C :]
+                nc.scalar.copy(out=held_back, in_=banks[1])
+
+        factor = make_factor(LAST)
+        scatter(1, (LAST - 1) * C, held_back)
+        dh = ring.tile([P, C, PACK], BF16, name="dh", align_bytes=64)
+        dx = ring.tile([P, K_TILES, C], F32, name="dx", align_bytes=64)
+        wa_codes, wa_plane = keep("wa_codes", [P, K], U32)[:], keep("wa_plane", [P, K], U8)[:]
+        dh_codes, dh_plane = keep("dh_codes", [P, C], U32), keep("dh_plane", [P, C], U8)
+        last_banks = [[spare, base[1]], [base[2], base[3]]]
+        for half in range(HALVES):
+            slots = slice(half * P, (half + 1) * P)
+            first_product(LAST, half, factor, dh)
+            if half == 0:
+                quantize_wa(LAST, wa_codes, wa_plane)
+            banks = [bank[:, :P] for bank in last_banks[half]]
+            second_product(dh[:, slots, :], dh_codes[:, slots], dh_plane[:, slots], wa_codes, wa_plane, banks)
+            for kt in range(K_TILES):
+                nc.scalar.copy(out=dx[:, kt, slots], in_=banks[kt])
+
+        pieces = [(kt, slice(h * BANK, (h + 1) * BANK)) for kt in range(K_TILES) for h in range(T // BANK)]
+        for bank, (kt, cols) in zip(base, pieces):
             for s in range(PASSES):
                 nc.tensor.matmul_mx(
                     out=bank[:],
@@ -253,76 +284,9 @@ def tile_moe_adb_relu2_kernel(
                     start=(s == 0),
                     stop=(s == PASSES - 1),
                 )
+        for half in range(HALVES):
+            for kt in range(K_TILES):
+                scatter(kt, LAST * C + half * P, dx[:, kt, half * P : (half + 1) * P])
+        for bank, (kt, cols) in zip(base, pieces):
             nc.vector.tensor_tensor(out=window[kt][:, cols], in0=bank[:], in1=window[kt][:, cols], op=ALU.add)
             nc.sync.dma_start(out=out[kt * P : (kt + 1) * P, cols], in_=window[kt][:, cols])
-
-        gate_sb = keep("gate_sb", [P, T], F32)
-
-        def spread_gate():
-            gate_cols = keep("gate_cols", [P, T // P], F32)
-            nc.tensor.transpose(acc[0][:, :P], gate_rows[:], identity[:])
-            nc.scalar.copy(out=gate_cols[:], in_=acc[0][:, : T // P])
-            for h in range(T // BANK):
-                for m in range(BANK // P):
-                    column = h * (BANK // P) + m
-                    nc.tensor.transpose(
-                        acc[1 + h][:, m * P : (m + 1) * P],
-                        gate_cols[:, column : column + 1].to_broadcast([P, P]),
-                        identity[:],
-                    )
-                nc.scalar.copy(out=gate_sb[:, h * BANK : (h + 1) * BANK], in_=acc[1 + h][:])
-
-        for item in HEADV:
-            if item == "g":
-                spread_gate()
-            elif item[0] == "d":
-                gather(slot_words[int(item[1])][:].bitcast(U32), dy[int(item[1])][:].bitcast(U32))
-            elif item == "s":
-                gather(slot_scales[:], dy_packed[:])
-            else:
-                quantize_wb(0, int(item[1]))
-        for e in range(E - 1):
-            make_factor(e)
-            first_product(e, 0)
-            first_product(e, 1)
-            quantize_wa(e)
-            second_product(
-                e, slice(0, C), wb_codes[CODES2][:, :C], wb_plane[CODES2][:, :C], [acc[0][:, :C], acc[0][:, C:]]
-            )
-            quantize_wb(e + 1, 0)
-            after = EVAC_AFTER[e]
-            if after == 1:
-                quantize_wb(e + 1, 1)
-            if after < 0:
-                dx = ring.tile([P, 2 * C], F32, name="dx", align_bytes=64)[:]
-                nc.vector.tensor_copy(out=dx, in_=acc[0][:])
-            else:
-                dx = as_row(wb_raw[e + 1, after])[:, PACK * H - 2 * C :]
-                nc.scalar.copy(out=dx, in_=acc[0][:])
-            for kt in range(K // P):
-                scatter(kt, e * C, dx[:, kt * C : (kt + 1) * C])
-            if after != 1:
-                quantize_wb(e + 1, 1)
-            quantize_wb(e + 1, 2)
-
-        last = E - 1
-        make_factor(last)
-        dx = ring.tile([P, 2 * C], F32, name="dx", align_bytes=64)
-        dh_codes = keep("dh_codes", [P, C], U32)
-        dh_plane = keep("dh_plane", [P, C], U8)
-        for half in range(C // P):
-            slots = slice(half * P, (half + 1) * P)
-            first_product(last, half)
-            if half == 0:
-                quantize_wa(last)
-            banks = [acc[2 * kt + half][:, :P] for kt in range(K // P)]
-            second_product(last, slots, dh_codes[:, slots], dh_plane[:, slots], banks)
-            for kt in range(K // P):
-                nc.scalar.copy(out=dx[:, kt * C + half * P : kt * C + (half + 1) * P], in_=banks[kt])
-        for kt, half in [(0, 0), (0, 1), (1, 0)]:
-            scatter(kt, last * C + half * P, dx[:, kt * C + half * P : kt * C + (half + 1) * P])
-        finish(0, 0)
-        scatter(1, last * C + P, dx[:, C + P :])
-        finish(0, 1)
-        finish(1, 0)
-        finish(1, 1)

@@ -52,7 +52,7 @@ def tile_moe_adb_relu2_kernel(
         offsets = held.tile([P, T // 16], U16, name="offsets")
         dy = [keep("dy%d" % s, [P, T], I32) for s in range(PASSES)]
         dy_packed = keep("dy_packed", [P, T], U8)
-        dy_plane = keep("dy_plane", [P, PASSES, T], U8)
+        dy_plane = keep("dy_plane", [P, PASSES - 1, T], U8)
         wt_codes = keep("wt_codes", [P, PASSES, 2 * K], U8)
         wt_plane = keep("wt_plane", [P, PASSES, K], U8)
         slot_words = [keep("slot_words%d" % s, [P, E * C], I32) for s in range(PASSES)]
@@ -91,6 +91,13 @@ def tile_moe_adb_relu2_kernel(
             for t in range(PACK):
                 nc.sync.dma_start(out=wa_raw[e][:, t, :], in_=rows[t])
 
+        def load_planes(planes, scales):
+            for quad in range(QUADS):
+                nc.sync.dma_start(
+                    out=planes[32 * quad : 32 * quad + 4, :, :].bitcast(I32),
+                    in_=scales[:, 4 * quad : 4 * quad + 4, :].rearrange("s b t -> b s t").bitcast(I32),
+                )
+
         nc.sync.dma_start(offsets[:], offs)
         load_dy(0)
         nc.sync.dma_start(out=gate_rows[: T // P, :], in_=gate[0, :].rearrange("(m p) -> m p", p=P))
@@ -102,43 +109,44 @@ def tile_moe_adb_relu2_kernel(
                 in_=dy_scales[:, 4 * quad : 4 * quad + 4, :].bitcast(I32),
             )
         load_wb(0, 1)
+        load_a(0, 1)
         load_dy(2)
         load_wb(0, 2)
-        load_a(0, 2)
         load_wa(0)
-        for e in range(1, LAST):
-            for s in range(PASSES):
-                load_wb(e, s)
+        for e in range(1, E):
+            if e == 2:
+                load_planes(dy_plane, dy_scales[1:])
+            load_wb(e, 0)
             if e not in a_sb:
-                load_a(e, 1)
-            load_wa(e)
-        for s in range(PASSES):
-            load_wb(LAST, s)
+                load_a(e, 2 if e < LAST else 1)
+            else:
+                nc.sync.dma_start(out=wt_codes[:].bitcast(I32), in_=wt_words.rearrange("s p b -> p s b").bitcast(I32))
+                load_planes(wt_plane, wt_scales)
+            load_wb(e, 1)
+            if e < LAST:
+                load_wa(e)
+            load_wb(e, 2)
         load_wa(LAST)
-        load_a(LAST, 1)
-        nc.sync.dma_start(out=wt_codes[:].bitcast(I32), in_=wt_words.rearrange("s p b -> p s b").bitcast(I32))
-        for quad in range(QUADS):
-            nc.sync.dma_start(
-                out=dy_plane[32 * quad : 32 * quad + 4, :, :].bitcast(I32),
-                in_=dy_scales[:, 4 * quad : 4 * quad + 4, :].rearrange("s b t -> b s t").bitcast(I32),
-            )
-            nc.sync.dma_start(
-                out=wt_plane[32 * quad : 32 * quad + 4, :, :].bitcast(I32),
-                in_=wt_scales[:, 4 * quad : 4 * quad + 4, :].rearrange("s b k -> b s k").bitcast(I32),
-            )
 
         staged = [keep("staged%d" % b, [P, PACK * H], BF16) for b in range(STAGES)]
-        wb_codes = [keep("wb_codes%d" % s, [P, H], U32) for s in range(PASSES)]
-        wb_plane = [keep("wb_plane%d" % s, [P, H], U8) for s in range(PASSES)]
+        wb_codes = [keep("wb_codes%d" % b, [P, H], U32) for b in range(STAGES)]
+        wb_plane = [keep("wb_plane%d" % b, [P, H], U8) for b in range(STAGES)]
         gate2 = keep("gate2", [P, T], F32)
         sums = [psum.tile([P, PACK, P], F32, name="sums%d" % half) for half in range(HALVES)]
         base = [psum.tile([P, BANK], F32, name="base%d" % b) for b in range(K_TILES * T // BANK)]
-        spare = psum.tile([P, BANK], F32, name="spare")
+        late_bank = psum.tile([P, BANK], F32, name="late_bank")
+        pieces = [(kt, slice(h * BANK, (h + 1) * BANK)) for kt in range(K_TILES) for h in range(T // BANK)]
+
+        def stage(e, s):
+            return (PASSES * e + s) % STAGES
+
+        def dx_bank(e, kt):
+            return (base[(e - 1) % len(base)] if kt == 0 else late_bank)[:, :C]
 
         def spread_gate():
             gate_cols = keep("gate_cols", [P, T // P], F32)
             nc.tensor.transpose(base[0][:, :P], gate_rows[:], identity[:])
-            nc.scalar.mul(gate_cols[:], base[0][:, : T // P], 2.0)
+            nc.scalar.copy(out=gate_cols[:], in_=base[0][:, : T // P])
             for h in range(T // BANK):
                 for m in range(BANK // P):
                     column = h * (BANK // P) + m
@@ -154,33 +162,53 @@ def tile_moe_adb_relu2_kernel(
                 nc.vector.tensor_copy(into[:, first : first + GATHER], source.indirect(list_slice(first, GATHER)))
 
         def quantize_wb(e, s):
-            rounded = staged[(PASSES * e + s) % STAGES][:]
+            rounded = staged[stage(e, s)][:]
             nc.scalar.copy(
                 out=rounded.rearrange("p (t c r d) -> p c t d r", t=PACK, r=RUN, d=PACK),
                 in_=wb_raw[e, s][:].rearrange("p d (c t r) -> p c t d r", t=PACK, r=RUN),
             )
-            nc.vector.quantize_mx(out=wb_codes[s][:].bitcast(FP8X4), scales=wb_plane[s][:], in_=rounded)
+            nc.vector.quantize_mx(
+                out=wb_codes[stage(e, s)][:].bitcast(FP8X4), scales=wb_plane[stage(e, s)][:], in_=rounded
+            )
 
-        def spent(e):
-            return as_row(wb_raw[e, PASSES - 1])
+        def spent(e, s):
+            return as_row(wb_raw[e, s])
 
-        def quantize_wa(e, codes, plane):
-            rounded = spent(e)[:, PACK * C : PACK * C + PACK * K // 2].bitcast(BF16)
+        def quantized(e, s):
+            return staged[stage(e, s)][:]
+
+        def round_wa_on_gpsimd(e):
+            rounded = quantized(e, 2)[:, : PACK * K]
+            nc.gpsimd.tensor_scalar(
+                out=rounded.rearrange("p (k t) -> p k t", t=PACK),
+                in0=wa_raw[e][:].rearrange("p t k -> p k t"),
+                scalar1=1.0,
+                scalar2=0.0,
+                op0=ALU.mult,
+                op1=ALU.add,
+            )
+            return rounded
+
+        def round_wa_on_scalar(e):
+            rounded = spent(e, 2)[:, PACK * C : PACK * C + PACK * K // 2].bitcast(BF16)
             nc.scalar.copy(
                 out=rounded.rearrange("p (c r t) -> p c t r", r=RUN, t=PACK),
                 in_=wa_raw[e][:].rearrange("p t (c r) -> p c t r", r=RUN),
             )
-            nc.vector.quantize_mx(out=codes.bitcast(FP8X4), scales=plane, in_=rounded)
+            return rounded
 
-        def make_factor(e):
-            factor = spent(e)[:, : PACK * C].rearrange("p (t j) -> p t j", t=PACK)
-            nc.vector.scalar_tensor_tensor(
+        def relu_twice(e):
+            doubled = quantized(e - 1, 2).bitcast(F32).rearrange("p (t j) -> p t j", t=PACK)
+            nc.vector.tensor_scalar(out=doubled, in0=a_sb[e], scalar1=0.0, scalar2=2.0, op0=ALU.max, op1=ALU.mult)
+            return doubled
+
+        def make_factor(e, doubled):
+            factor = quantized(e, 1).bitcast(F32).rearrange("p (t j) -> p t j", t=PACK)
+            nc.gpsimd.tensor_tensor(
                 out=factor,
-                in0=a_sb[e],
-                scalar=0.0,
+                in0=doubled,
                 in1=gate2[:, e * C : (e + 1) * C].unsqueeze(1).to_broadcast([P, PACK, C]),
-                op0=ALU.max,
-                op1=ALU.mult,
+                op=ALU.mult,
             )
             return factor
 
@@ -191,8 +219,8 @@ def tile_moe_adb_relu2_kernel(
                 for s in range(PASSES):
                     nc.tensor.matmul_mx(
                         out=sums[half][:, t, :],
-                        lhsT=wb_codes[s][:, t * P : (t + 1) * P].bitcast(FP8X4),
-                        lhsT_scale=wb_plane[s][:, t * P : (t + 1) * P],
+                        lhsT=wb_codes[stage(e, s)][:, t * P : (t + 1) * P].bitcast(FP8X4),
+                        lhsT_scale=wb_plane[stage(e, s)][:, t * P : (t + 1) * P],
                         rhs=slot_words[s][:, cols].bitcast(FP8X4),
                         rhs_scale=slot_scales[4 * s :, cols],
                         start=(s == 0),
@@ -223,67 +251,74 @@ def tile_moe_adb_relu2_kernel(
         def scatter(kt, first, values):
             nc.vector.tensor_copy(window[kt][:].indirect(list_slice(first, values.shape[1])), values)
 
+        def frozen_layer(piece):
+            kt, cols = pieces[piece]
+            for s in range(PASSES):
+                nc.tensor.matmul_mx(
+                    out=base[piece][:],
+                    lhsT=wt_codes[:, s, 2 * kt * P : 2 * (kt + 1) * P].bitcast(FP4X4),
+                    lhsT_scale=wt_plane[:, s, kt * P : (kt + 1) * P],
+                    rhs=dy[s][:, cols].bitcast(FP8X4),
+                    rhs_scale=dy_packed[:, cols] if s == 0 else dy_plane[:, s - 1, cols],
+                    start=(s == 0),
+                    stop=(s == PASSES - 1),
+                )
+
+        def empty_and_scatter(kt, e):
+            dx = spent(e + 1, kt + 1)[:, :C]
+            nc.scalar.copy(out=dx, in_=dx_bank(e, kt))
+            scatter(kt, e * C, dx)
+
         spread_gate()
         for s in range(PASSES):
             gather(slot_words[s][:].bitcast(U32), dy[s][:].bitcast(U32))
             if s == 0:
                 gather(slot_scales[:], dy_packed[:])
+            if s == 1:
+                doubled = relu_twice(0)
             quantize_wb(0, s)
+            if s == 1:
+                factor = make_factor(0, doubled)
 
-        held_back = None
         for e in range(LAST):
-            factor = make_factor(e)
-            if held_back is not None:
-                scatter(1, (e - 1) * C, held_back)
+            if e > 0:
+                empty_and_scatter(1, e - 1)
+            wa_rounded = round_wa_on_gpsimd(e)
             dh = ring.tile([P, C, PACK], BF16, name="dh", align_bytes=64)
             for half in range(HALVES):
                 first_product(e, half, factor, dh)
-            wa_codes, wa_plane = wb_codes[2][:, :K], wb_plane[2][:, :K]
-            quantize_wa(e, wa_codes, wa_plane)
-            banks = [base[1][:, :C], spare[:, :C]]
-            second_product(dh[:], wb_codes[1][:, :C], wb_plane[1][:, :C], wa_codes, wa_plane, banks)
             quantize_wb(e + 1, 0)
-            tiles_now = K_TILES if e == 0 else 1
-            dx = ring.tile([P, K_TILES, C], F32, name="dx", align_bytes=64)
-            for kt in range(tiles_now):
-                nc.vector.tensor_copy(out=dx[:, kt, :], in_=banks[kt])
-            for kt in range(tiles_now):
-                scatter(kt, e * C, dx[:, kt, :])
+            wa_codes, wa_plane = wb_codes[stage(e + 1, 2)][:, :K], wb_plane[stage(e + 1, 2)][:, :K]
+            nc.vector.quantize_mx(out=wa_codes.bitcast(FP8X4), scales=wa_plane, in_=wa_rounded)
+            banks = [dx_bank(e, kt) for kt in range(K_TILES)]
+            dh_codes, dh_plane = wb_codes[stage(e + 1, 1)][:, :C], wb_plane[stage(e + 1, 1)][:, :C]
+            second_product(dh[:], dh_codes, dh_plane, wa_codes, wa_plane, banks)
+            doubled = relu_twice(e + 1)
             quantize_wb(e + 1, 1)
-            quantize_wb(e + 1, 2)
+            factor = make_factor(e + 1, doubled)
+            empty_and_scatter(0, e)
             if e > 0:
-                held_back = spent(e + 1)[:, PACK * H - C :]
-                nc.scalar.copy(out=held_back, in_=banks[1])
+                frozen_layer(e - 1)
+            quantize_wb(e + 1, 2)
 
-        factor = make_factor(LAST)
-        scatter(1, (LAST - 1) * C, held_back)
+        empty_and_scatter(1, LAST - 1)
+        wa_rounded = round_wa_on_scalar(LAST)
         dh = ring.tile([P, C, PACK], BF16, name="dh", align_bytes=64)
-        dx = ring.tile([P, K_TILES, C], F32, name="dx", align_bytes=64)
+        dx = keep("dx", [P, K_TILES, C], F32)
         wa_codes, wa_plane = keep("wa_codes", [P, K], U32)[:], keep("wa_plane", [P, K], U8)[:]
         dh_codes, dh_plane = keep("dh_codes", [P, C], U32), keep("dh_plane", [P, C], U8)
-        last_banks = [[spare, base[1]], [base[2], base[3]]]
         for half in range(HALVES):
             slots = slice(half * P, (half + 1) * P)
             first_product(LAST, half, factor, dh)
             if half == 0:
-                quantize_wa(LAST, wa_codes, wa_plane)
-            banks = [bank[:, :P] for bank in last_banks[half]]
+                nc.vector.quantize_mx(out=wa_codes.bitcast(FP8X4), scales=wa_plane, in_=wa_rounded)
+            banks = [base[K_TILES + half][:, kt * P : (kt + 1) * P] for kt in range(K_TILES)]
             second_product(dh[:, slots, :], dh_codes[:, slots], dh_plane[:, slots], wa_codes, wa_plane, banks)
-            for kt in range(K_TILES):
-                nc.scalar.copy(out=dx[:, kt, slots], in_=banks[kt])
+            both = base[K_TILES + half][:, : K_TILES * P].rearrange("p (kt j) -> p kt j", kt=K_TILES)
+            nc.scalar.copy(out=dx[:, :, slots], in_=both)
 
-        pieces = [(kt, slice(h * BANK, (h + 1) * BANK)) for kt in range(K_TILES) for h in range(T // BANK)]
-        for bank, (kt, cols) in zip(base, pieces):
-            for s in range(PASSES):
-                nc.tensor.matmul_mx(
-                    out=bank[:],
-                    lhsT=wt_codes[:, s, 2 * kt * P : 2 * (kt + 1) * P].bitcast(FP4X4),
-                    lhsT_scale=wt_plane[:, s, kt * P : (kt + 1) * P],
-                    rhs=dy[s][:, cols].bitcast(FP8X4),
-                    rhs_scale=dy_plane[:, s, cols],
-                    start=(s == 0),
-                    stop=(s == PASSES - 1),
-                )
+        for piece in range(K_TILES, len(pieces)):
+            frozen_layer(piece)
         for half in range(HALVES):
             for kt in range(K_TILES):
                 scatter(kt, LAST * C + half * P, dx[:, kt, half * P : (half + 1) * P])

@@ -79,17 +79,17 @@ def tile_moe_adb_relu2_kernel(
 
         def load_a(e, count):
             tile = keep("a%d" % e, [P, PACK, count * C], F32)
-            rows = a.rearrange("(c t r) j -> t c r j", t=PACK, r=RUN)
+            rows = a.rearrange("(c u r v) j -> u v c r j", u=2, r=2, v=2)
             for t in range(PACK):
-                nc.sync.dma_start(out=tile[:, t, :], in_=rows[t, :, :, e * C : (e + count) * C])
+                nc.sync.dma_start(out=tile[:, t, :], in_=rows[t // 2, t % 2, :, :, e * C : (e + count) * C])
             for u in range(count):
                 a_sb[e + u] = tile[:, :, u * C : (u + 1) * C]
 
         def load_wa(e):
             wa_raw[e] = keep("wa_raw%d" % e, [P, PACK, K], F32)
-            rows = wat[e].rearrange("(c t r) k -> t c r k", t=PACK, r=RUN)
-            for t in range(PACK):
-                nc.sync.dma_start(out=wa_raw[e][:, t, :], in_=rows[t])
+            rows = wat[e].rearrange("(c u r v) k -> u c r (v k)", u=2, r=2, v=2)
+            for u in range(2):
+                nc.sync.dma_start(out=as_row(wa_raw[e])[:, 2 * u * K : 2 * (u + 1) * K], in_=rows[u])
 
         def load_planes(planes, scales):
             for quad in range(QUADS):
@@ -113,20 +113,21 @@ def tile_moe_adb_relu2_kernel(
         load_dy(2)
         load_wb(0, 2)
         load_wa(0)
-        for e in range(1, E):
-            if e == 2:
-                load_planes(dy_plane, dy_scales[1:])
+        for e in range(1, LAST):
             load_wb(e, 0)
             if e not in a_sb:
-                load_a(e, 2 if e < LAST else 1)
-            else:
-                nc.sync.dma_start(out=wt_codes[:].bitcast(I32), in_=wt_words.rearrange("s p b -> p s b").bitcast(I32))
-                load_planes(wt_plane, wt_scales)
+                load_a(e, 2)
             load_wb(e, 1)
-            if e < LAST:
-                load_wa(e)
+            load_wa(e)
             load_wb(e, 2)
+        load_wb(LAST, 0)
+        load_a(LAST, 1)
+        load_wb(LAST, 1)
+        load_wb(LAST, 2)
         load_wa(LAST)
+        nc.sync.dma_start(out=wt_codes[:].bitcast(I32), in_=wt_words.rearrange("s p b -> p s b").bitcast(I32))
+        load_planes(dy_plane, dy_scales[1:])
+        load_planes(wt_plane, wt_scales)
 
         staged = [keep("staged%d" % b, [P, PACK * H], BF16) for b in range(STAGES)]
         wb_codes = [keep("wb_codes%d" % b, [P, H], U32) for b in range(STAGES)]
@@ -134,14 +135,11 @@ def tile_moe_adb_relu2_kernel(
         gate2 = keep("gate2", [P, T], F32)
         sums = [psum.tile([P, PACK, P], F32, name="sums%d" % half) for half in range(HALVES)]
         base = [psum.tile([P, BANK], F32, name="base%d" % b) for b in range(K_TILES * T // BANK)]
-        late_bank = psum.tile([P, BANK], F32, name="late_bank")
+        dx_bank = [psum.tile([P, BANK], F32, name="dx_bank%d" % kt) for kt in range(K_TILES)]
         pieces = [(kt, slice(h * BANK, (h + 1) * BANK)) for kt in range(K_TILES) for h in range(T // BANK)]
 
         def stage(e, s):
             return (PASSES * e + s) % STAGES
-
-        def dx_bank(e, kt):
-            return (base[(e - 1) % len(base)] if kt == 0 else late_bank)[:, :C]
 
         def spread_gate():
             gate_cols = keep("gate_cols", [P, T // P], F32)
@@ -162,14 +160,19 @@ def tile_moe_adb_relu2_kernel(
                 nc.vector.tensor_copy(into[:, first : first + GATHER], source.indirect(list_slice(first, GATHER)))
 
         def quantize_wb(e, s):
-            rounded = staged[stage(e, s)][:]
-            nc.scalar.copy(
-                out=rounded.rearrange("p (t c r d) -> p c t d r", t=PACK, r=RUN, d=PACK),
-                in_=wb_raw[e, s][:].rearrange("p d (c t r) -> p c t d r", t=PACK, r=RUN),
-            )
-            nc.vector.quantize_mx(
-                out=wb_codes[stage(e, s)][:].bitcast(FP8X4), scales=wb_plane[stage(e, s)][:], in_=rounded
-            )
+            rounded, codes, plane = staged[stage(e, s)], wb_codes[stage(e, s)], wb_plane[stage(e, s)]
+            raw = wb_raw[e, s][:].rearrange("p d (c u q) -> p d c u q", u=2, q=RUN)
+            for u in range(2):
+                values = rounded[:, u * 2 * H : (u + 1) * 2 * H]
+                nc.scalar.copy(
+                    out=values.rearrange("p (v c r d) -> p c d r v", v=2, r=2, d=PACK),
+                    in_=raw[:, :, :, u, :].rearrange("p d c (r v) -> p c d r v", v=2),
+                )
+                if s == PASSES - 1:
+                    cols = slice(u * H // 2, (u + 1) * H // 2)
+                    nc.vector.quantize_mx(out=codes[:, cols].bitcast(FP8X4), scales=plane[:, cols], in_=values)
+            if s < PASSES - 1:
+                nc.vector.quantize_mx(out=codes[:].bitcast(FP8X4), scales=plane[:], in_=rounded[:])
 
         def spent(e, s):
             return as_row(wb_raw[e, s])
@@ -177,55 +180,47 @@ def tile_moe_adb_relu2_kernel(
         def quantized(e, s):
             return staged[stage(e, s)][:]
 
-        def round_wa_on_gpsimd(e):
-            rounded = quantized(e, 2)[:, : PACK * K]
-            nc.gpsimd.tensor_scalar(
-                out=rounded.rearrange("p (k t) -> p k t", t=PACK),
-                in0=wa_raw[e][:].rearrange("p t k -> p k t"),
-                scalar1=1.0,
-                scalar2=0.0,
-                op0=ALU.mult,
-                op1=ALU.add,
-            )
-            return rounded
-
-        def round_wa_on_scalar(e):
-            rounded = spent(e, 2)[:, PACK * C : PACK * C + PACK * K // 2].bitcast(BF16)
-            nc.scalar.copy(
-                out=rounded.rearrange("p (c r t) -> p c t r", r=RUN, t=PACK),
+        def round_wa(e):
+            rounded = ring.tile([P, PACK * K], BF16, name="wa_rounded", align_bytes=64)
+            nc.vector.tensor_copy(
+                out=rounded[:].rearrange("p (c r t) -> p c t r", r=RUN, t=PACK),
                 in_=wa_raw[e][:].rearrange("p t (c r) -> p c t r", r=RUN),
             )
-            return rounded
+            return rounded[:]
 
         def relu_twice(e):
-            doubled = quantized(e - 1, 2).bitcast(F32).rearrange("p (t j) -> p t j", t=PACK)
-            nc.vector.tensor_scalar(out=doubled, in0=a_sb[e], scalar1=0.0, scalar2=2.0, op0=ALU.max, op1=ALU.mult)
-            return doubled
+            nc.vector.tensor_scalar(out=a_sb[e], in0=a_sb[e], scalar1=0.0, scalar2=2.0, op0=ALU.max, op1=ALU.mult)
 
-        def make_factor(e, doubled):
+        def make_factor(e):
             factor = quantized(e, 1).bitcast(F32).rearrange("p (t j) -> p t j", t=PACK)
             nc.gpsimd.tensor_tensor(
                 out=factor,
-                in0=doubled,
+                in0=a_sb[e],
                 in1=gate2[:, e * C : (e + 1) * C].unsqueeze(1).to_broadcast([P, PACK, C]),
                 op=ALU.mult,
             )
             return factor
 
-        def first_product(e, half, factor, dh):
-            cols = slice(e * C + half * P, e * C + (half + 1) * P)
+        def first_product(e):
+            def one_pass(half, t, s):
+                cols = slice(e * C + half * P, e * C + (half + 1) * P)
+                nc.tensor.matmul_mx(
+                    out=sums[half][:, t, :],
+                    lhsT=wb_codes[stage(e, s)][:, t * P : (t + 1) * P].bitcast(FP8X4),
+                    lhsT_scale=wb_plane[stage(e, s)][:, t * P : (t + 1) * P],
+                    rhs=slot_words[s][:, cols].bitcast(FP8X4),
+                    rhs_scale=slot_scales[4 * s :, cols],
+                    start=(s == 0),
+                    stop=(s == PASSES - 1),
+                )
+
+            for half in range(HALVES):
+                for t in range(PACK):
+                    for s in range(PASSES):
+                        one_pass(half, t, s)
+
+        def make_dh(half, factor, dh):
             slots = slice(half * P, (half + 1) * P)
-            for t in range(PACK):
-                for s in range(PASSES):
-                    nc.tensor.matmul_mx(
-                        out=sums[half][:, t, :],
-                        lhsT=wb_codes[stage(e, s)][:, t * P : (t + 1) * P].bitcast(FP8X4),
-                        lhsT_scale=wb_plane[stage(e, s)][:, t * P : (t + 1) * P],
-                        rhs=slot_words[s][:, cols].bitcast(FP8X4),
-                        rhs_scale=slot_scales[4 * s :, cols],
-                        start=(s == 0),
-                        stop=(s == PASSES - 1),
-                    )
             nc.vector.tensor_tensor(
                 out=dh[:, slots, :].rearrange("p (c r) t -> p c t r", r=RUN),
                 in0=sums[half][:].rearrange("p t (c r) -> p c t r", r=RUN),
@@ -264,64 +259,60 @@ def tile_moe_adb_relu2_kernel(
                     stop=(s == PASSES - 1),
                 )
 
-        def empty_and_scatter(kt, e):
-            dx = spent(e + 1, kt + 1)[:, :C]
-            nc.scalar.copy(out=dx, in_=dx_bank(e, kt))
-            scatter(kt, e * C, dx)
+        def empty_and_scatter(through, e, kt, first, count):
+            nc.scalar.copy(out=through[:, :count], in_=dx_bank[kt][:, first : first + count])
+            scatter(kt, e * C + first, through[:, :count])
 
         spread_gate()
         for s in range(PASSES):
             gather(slot_words[s][:].bitcast(U32), dy[s][:].bitcast(U32))
             if s == 0:
                 gather(slot_scales[:], dy_packed[:])
-            if s == 1:
-                doubled = relu_twice(0)
             quantize_wb(0, s)
             if s == 1:
-                factor = make_factor(0, doubled)
+                relu_twice(0)
+                factor = make_factor(0)
 
         for e in range(LAST):
-            if e > 0:
-                empty_and_scatter(1, e - 1)
-            wa_rounded = round_wa_on_gpsimd(e)
+            wa_rounded = round_wa(e)
             dh = ring.tile([P, C, PACK], BF16, name="dh", align_bytes=64)
-            for half in range(HALVES):
-                first_product(e, half, factor, dh)
-            quantize_wb(e + 1, 0)
+            first_product(e)
             wa_codes, wa_plane = wb_codes[stage(e + 1, 2)][:, :K], wb_plane[stage(e + 1, 2)][:, :K]
             nc.vector.quantize_mx(out=wa_codes.bitcast(FP8X4), scales=wa_plane, in_=wa_rounded)
-            banks = [dx_bank(e, kt) for kt in range(K_TILES)]
+            for half in range(HALVES):
+                make_dh(half, factor, dh)
+            banks = [bank[:, :C] for bank in dx_bank]
             dh_codes, dh_plane = wb_codes[stage(e + 1, 1)][:, :C], wb_plane[stage(e + 1, 1)][:, :C]
             second_product(dh[:], dh_codes, dh_plane, wa_codes, wa_plane, banks)
-            doubled = relu_twice(e + 1)
+            relu_twice(e + 1)
+            quantize_wb(e + 1, 0)
             quantize_wb(e + 1, 1)
-            factor = make_factor(e + 1, doubled)
-            empty_and_scatter(0, e)
-            if e > 0:
-                frozen_layer(e - 1)
+            factor = make_factor(e + 1)
+            empty_and_scatter(spent(e + 1, 1), e, 0, 0, C)
             quantize_wb(e + 1, 2)
+            empty_and_scatter(spent(e + 1, 2), e, 1, 0, C)
 
-        empty_and_scatter(1, LAST - 1)
-        wa_rounded = round_wa_on_scalar(LAST)
+        wa_rounded = round_wa(LAST)
+        first_product(LAST)
         dh = ring.tile([P, C, PACK], BF16, name="dh", align_bytes=64)
         dx = keep("dx", [P, K_TILES, C], F32)
         wa_codes, wa_plane = keep("wa_codes", [P, K], U32)[:], keep("wa_plane", [P, K], U8)[:]
         dh_codes, dh_plane = keep("dh_codes", [P, C], U32), keep("dh_plane", [P, C], U8)
         for half in range(HALVES):
             slots = slice(half * P, (half + 1) * P)
-            first_product(LAST, half, factor, dh)
+            make_dh(half, factor, dh)
             if half == 0:
                 nc.vector.quantize_mx(out=wa_codes.bitcast(FP8X4), scales=wa_plane, in_=wa_rounded)
-            banks = [base[K_TILES + half][:, kt * P : (kt + 1) * P] for kt in range(K_TILES)]
+            banks = [base[K_TILES * half + kt][:, :P] for kt in range(K_TILES)]
             second_product(dh[:, slots, :], dh_codes[:, slots], dh_plane[:, slots], wa_codes, wa_plane, banks)
-            both = base[K_TILES + half][:, : K_TILES * P].rearrange("p (kt j) -> p kt j", kt=K_TILES)
-            nc.scalar.copy(out=dx[:, :, slots], in_=both)
+            for kt in range(K_TILES):
+                nc.scalar.copy(out=dx[:, kt, slots], in_=banks[kt])
 
-        for piece in range(K_TILES, len(pieces)):
+        for piece in range(len(pieces)):
             frozen_layer(piece)
         for half in range(HALVES):
             for kt in range(K_TILES):
                 scatter(kt, LAST * C + half * P, dx[:, kt, half * P : (half + 1) * P])
-        for bank, (kt, cols) in zip(base, pieces):
-            nc.vector.tensor_tensor(out=window[kt][:, cols], in0=bank[:], in1=window[kt][:, cols], op=ALU.add)
+        for piece, (kt, cols) in enumerate(pieces):
+            nc.vector.tensor_tensor(out=window[kt][:, cols], in0=base[piece][:], in1=window[kt][:, cols], op=ALU.add)
             nc.sync.dma_start(out=out[kt * P : (kt + 1) * P, cols], in_=window[kt][:, cols])

@@ -109,22 +109,16 @@ def tile_moe_adb_relu2_kernel(
                 in_=dy_scales[:, 4 * quad : 4 * quad + 4, :].bitcast(I32),
             )
         load_wb(0, 1)
-        load_a(0, 1)
         load_dy(2)
         load_wb(0, 2)
+        load_a(0, 2)
         load_wa(0)
-        for e in range(1, LAST):
-            load_wb(e, 0)
+        for e in range(1, E):
+            for s in range(PASSES):
+                load_wb(e, s)
             if e not in a_sb:
-                load_a(e, 2)
-            load_wb(e, 1)
+                load_a(e, 1)
             load_wa(e)
-            load_wb(e, 2)
-        load_wb(LAST, 0)
-        load_a(LAST, 1)
-        load_wb(LAST, 1)
-        load_wb(LAST, 2)
-        load_wa(LAST)
         nc.sync.dma_start(out=wt_codes[:].bitcast(I32), in_=wt_words.rearrange("s p b -> p s b").bitcast(I32))
         load_planes(dy_plane, dy_scales[1:])
         load_planes(wt_plane, wt_scales)
@@ -134,7 +128,8 @@ def tile_moe_adb_relu2_kernel(
         wb_plane = [keep("wb_plane%d" % b, [P, H], U8) for b in range(STAGES)]
         gate2 = keep("gate2", [P, T], F32)
         sums = [psum.tile([P, PACK, P], F32, name="sums%d" % half) for half in range(HALVES)]
-        base = [psum.tile([P, BANK], F32, name="base%d" % b) for b in range(K_TILES * T // BANK)]
+        spare = [psum.tile([P, BANK], F32, name="spare%d" % half) for half in range(HALVES)]
+        base = [as_row(bank) for bank in sums] + [bank[:] for bank in spare]
         dx_bank = [psum.tile([P, BANK], F32, name="dx_bank%d" % kt) for kt in range(K_TILES)]
         pieces = [(kt, slice(h * BANK, (h + 1) * BANK)) for kt in range(K_TILES) for h in range(T // BANK)]
 
@@ -144,7 +139,7 @@ def tile_moe_adb_relu2_kernel(
         def spread_gate():
             gate_cols = keep("gate_cols", [P, T // P], F32)
             nc.tensor.transpose(base[0][:, :P], gate_rows[:], identity[:])
-            nc.scalar.copy(out=gate_cols[:], in_=base[0][:, : T // P])
+            nc.scalar.mul(gate_cols[:], base[0][:, : T // P], 2.0)
             for h in range(T // BANK):
                 for m in range(BANK // P):
                     column = h * (BANK // P) + m
@@ -153,7 +148,7 @@ def tile_moe_adb_relu2_kernel(
                         gate_cols[:, column : column + 1].to_broadcast([P, P]),
                         identity[:],
                     )
-                nc.scalar.copy(out=gate2[:, h * BANK : (h + 1) * BANK], in_=base[1 + h][:])
+                nc.scalar.copy(out=gate2[:, h * BANK : (h + 1) * BANK], in_=base[1 + h])
 
         def gather(into, source):
             for first in range(0, E * C, GATHER):
@@ -181,23 +176,22 @@ def tile_moe_adb_relu2_kernel(
             return staged[stage(e, s)][:]
 
         def round_wa(e):
-            rounded = ring.tile([P, PACK * K], BF16, name="wa_rounded", align_bytes=64)
-            nc.vector.tensor_copy(
-                out=rounded[:].rearrange("p (c r t) -> p c t r", r=RUN, t=PACK),
+            rounded = spent(e, 2)[:, PACK * C : PACK * C + PACK * K // 2].bitcast(BF16)
+            nc.scalar.copy(
+                out=rounded.rearrange("p (c r t) -> p c t r", r=RUN, t=PACK),
                 in_=wa_raw[e][:].rearrange("p t (c r) -> p c t r", r=RUN),
             )
-            return rounded[:]
-
-        def relu_twice(e):
-            nc.vector.tensor_scalar(out=a_sb[e], in0=a_sb[e], scalar1=0.0, scalar2=2.0, op0=ALU.max, op1=ALU.mult)
+            return rounded
 
         def make_factor(e):
             factor = quantized(e, 1).bitcast(F32).rearrange("p (t j) -> p t j", t=PACK)
-            nc.gpsimd.tensor_tensor(
+            nc.vector.scalar_tensor_tensor(
                 out=factor,
                 in0=a_sb[e],
+                scalar=0.0,
                 in1=gate2[:, e * C : (e + 1) * C].unsqueeze(1).to_broadcast([P, PACK, C]),
-                op=ALU.mult,
+                op0=ALU.max,
+                op1=ALU.mult,
             )
             return factor
 
@@ -222,9 +216,9 @@ def tile_moe_adb_relu2_kernel(
         def make_dh(half, factor, dh):
             slots = slice(half * P, (half + 1) * P)
             nc.vector.tensor_tensor(
-                out=dh[:, slots, :].rearrange("p (c r) t -> p c t r", r=RUN),
-                in0=sums[half][:].rearrange("p t (c r) -> p c t r", r=RUN),
-                in1=factor[:, :, slots].rearrange("p t (c r) -> p c t r", r=RUN),
+                out=dh[:, slots, :].rearrange("p (c r) t -> p c t r", r=2),
+                in0=sums[half][:].rearrange("p t (c r) -> p c t r", r=2),
+                in1=factor[:, :, slots].rearrange("p t (c r) -> p c t r", r=2),
                 op=ALU.mult,
             )
 
@@ -250,7 +244,7 @@ def tile_moe_adb_relu2_kernel(
             kt, cols = pieces[piece]
             for s in range(PASSES):
                 nc.tensor.matmul_mx(
-                    out=base[piece][:],
+                    out=base[piece],
                     lhsT=wt_codes[:, s, 2 * kt * P : 2 * (kt + 1) * P].bitcast(FP4X4),
                     lhsT_scale=wt_plane[:, s, kt * P : (kt + 1) * P],
                     rhs=dy[s][:, cols].bitcast(FP8X4),
@@ -259,9 +253,9 @@ def tile_moe_adb_relu2_kernel(
                     stop=(s == PASSES - 1),
                 )
 
-        def empty_and_scatter(through, e, kt, first, count):
-            nc.scalar.copy(out=through[:, :count], in_=dx_bank[kt][:, first : first + count])
-            scatter(kt, e * C + first, through[:, :count])
+        def empty_and_scatter(copy, through, e, kt):
+            copy(out=through[:, :C], in_=dx_bank[kt][:, :C])
+            scatter(kt, e * C, through[:, :C])
 
         spread_gate()
         for s in range(PASSES):
@@ -270,7 +264,6 @@ def tile_moe_adb_relu2_kernel(
                 gather(slot_scales[:], dy_packed[:])
             quantize_wb(0, s)
             if s == 1:
-                relu_twice(0)
                 factor = make_factor(0)
 
         for e in range(LAST):
@@ -284,13 +277,12 @@ def tile_moe_adb_relu2_kernel(
             banks = [bank[:, :C] for bank in dx_bank]
             dh_codes, dh_plane = wb_codes[stage(e + 1, 1)][:, :C], wb_plane[stage(e + 1, 1)][:, :C]
             second_product(dh[:], dh_codes, dh_plane, wa_codes, wa_plane, banks)
-            relu_twice(e + 1)
             quantize_wb(e + 1, 0)
+            empty_and_scatter(nc.vector.tensor_copy, spent(e, 1), e, 0)
             quantize_wb(e + 1, 1)
             factor = make_factor(e + 1)
-            empty_and_scatter(spent(e + 1, 1), e, 0, 0, C)
             quantize_wb(e + 1, 2)
-            empty_and_scatter(spent(e + 1, 2), e, 1, 0, C)
+            empty_and_scatter(nc.scalar.copy, spent(e + 1, 2), e, 1)
 
         wa_rounded = round_wa(LAST)
         first_product(LAST)
@@ -303,10 +295,10 @@ def tile_moe_adb_relu2_kernel(
             make_dh(half, factor, dh)
             if half == 0:
                 nc.vector.quantize_mx(out=wa_codes.bitcast(FP8X4), scales=wa_plane, in_=wa_rounded)
-            banks = [base[K_TILES * half + kt][:, :P] for kt in range(K_TILES)]
+            banks = [spare[half][:, kt * P : (kt + 1) * P] for kt in range(K_TILES)]
             second_product(dh[:, slots, :], dh_codes[:, slots], dh_plane[:, slots], wa_codes, wa_plane, banks)
-            for kt in range(K_TILES):
-                nc.scalar.copy(out=dx[:, kt, slots], in_=banks[kt])
+            both = spare[half][:, : K_TILES * P].rearrange("p (kt j) -> p kt j", kt=K_TILES)
+            nc.scalar.copy(out=dx[:, :, slots], in_=both)
 
         for piece in range(len(pieces)):
             frozen_layer(piece)
@@ -314,5 +306,9 @@ def tile_moe_adb_relu2_kernel(
             for kt in range(K_TILES):
                 scatter(kt, LAST * C + half * P, dx[:, kt, half * P : (half + 1) * P])
         for piece, (kt, cols) in enumerate(pieces):
-            nc.vector.tensor_tensor(out=window[kt][:, cols], in0=base[piece][:], in1=window[kt][:, cols], op=ALU.add)
-            nc.sync.dma_start(out=out[kt * P : (kt + 1) * P, cols], in_=window[kt][:, cols])
+            width = BANK if piece < len(pieces) - 1 else BANK // 2
+            for first in range(0, BANK, width):
+                tokens = slice(cols.start + first, cols.start + first + width)
+                sums_here = base[piece][:, first : first + width]
+                nc.vector.tensor_tensor(out=window[kt][:, tokens], in0=sums_here, in1=window[kt][:, tokens], op=ALU.add)
+                nc.sync.dma_start(out=out[kt * P : (kt + 1) * P, tokens], in_=window[kt][:, tokens])

@@ -101,15 +101,15 @@ def tile_moe_adb_relu2_kernel(
         nc.sync.dma_start(offsets[:], offs)
         load_dy(0)
         nc.sync.dma_start(out=gate_rows[: T // P, :], in_=gate[0, :].rearrange("(m p) -> m p", p=P))
-        load_wb(0, 0)
         load_dy(1)
+        load_wb(0, 0)
         for quad in range(QUADS):
             nc.sync.dma_start(
                 out=dy_packed[32 * quad : 32 * quad + 4 * PASSES, :].bitcast(I32),
                 in_=dy_scales[:, 4 * quad : 4 * quad + 4, :].bitcast(I32),
             )
-        load_wb(0, 1)
         load_dy(2)
+        load_wb(0, 1)
         load_wb(0, 2)
         load_a(0, 2)
         load_wa(0)
@@ -174,6 +174,18 @@ def tile_moe_adb_relu2_kernel(
 
         def quantized(e, s):
             return staged[stage(e, s)][:]
+
+        def round_wa_on_gpsimd(e):
+            rounded = quantized(e, 2)[:, PACK * H - PACK * K :]
+            nc.gpsimd.tensor_scalar(
+                out=rounded.rearrange("p (k t) -> p k t", t=PACK),
+                in0=wa_raw[e][:].rearrange("p t k -> p k t"),
+                scalar1=1.0,
+                scalar2=0.0,
+                op0=ALU.mult,
+                op1=ALU.add,
+            )
+            return rounded
 
         def round_wa(e):
             rounded = spent(e, 2)[:, PACK * C : PACK * C + PACK * K // 2].bitcast(BF16)
@@ -267,18 +279,18 @@ def tile_moe_adb_relu2_kernel(
                 factor = make_factor(0)
 
         for e in range(LAST):
-            wa_rounded = round_wa(e)
+            wa_rounded = round_wa_on_gpsimd(e)
             dh = ring.tile([P, C, PACK], BF16, name="dh", align_bytes=64)
             first_product(e)
-            wa_codes, wa_plane = wb_codes[stage(e + 1, 2)][:, :K], wb_plane[stage(e + 1, 2)][:, :K]
-            nc.vector.quantize_mx(out=wa_codes.bitcast(FP8X4), scales=wa_plane, in_=wa_rounded)
             for half in range(HALVES):
                 make_dh(half, factor, dh)
+            wa_codes, wa_plane = wb_codes[stage(e, 2)][:, :K], wb_plane[stage(e, 2)][:, :K]
+            nc.vector.quantize_mx(out=wa_codes.bitcast(FP8X4), scales=wa_plane, in_=wa_rounded)
             banks = [bank[:, :C] for bank in dx_bank]
             dh_codes, dh_plane = wb_codes[stage(e + 1, 1)][:, :C], wb_plane[stage(e + 1, 1)][:, :C]
             second_product(dh[:], dh_codes, dh_plane, wa_codes, wa_plane, banks)
             quantize_wb(e + 1, 0)
-            empty_and_scatter(nc.vector.tensor_copy, spent(e, 1), e, 0)
+            empty_and_scatter(nc.vector.tensor_copy, quantized(e + 1, 0).bitcast(F32), e, 0)
             quantize_wb(e + 1, 1)
             factor = make_factor(e + 1)
             quantize_wb(e + 1, 2)

@@ -16,10 +16,10 @@ U8 = mybir.dt.uint8
 FP8X4 = mybir.dt.float8_e4m3fn_x4
 FP4X4 = mybir.dt.float4_e2m1fn_x4
 ALU = mybir.AluOpType
+COPY = mybir.ActivationFunctionType.Copy
 
 P = 128
 PACK = 4
-RUN = 4
 PASS = P * PACK
 PASSES = N // PASS
 BANK = 512
@@ -27,7 +27,6 @@ K_TILES = K // P
 HALVES = C // P
 QUADS = P // 32
 GATHER = T // 2
-STAGES = 2 * PASSES
 LAST = E - 1
 
 
@@ -43,8 +42,8 @@ def tile_moe_adb_relu2_kernel(
         def keep(name, shape, dtype):
             return held.tile(shape, dtype, name=name, align_bytes=64)
 
-        def as_row(tile):
-            return tile[:].rearrange("p j c -> p (j c)")
+        def turn(name, shape, dtype):
+            return ring.tile(shape, dtype, name=name, align_bytes=64)
 
         def list_slice(first, count):
             return offsets[:, first // 16 : (first + count) // 16]
@@ -77,25 +76,20 @@ def tile_moe_adb_relu2_kernel(
             rows = wbt[e, s * PASS : (s + 1) * PASS, :].rearrange("(p d) i -> p d i", d=PACK)
             nc.sync.dma_start(out=wb_raw[e, s][:], in_=rows)
 
-        def load_a(e, count):
-            tile = keep("a%d" % e, [P, PACK, count * C], F32)
-            rows = a.rearrange("(c u r v) j -> u v c r j", u=2, r=2, v=2)
-            for t in range(PACK):
-                nc.sync.dma_start(out=tile[:, t, :], in_=rows[t // 2, t % 2, :, :, e * C : (e + count) * C])
-            for u in range(count):
-                a_sb[e + u] = tile[:, :, u * C : (u + 1) * C]
+        def load_a(e):
+            a_sb[e] = keep("a%d" % e, [P, PACK, C], F32)
+            rows = a.rearrange("(p t) j -> p t j", t=PACK)
+            nc.sync.dma_start(out=a_sb[e][:], in_=rows[:, :, e * C : (e + 1) * C])
 
         def load_wa(e):
             wa_raw[e] = keep("wa_raw%d" % e, [P, PACK, K], F32)
-            rows = wat[e].rearrange("(c u r v) k -> u c r (v k)", u=2, r=2, v=2)
-            for u in range(2):
-                nc.sync.dma_start(out=as_row(wa_raw[e])[:, 2 * u * K : 2 * (u + 1) * K], in_=rows[u])
+            nc.sync.dma_start(out=wa_raw[e][:], in_=wat[e].rearrange("(p t) k -> p t k", t=PACK))
 
         def load_planes(planes, scales):
-            for quad in range(QUADS):
+            for row in range(4):
                 nc.sync.dma_start(
-                    out=planes[32 * quad : 32 * quad + 4, :, :].bitcast(I32),
-                    in_=scales[:, 4 * quad : 4 * quad + 4, :].rearrange("s b t -> b s t").bitcast(I32),
+                    out=planes[row:P:32, :, :].bitcast(I32),
+                    in_=scales[:, row::4, :].rearrange("s q t -> q s t").bitcast(I32),
                 )
 
         nc.sync.dma_start(offsets[:], offs)
@@ -109,32 +103,23 @@ def tile_moe_adb_relu2_kernel(
                 in_=dy_scales[:, 4 * quad : 4 * quad + 4, :].bitcast(I32),
             )
         load_dy(2)
-        load_wb(0, 1)
-        load_wb(0, 2)
-        load_a(0, 2)
-        load_wa(0)
-        for e in range(1, E):
+        for e in range(E):
+            if e == LAST:
+                nc.sync.dma_start(out=wt_codes[:].bitcast(I32), in_=wt_words.rearrange("s p b -> p s b").bitcast(I32))
+                load_planes(wt_plane, wt_scales)
             for s in range(PASSES):
-                load_wb(e, s)
-            if e not in a_sb:
-                load_a(e, 1)
+                if (e, s) not in wb_raw:
+                    load_wb(e, s)
+                if (e, s) == (LAST, 0):
+                    load_planes(dy_plane, dy_scales[1:])
+            load_a(e)
             load_wa(e)
-        nc.sync.dma_start(out=wt_codes[:].bitcast(I32), in_=wt_words.rearrange("s p b -> p s b").bitcast(I32))
-        load_planes(dy_plane, dy_scales[1:])
-        load_planes(wt_plane, wt_scales)
 
-        staged = [keep("staged%d" % b, [P, PACK * H], BF16) for b in range(STAGES)]
-        wb_codes = [keep("wb_codes%d" % b, [P, H], U32) for b in range(STAGES)]
-        wb_plane = [keep("wb_plane%d" % b, [P, H], U8) for b in range(STAGES)]
         gate2 = keep("gate2", [P, T], F32)
         sums = [psum.tile([P, PACK, P], F32, name="sums%d" % half) for half in range(HALVES)]
-        spare = [psum.tile([P, BANK], F32, name="spare%d" % half) for half in range(HALVES)]
-        base = [as_row(bank) for bank in sums] + [bank[:] for bank in spare]
-        dx_bank = [psum.tile([P, BANK], F32, name="dx_bank%d" % kt) for kt in range(K_TILES)]
+        dx_bank = [psum.tile([P, BANK], F32, name="dx_bank%d" % b) for b in range(2)]
         pieces = [(kt, slice(h * BANK, (h + 1) * BANK)) for kt in range(K_TILES) for h in range(T // BANK)]
-
-        def stage(e, s):
-            return (PASSES * e + s) % STAGES
+        base = [psum.tile([P, BANK], F32, name="base%d" % piece) for piece in range(len(pieces))]
 
         def spread_gate():
             gate_cols = keep("gate_cols", [P, T // P], F32)
@@ -148,82 +133,73 @@ def tile_moe_adb_relu2_kernel(
                         gate_cols[:, column : column + 1].to_broadcast([P, P]),
                         identity[:],
                     )
-                nc.scalar.copy(out=gate2[:, h * BANK : (h + 1) * BANK], in_=base[1 + h])
+                nc.scalar.copy(out=gate2[:, h * BANK : (h + 1) * BANK], in_=base[1 + h][:])
 
         def gather(into, source):
             for first in range(0, E * C, GATHER):
                 nc.vector.tensor_copy(into[:, first : first + GATHER], source.indirect(list_slice(first, GATHER)))
 
-        def quantize_wb(e, s):
-            rounded, codes, plane = staged[stage(e, s)], wb_codes[stage(e, s)], wb_plane[stage(e, s)]
-            raw = wb_raw[e, s][:].rearrange("p d (c u q) -> p d c u q", u=2, q=RUN)
-            for u in range(2):
-                values = rounded[:, u * 2 * H : (u + 1) * 2 * H]
-                nc.scalar.copy(
-                    out=values.rearrange("p (v c r d) -> p c d r v", v=2, r=2, d=PACK),
-                    in_=raw[:, :, :, u, :].rearrange("p d c (r v) -> p c d r v", v=2),
-                )
-                if s == PASSES - 1:
-                    cols = slice(u * H // 2, (u + 1) * H // 2)
-                    nc.vector.quantize_mx(out=codes[:, cols].bitcast(FP8X4), scales=plane[:, cols], in_=values)
-            if s < PASSES - 1:
-                nc.vector.quantize_mx(out=codes[:].bitcast(FP8X4), scales=plane[:], in_=rounded[:])
+        def quantize(codes, plane, values):
+            nc.vector.quantize_mx(out=codes.bitcast(FP8X4), scales=plane, in_=values)
 
-        def spent(e, s):
-            return as_row(wb_raw[e, s])
+        def accumulate(e, s, codes, plane, tiles):
+            for half in range(HALVES):
+                cols = slice(e * C + half * P, e * C + (half + 1) * P)
+                for t in tiles:
+                    nc.tensor.matmul_mx(
+                        out=sums[half][:, t, :],
+                        lhsT=codes[:, t * P : (t + 1) * P].bitcast(FP8X4),
+                        lhsT_scale=plane[:, t * P : (t + 1) * P],
+                        rhs=slot_words[s][:, cols].bitcast(FP8X4),
+                        rhs_scale=slot_scales[4 * s :, cols],
+                        start=(s == 0 and t == 0),
+                        stop=(s == PASSES - 1 and t == PACK - 1),
+                    )
 
-        def quantized(e, s):
-            return staged[stage(e, s)][:]
-
-        def round_wa_on_gpsimd(e):
-            rounded = quantized(e, 2)[:, PACK * H - PACK * K :]
-            nc.gpsimd.tensor_scalar(
-                out=rounded.rearrange("p (k t) -> p k t", t=PACK),
-                in0=wa_raw[e][:].rearrange("p t k -> p k t"),
-                scalar1=1.0,
-                scalar2=0.0,
-                op0=ALU.mult,
-                op1=ALU.add,
+        def whole_pass(e, s, copy):
+            rounded = turn("rounded", [P, PACK * H], BF16)
+            codes, plane = turn("wb_codes", [P, H], U32), turn("wb_plane", [P, H], U8)
+            copy(
+                out=rounded[:].rearrange("p (u v m d) -> p u m d v", u=2, v=2, d=PACK),
+                in_=wb_raw[e, s][:].rearrange("p d (m u v) -> p u m d v", u=2, v=2),
             )
-            return rounded
+            quantize(codes[:], plane[:], rounded[:])
+            accumulate(e, s, codes, plane, range(PACK))
+
+        def split_pass(e, s, first_copy):
+            codes, plane = turn("wb_codes", [P, H], U32), turn("wb_plane", [P, H], U8)
+            raw = wb_raw[e, s][:].rearrange("p d (m u v) -> p u m d v", u=2, v=2)
+            for u, copy in enumerate((first_copy, nc.scalar.copy)):
+                rounded = turn("rounded_half%d" % u, [P, PACK * H // 2], BF16)
+                copy(out=rounded[:].rearrange("p (v m d) -> p m d v", v=2, d=PACK), in_=raw[:, u])
+                cols = slice(u * H // 2, (u + 1) * H // 2)
+                quantize(codes[:, cols], plane[:, cols], rounded[:])
+                accumulate(e, s, codes, plane, range(2 * u, 2 * u + 2))
+
+        def spent(tile):
+            return tile[:].rearrange("p d i -> p (d i)")
+
+        def empty_and_scatter(e, kt, first, count, through):
+            nc.scalar.copy(out=through[:, :count], in_=dx_bank[e % 2][:, kt * C + first : kt * C + first + count])
+            scatter_on_scalar(kt, e * C + first, through[:, :count])
 
         def round_wa(e):
-            rounded = spent(e, 2)[:, PACK * C : PACK * C + PACK * K // 2].bitcast(BF16)
+            rounded = turn("wa_rounded", [P, PACK * K], BF16)
             nc.scalar.copy(
-                out=rounded.rearrange("p (c r t) -> p c t r", r=RUN, t=PACK),
-                in_=wa_raw[e][:].rearrange("p t (c r) -> p c t r", r=RUN),
+                out=rounded[:].rearrange("p (c r t) -> p c t r", r=2, t=PACK),
+                in_=wa_raw[e][:].rearrange("p t (c r) -> p c t r", r=2),
             )
             return rounded
 
-        def make_factor(e):
-            factor = quantized(e, 1).bitcast(F32).rearrange("p (t j) -> p t j", t=PACK)
+        def make_factor(e, factor, first, count):
             nc.vector.scalar_tensor_tensor(
-                out=factor,
-                in0=a_sb[e],
+                out=factor[:, :, first : first + count],
+                in0=a_sb[e][:, :, first : first + count],
                 scalar=0.0,
-                in1=gate2[:, e * C : (e + 1) * C].unsqueeze(1).to_broadcast([P, PACK, C]),
+                in1=gate2[:, e * C + first : e * C + first + count].unsqueeze(1).to_broadcast([P, PACK, count]),
                 op0=ALU.max,
                 op1=ALU.mult,
             )
-            return factor
-
-        def first_product(e):
-            def one_pass(half, t, s):
-                cols = slice(e * C + half * P, e * C + (half + 1) * P)
-                nc.tensor.matmul_mx(
-                    out=sums[half][:, t, :],
-                    lhsT=wb_codes[stage(e, s)][:, t * P : (t + 1) * P].bitcast(FP8X4),
-                    lhsT_scale=wb_plane[stage(e, s)][:, t * P : (t + 1) * P],
-                    rhs=slot_words[s][:, cols].bitcast(FP8X4),
-                    rhs_scale=slot_scales[4 * s :, cols],
-                    start=(s == 0),
-                    stop=(s == PASSES - 1),
-                )
-
-            for half in range(HALVES):
-                for t in range(PACK):
-                    for s in range(PASSES):
-                        one_pass(half, t, s)
 
         def make_dh(half, factor, dh):
             slots = slice(half * P, (half + 1) * P)
@@ -234,13 +210,11 @@ def tile_moe_adb_relu2_kernel(
                 op=ALU.mult,
             )
 
-        def second_product(dh_slots, dh_codes, dh_plane, wa_codes, wa_plane, banks):
-            nc.vector.quantize_mx(
-                out=dh_codes.bitcast(FP8X4), scales=dh_plane, in_=dh_slots.rearrange("p j t -> p (j t)")
-            )
+        def second_product(bank, wa_codes, wa_plane, dh_codes, dh_plane):
+            width = dh_codes.shape[1]
             for kt in range(K_TILES):
                 nc.tensor.matmul_mx(
-                    out=banks[kt],
+                    out=bank[:, kt * width : (kt + 1) * width],
                     lhsT=wa_codes[:, kt * P : (kt + 1) * P].bitcast(FP8X4),
                     lhsT_scale=wa_plane[:, kt * P : (kt + 1) * P],
                     rhs=dh_codes.bitcast(FP8X4),
@@ -249,76 +223,74 @@ def tile_moe_adb_relu2_kernel(
                     stop=True,
                 )
 
-        def scatter(kt, first, values):
+        def scatter_on_scalar(kt, first, values):
+            nc.scalar.activation(window[kt][:].indirect(list_slice(first, values.shape[1])), values, COPY)
+
+        def scatter_on_vector(kt, first, values):
             nc.vector.tensor_copy(window[kt][:].indirect(list_slice(first, values.shape[1])), values)
 
-        def frozen_layer(piece):
-            kt, cols = pieces[piece]
+        def frozen_layer():
             for s in range(PASSES):
-                nc.tensor.matmul_mx(
-                    out=base[piece],
-                    lhsT=wt_codes[:, s, 2 * kt * P : 2 * (kt + 1) * P].bitcast(FP4X4),
-                    lhsT_scale=wt_plane[:, s, kt * P : (kt + 1) * P],
-                    rhs=dy[s][:, cols].bitcast(FP8X4),
-                    rhs_scale=dy_packed[:, cols] if s == 0 else dy_plane[:, s - 1, cols],
-                    start=(s == 0),
-                    stop=(s == PASSES - 1),
-                )
-
-        def empty_and_scatter(copy, through, e, kt):
-            copy(out=through[:, :C], in_=dx_bank[kt][:, :C])
-            scatter(kt, e * C, through[:, :C])
+                for piece, (kt, cols) in enumerate(pieces):
+                    nc.tensor.matmul_mx(
+                        out=base[piece][:],
+                        lhsT=wt_codes[:, s, 2 * kt * P : 2 * (kt + 1) * P].bitcast(FP4X4),
+                        lhsT_scale=wt_plane[:, s, kt * P : (kt + 1) * P],
+                        rhs=dy[s][:, cols].bitcast(FP8X4),
+                        rhs_scale=dy_packed[:, cols] if s == 0 else dy_plane[:, s - 1, cols],
+                        start=(s == 0),
+                        stop=(s == PASSES - 1),
+                    )
 
         spread_gate()
         for s in range(PASSES):
             gather(slot_words[s][:].bitcast(U32), dy[s][:].bitcast(U32))
-            if s == 0:
-                gather(slot_scales[:], dy_packed[:])
-            quantize_wb(0, s)
             if s == 1:
-                factor = make_factor(0)
+                gather(slot_scales[:], dy_packed[:])
 
-        for e in range(LAST):
-            wa_rounded = round_wa_on_gpsimd(e)
-            dh = ring.tile([P, C, PACK], BF16, name="dh", align_bytes=64)
-            first_product(e)
-            for half in range(HALVES):
-                make_dh(half, factor, dh)
-            wa_codes, wa_plane = wb_codes[stage(e, 2)][:, :K], wb_plane[stage(e, 2)][:, :K]
-            nc.vector.quantize_mx(out=wa_codes.bitcast(FP8X4), scales=wa_plane, in_=wa_rounded)
-            banks = [bank[:, :C] for bank in dx_bank]
-            dh_codes, dh_plane = wb_codes[stage(e + 1, 1)][:, :C], wb_plane[stage(e + 1, 1)][:, :C]
-            second_product(dh[:], dh_codes, dh_plane, wa_codes, wa_plane, banks)
-            quantize_wb(e + 1, 0)
-            empty_and_scatter(nc.vector.tensor_copy, quantized(e + 1, 0).bitcast(F32), e, 0)
-            quantize_wb(e + 1, 1)
-            factor = make_factor(e + 1)
-            quantize_wb(e + 1, 2)
-            empty_and_scatter(nc.scalar.copy, spent(e + 1, 2), e, 1)
+        for e in range(E):
+            if e == 0:
+                whole_pass(e, 0, nc.scalar.copy)
+                whole_pass(e, 1, nc.scalar.copy)
+                split_pass(e, 2, nc.scalar.copy)
+                wa_rounded = round_wa(e)
+            else:
+                split_pass(e, 0, nc.vector.tensor_copy)
+                empty_and_scatter(e - 1, 0, 0, C, spent(wb_raw[e, 0]))
+                whole_pass(e, 1, nc.vector.tensor_copy)
+                split_pass(e, 2, nc.vector.tensor_copy)
+                empty_and_scatter(e - 1, 1, 0, P, spent(wb_raw[e, 2]))
+                wa_rounded = round_wa(e)
+                empty_and_scatter(e - 1, 1, P, P, spent(wa_raw[e]))
+            factor = turn("factor", [P, PACK, C], F32)
+            dh = turn("dh", [P, C, PACK], BF16)
+            wa_codes, wa_plane = turn("wa_codes", [P, K], U32), turn("wa_plane", [P, K], U8)
+            dh_codes, dh_plane = turn("dh_codes", [P, C], U32), turn("dh_plane", [P, C], U8)
+            if e < LAST:
+                make_factor(e, factor, 0, C)
+                for half in range(HALVES):
+                    make_dh(half, factor, dh)
+                quantize(wa_codes[:], wa_plane[:], wa_rounded[:])
+                quantize(dh_codes[:], dh_plane[:], dh[:].rearrange("p j t -> p (j t)"))
+                second_product(dx_bank[e % 2], wa_codes, wa_plane, dh_codes[:], dh_plane[:])
+            else:
+                for half in range(HALVES):
+                    slots = slice(half * P, (half + 1) * P)
+                    make_factor(e, factor, half * P, P)
+                    make_dh(half, factor, dh)
+                    if half == 0:
+                        quantize(wa_codes[:], wa_plane[:], wa_rounded[:])
+                    quantize(dh_codes[:, slots], dh_plane[:, slots], dh[:, slots, :].rearrange("p j t -> p (j t)"))
+                    bank = dx_bank[(e + half) % 2]
+                    second_product(bank, wa_codes, wa_plane, dh_codes[:, slots], dh_plane[:, slots])
+                    dx = keep("dx_half%d" % half, [P, K_TILES * P], F32)
+                    nc.scalar.copy(out=dx[:], in_=bank[:, : K_TILES * P])
+                    scatter_on_vector(0, e * C + half * P, dx[:, :P])
+                    scatter_on_scalar(1, e * C + half * P, dx[:, P:])
 
-        wa_rounded = round_wa(LAST)
-        first_product(LAST)
-        dh = ring.tile([P, C, PACK], BF16, name="dh", align_bytes=64)
-        dx = keep("dx", [P, K_TILES, C], F32)
-        wa_codes, wa_plane = keep("wa_codes", [P, K], U32)[:], keep("wa_plane", [P, K], U8)[:]
-        dh_codes, dh_plane = keep("dh_codes", [P, C], U32), keep("dh_plane", [P, C], U8)
-        for half in range(HALVES):
-            slots = slice(half * P, (half + 1) * P)
-            make_dh(half, factor, dh)
-            if half == 0:
-                nc.vector.quantize_mx(out=wa_codes.bitcast(FP8X4), scales=wa_plane, in_=wa_rounded)
-            banks = [spare[half][:, kt * P : (kt + 1) * P] for kt in range(K_TILES)]
-            second_product(dh[:, slots, :], dh_codes[:, slots], dh_plane[:, slots], wa_codes, wa_plane, banks)
-            both = spare[half][:, : K_TILES * P].rearrange("p (kt j) -> p kt j", kt=K_TILES)
-            nc.scalar.copy(out=dx[:, :, slots], in_=both)
-
-        for piece in range(len(pieces)):
-            frozen_layer(piece)
-        for half in range(HALVES):
-            for kt in range(K_TILES):
-                scatter(kt, LAST * C + half * P, dx[:, kt, half * P : (half + 1) * P])
+        frozen_layer()
         for piece, (kt, cols) in enumerate(pieces):
-            width = BANK if piece < len(pieces) - 1 else BANK // 2
+            width = BANK // 2 if piece == 0 else BANK
             for first in range(0, BANK, width):
                 tokens = slice(cols.start + first, cols.start + first + width)
                 sums_here = base[piece][:, first : first + width]

@@ -104,16 +104,14 @@ def tile_moe_adb_relu2_kernel(
             )
         load_dy(2)
         for e in range(E):
-            if e == LAST:
-                nc.sync.dma_start(out=wt_codes[:].bitcast(I32), in_=wt_words.rearrange("s p b -> p s b").bitcast(I32))
-                load_planes(wt_plane, wt_scales)
             for s in range(PASSES):
                 if (e, s) not in wb_raw:
                     load_wb(e, s)
-                if (e, s) == (LAST, 0):
-                    load_planes(dy_plane, dy_scales[1:])
             load_a(e)
             load_wa(e)
+        nc.sync.dma_start(out=wt_codes[:].bitcast(I32), in_=wt_words.rearrange("s p b -> p s b").bitcast(I32))
+        load_planes(wt_plane, wt_scales)
+        load_planes(dy_plane, dy_scales[1:])
 
         gate2 = keep("gate2", [P, T], F32)
         sums = [psum.tile([P, PACK, P], F32, name="sums%d" % half) for half in range(HALVES)]
@@ -179,15 +177,28 @@ def tile_moe_adb_relu2_kernel(
         def spent(tile):
             return tile[:].rearrange("p d i -> p (d i)")
 
-        def empty_and_scatter(e, kt, first, count, through):
-            nc.scalar.copy(out=through[:, :count], in_=dx_bank[e % 2][:, kt * C + first : kt * C + first + count])
-            scatter_on_scalar(kt, e * C + first, through[:, :count])
+        def empty_and_scatter(e, through):
+            nc.scalar.copy(out=through[:, : K_TILES * C], in_=dx_bank[e % 2][:])
+            for kt in range(K_TILES):
+                scatter_on_scalar(kt, e * C, through[:, kt * C : (kt + 1) * C])
 
         def round_wa(e):
             rounded = turn("wa_rounded", [P, PACK * K], BF16)
             nc.scalar.copy(
                 out=rounded[:].rearrange("p (c r t) -> p c t r", r=2, t=PACK),
                 in_=wa_raw[e][:].rearrange("p t (c r) -> p c t r", r=2),
+            )
+            return rounded
+
+        def round_wa_on_gpsimd(e):
+            rounded = spent(a_sb[e])[:, : PACK * K // 2].bitcast(BF16)
+            nc.gpsimd.tensor_scalar(
+                out=rounded.rearrange("p (k t) -> p k t", t=PACK),
+                in0=wa_raw[e][:].rearrange("p t k -> p k t"),
+                scalar1=1.0,
+                scalar2=0.0,
+                op0=ALU.mult,
+                op1=ALU.add,
             )
             return rounded
 
@@ -210,11 +221,10 @@ def tile_moe_adb_relu2_kernel(
                 op=ALU.mult,
             )
 
-        def second_product(bank, wa_codes, wa_plane, dh_codes, dh_plane):
-            width = dh_codes.shape[1]
+        def second_product(banks, wa_codes, wa_plane, dh_codes, dh_plane):
             for kt in range(K_TILES):
                 nc.tensor.matmul_mx(
-                    out=bank[:, kt * width : (kt + 1) * width],
+                    out=banks[kt],
                     lhsT=wa_codes[:, kt * P : (kt + 1) * P].bitcast(FP8X4),
                     lhsT_scale=wa_plane[:, kt * P : (kt + 1) * P],
                     rhs=dh_codes.bitcast(FP8X4),
@@ -230,8 +240,8 @@ def tile_moe_adb_relu2_kernel(
             nc.vector.tensor_copy(window[kt][:].indirect(list_slice(first, values.shape[1])), values)
 
         def frozen_layer():
-            for s in range(PASSES):
-                for piece, (kt, cols) in enumerate(pieces):
+            for piece, (kt, cols) in enumerate(pieces):
+                for s in range(PASSES):
                     nc.tensor.matmul_mx(
                         out=base[piece][:],
                         lhsT=wt_codes[:, s, 2 * kt * P : 2 * (kt + 1) * P].bitcast(FP4X4),
@@ -253,44 +263,51 @@ def tile_moe_adb_relu2_kernel(
                 whole_pass(e, 0, nc.scalar.copy)
                 whole_pass(e, 1, nc.scalar.copy)
                 split_pass(e, 2, nc.scalar.copy)
-                wa_rounded = round_wa(e)
+                wa_rounded = round_wa(e)[:]
+            elif e == 1:
+                whole_pass(e, 0, nc.scalar.copy)
+                split_pass(e, 1, nc.vector.tensor_copy)
+                split_pass(e, 2, nc.vector.tensor_copy)
+                empty_and_scatter(e - 1, spent(wb_raw[e, 2]))
+            elif e < LAST:
+                whole_pass(e, 0, nc.vector.tensor_copy)
+                split_pass(e, 1, nc.vector.tensor_copy)
+                split_pass(e, 2, nc.vector.tensor_copy)
+                empty_and_scatter(e - 1, spent(wb_raw[e, 2]))
             else:
-                split_pass(e, 0, nc.vector.tensor_copy)
-                empty_and_scatter(e - 1, 0, 0, C, spent(wb_raw[e, 0]))
+                empty_and_scatter(e - 1, keep("dx", [P, K_TILES * C], F32)[:])
+                whole_pass(e, 0, nc.vector.tensor_copy)
                 whole_pass(e, 1, nc.vector.tensor_copy)
                 split_pass(e, 2, nc.vector.tensor_copy)
-                empty_and_scatter(e - 1, 1, 0, P, spent(wb_raw[e, 2]))
-                wa_rounded = round_wa(e)
-                empty_and_scatter(e - 1, 1, P, P, spent(wa_raw[e]))
+                wa_rounded = round_wa(e)[:]
             factor = turn("factor", [P, PACK, C], F32)
             dh = turn("dh", [P, C, PACK], BF16)
             wa_codes, wa_plane = turn("wa_codes", [P, K], U32), turn("wa_plane", [P, K], U8)
             dh_codes, dh_plane = turn("dh_codes", [P, C], U32), turn("dh_plane", [P, C], U8)
+            for half in range(HALVES):
+                make_factor(e, factor, half * P, P)
+            if 0 < e < LAST:
+                wa_rounded = round_wa_on_gpsimd(e)
+            for half in range(HALVES):
+                make_dh(half, factor, dh)
+            if e in (0, LAST):
+                quantize(wa_codes[:], wa_plane[:], wa_rounded)
+            quantize(dh_codes[:], dh_plane[:], dh[:].rearrange("p j t -> p (j t)"))
+            if 0 < e < LAST:
+                quantize(wa_codes[:], wa_plane[:], wa_rounded)
             if e < LAST:
-                make_factor(e, factor, 0, C)
-                for half in range(HALVES):
-                    make_dh(half, factor, dh)
-                quantize(wa_codes[:], wa_plane[:], wa_rounded[:])
-                quantize(dh_codes[:], dh_plane[:], dh[:].rearrange("p j t -> p (j t)"))
-                second_product(dx_bank[e % 2], wa_codes, wa_plane, dh_codes[:], dh_plane[:])
+                banks = [dx_bank[e % 2][:, kt * C : (kt + 1) * C] for kt in range(K_TILES)]
             else:
-                for half in range(HALVES):
-                    slots = slice(half * P, (half + 1) * P)
-                    make_factor(e, factor, half * P, P)
-                    make_dh(half, factor, dh)
-                    if half == 0:
-                        quantize(wa_codes[:], wa_plane[:], wa_rounded[:])
-                    quantize(dh_codes[:, slots], dh_plane[:, slots], dh[:, slots, :].rearrange("p j t -> p (j t)"))
-                    bank = dx_bank[(e + half) % 2]
-                    second_product(bank, wa_codes, wa_plane, dh_codes[:, slots], dh_plane[:, slots])
-                    dx = keep("dx_half%d" % half, [P, K_TILES * P], F32)
-                    nc.scalar.copy(out=dx[:], in_=bank[:, : K_TILES * P])
-                    scatter_on_vector(0, e * C + half * P, dx[:, :P])
-                    scatter_on_scalar(1, e * C + half * P, dx[:, P:])
+                banks = [dx_bank[(e + kt) % 2][:, :C] for kt in range(K_TILES)]
+            second_product(banks, wa_codes, wa_plane, dh_codes[:], dh_plane[:])
+        for kt, scatter in enumerate((scatter_on_vector, scatter_on_scalar)):
+            dx = keep("dx_last%d" % kt, [P, C], F32)
+            nc.scalar.copy(out=dx[:], in_=banks[kt])
+            scatter(kt, LAST * C, dx[:])
 
         frozen_layer()
         for piece, (kt, cols) in enumerate(pieces):
-            width = BANK // 2 if piece == 0 else BANK
+            width = BANK // 2 if piece in (0, len(pieces) - 1) else BANK
             for first in range(0, BANK, width):
                 tokens = slice(cols.start + first, cols.start + first + width)
                 sums_here = base[piece][:, first : first + width]

@@ -107,8 +107,11 @@ def tile_moe_adb_relu2_kernel(
             for s in range(PASSES):
                 if (e, s) not in wb_raw:
                     load_wb(e, s)
+                if s == 0 and 0 < e < LAST:
+                    load_wa(e)
             load_a(e)
-            load_wa(e)
+            if not (0 < e < LAST):
+                load_wa(e)
         nc.sync.dma_start(out=wt_codes[:].bitcast(I32), in_=wt_words.rearrange("s p b -> p s b").bitcast(I32))
         load_planes(wt_plane, wt_scales)
         load_planes(dy_plane, dy_scales[1:])
@@ -164,41 +167,29 @@ def tile_moe_adb_relu2_kernel(
             quantize(codes[:], plane[:], rounded[:])
             accumulate(e, s, codes, plane, range(PACK))
 
-        def split_pass(e, s, first_copy):
+        def split_pass(e, s, first_copy, second_copy=nc.scalar.copy):
             codes, plane = turn("wb_codes", [P, H], U32), turn("wb_plane", [P, H], U8)
             raw = wb_raw[e, s][:].rearrange("p d (m u v) -> p u m d v", u=2, v=2)
-            for u, copy in enumerate((first_copy, nc.scalar.copy)):
-                rounded = turn("rounded_half%d" % u, [P, PACK * H // 2], BF16)
-                copy(out=rounded[:].rearrange("p (v m d) -> p m d v", v=2, d=PACK), in_=raw[:, u])
+            rounded = [turn("rounded_half%d" % u, [P, PACK * H // 2], BF16) for u in range(2)]
+            for u, copy in enumerate((first_copy, second_copy)):
+                copy(out=rounded[u][:].rearrange("p (v m d) -> p m d v", v=2, d=PACK), in_=raw[:, u])
+            for u in range(2):
                 cols = slice(u * H // 2, (u + 1) * H // 2)
-                quantize(codes[:, cols], plane[:, cols], rounded[:])
+                quantize(codes[:, cols], plane[:, cols], rounded[u][:])
                 accumulate(e, s, codes, plane, range(2 * u, 2 * u + 2))
 
         def spent(tile):
             return tile[:].rearrange("p d i -> p (d i)")
 
-        def empty_and_scatter(e, through):
-            nc.scalar.copy(out=through[:, : K_TILES * C], in_=dx_bank[e % 2][:])
-            for kt in range(K_TILES):
-                scatter_on_scalar(kt, e * C, through[:, kt * C : (kt + 1) * C])
+        def empty_and_scatter(e, kt, first, count, through):
+            nc.scalar.copy(out=through[:, :count], in_=dx_bank[e % 2][:, kt * C + first : kt * C + first + count])
+            scatter_on_scalar(kt, e * C + first, through[:, :count])
 
         def round_wa(e):
             rounded = turn("wa_rounded", [P, PACK * K], BF16)
             nc.scalar.copy(
                 out=rounded[:].rearrange("p (c r t) -> p c t r", r=2, t=PACK),
                 in_=wa_raw[e][:].rearrange("p t (c r) -> p c t r", r=2),
-            )
-            return rounded
-
-        def round_wa_on_gpsimd(e):
-            rounded = spent(a_sb[e])[:, : PACK * K // 2].bitcast(BF16)
-            nc.gpsimd.tensor_scalar(
-                out=rounded.rearrange("p (k t) -> p k t", t=PACK),
-                in0=wa_raw[e][:].rearrange("p t k -> p k t"),
-                scalar1=1.0,
-                scalar2=0.0,
-                op0=ALU.mult,
-                op1=ALU.add,
             )
             return rounded
 
@@ -262,52 +253,49 @@ def tile_moe_adb_relu2_kernel(
             if e == 0:
                 whole_pass(e, 0, nc.scalar.copy)
                 whole_pass(e, 1, nc.scalar.copy)
-                split_pass(e, 2, nc.scalar.copy)
-                wa_rounded = round_wa(e)[:]
-            elif e == 1:
-                whole_pass(e, 0, nc.scalar.copy)
-                split_pass(e, 1, nc.vector.tensor_copy)
                 split_pass(e, 2, nc.vector.tensor_copy)
-                empty_and_scatter(e - 1, spent(wb_raw[e, 2]))
+                wa_rounded = round_wa(e)[:]
             elif e < LAST:
-                whole_pass(e, 0, nc.vector.tensor_copy)
-                split_pass(e, 1, nc.vector.tensor_copy)
+                split_pass(e, 0, nc.vector.tensor_copy)
+                wa_rounded = round_wa(e)[:]
+                empty_and_scatter(e - 1, 0, 0, C, spent(wa_raw[e]))
+                split_pass(e, 1, nc.vector.tensor_copy, nc.vector.tensor_copy)
                 split_pass(e, 2, nc.vector.tensor_copy)
-                empty_and_scatter(e - 1, spent(wb_raw[e, 2]))
+                empty_and_scatter(e - 1, 1, 0, C, spent(wb_raw[e, 2]))
             else:
-                empty_and_scatter(e - 1, keep("dx", [P, K_TILES * C], F32)[:])
-                whole_pass(e, 0, nc.vector.tensor_copy)
-                whole_pass(e, 1, nc.vector.tensor_copy)
+                split_pass(e, 0, nc.vector.tensor_copy)
+                empty_and_scatter(e - 1, 0, 0, C, spent(wb_raw[e, 0]))
+                split_pass(e, 1, nc.vector.tensor_copy, nc.vector.tensor_copy)
                 split_pass(e, 2, nc.vector.tensor_copy)
                 wa_rounded = round_wa(e)[:]
+                empty_and_scatter(e - 1, 1, 0, C, spent(wa_raw[e]))
             factor = turn("factor", [P, PACK, C], F32)
             dh = turn("dh", [P, C, PACK], BF16)
             wa_codes, wa_plane = turn("wa_codes", [P, K], U32), turn("wa_plane", [P, K], U8)
             dh_codes, dh_plane = turn("dh_codes", [P, C], U32), turn("dh_plane", [P, C], U8)
             for half in range(HALVES):
                 make_factor(e, factor, half * P, P)
-            if 0 < e < LAST:
-                wa_rounded = round_wa_on_gpsimd(e)
             for half in range(HALVES):
                 make_dh(half, factor, dh)
-            if e in (0, LAST):
-                quantize(wa_codes[:], wa_plane[:], wa_rounded)
-            quantize(dh_codes[:], dh_plane[:], dh[:].rearrange("p j t -> p (j t)"))
-            if 0 < e < LAST:
-                quantize(wa_codes[:], wa_plane[:], wa_rounded)
+            for half in range(HALVES):
+                slots = slice(half * P, (half + 1) * P)
+                quantize(dh_codes[:, slots], dh_plane[:, slots], dh[:, slots, :].rearrange("p j t -> p (j t)"))
+                if half == 0:
+                    quantize(wa_codes[:], wa_plane[:], wa_rounded)
             if e < LAST:
                 banks = [dx_bank[e % 2][:, kt * C : (kt + 1) * C] for kt in range(K_TILES)]
             else:
                 banks = [dx_bank[(e + kt) % 2][:, :C] for kt in range(K_TILES)]
             second_product(banks, wa_codes, wa_plane, dh_codes[:], dh_plane[:])
-        for kt, scatter in enumerate((scatter_on_vector, scatter_on_scalar)):
+        last_steps = ((nc.vector.tensor_copy, scatter_on_vector), (nc.scalar.copy, scatter_on_scalar))
+        for kt, (copy, scatter) in enumerate(last_steps):
             dx = keep("dx_last%d" % kt, [P, C], F32)
-            nc.scalar.copy(out=dx[:], in_=banks[kt])
+            copy(out=dx[:], in_=banks[kt])
             scatter(kt, LAST * C, dx[:])
 
         frozen_layer()
         for piece, (kt, cols) in enumerate(pieces):
-            width = BANK // 2 if piece in (0, len(pieces) - 1) else BANK
+            width = BANK // 2 if piece == 0 else BANK
             for first in range(0, BANK, width):
                 tokens = slice(cols.start + first, cols.start + first + width)
                 sums_here = base[piece][:, first : first + width]

@@ -28,6 +28,8 @@ HALVES = C // P
 QUADS = P // 32
 GATHER = T // 2
 LAST = E - 1
+FIRST_SHARE = 40
+LAST_SHARE = 88
 
 
 def tile_moe_adb_relu2_kernel(
@@ -112,9 +114,9 @@ def tile_moe_adb_relu2_kernel(
             load_a(e)
             if not (0 < e < LAST):
                 load_wa(e)
-        nc.sync.dma_start(out=wt_codes[:].bitcast(I32), in_=wt_words.rearrange("s p b -> p s b").bitcast(I32))
-        load_planes(wt_plane, wt_scales)
         load_planes(dy_plane, dy_scales[1:])
+        load_planes(wt_plane, wt_scales)
+        nc.sync.dma_start(out=wt_codes[:].bitcast(I32), in_=wt_words.rearrange("s p b -> p s b").bitcast(I32))
 
         gate2 = keep("gate2", [P, T], F32)
         sums = [psum.tile([P, PACK, P], F32, name="sums%d" % half) for half in range(HALVES)]
@@ -157,26 +159,17 @@ def tile_moe_adb_relu2_kernel(
                         stop=(s == PASSES - 1 and t == PACK - 1),
                     )
 
-        def whole_pass(e, s, copy):
+        def round_and_accumulate(e, s, on_vector):
             rounded = turn("rounded", [P, PACK * H], BF16)
             codes, plane = turn("wb_codes", [P, H], U32), turn("wb_plane", [P, H], U8)
-            copy(
-                out=rounded[:].rearrange("p (u v m d) -> p u m d v", u=2, v=2, d=PACK),
-                in_=wb_raw[e, s][:].rearrange("p d (m u v) -> p u m d v", u=2, v=2),
-            )
+            words = rounded[:].rearrange("p (t m d) -> p m d t", t=PACK, d=PACK)
+            raw = wb_raw[e, s][:].rearrange("p d (m t) -> p m d t", t=PACK)
+            if on_vector > 0:
+                nc.vector.tensor_copy(out=words[:, :on_vector], in_=raw[:, :on_vector])
+            if on_vector < P:
+                nc.scalar.copy(out=words[:, on_vector:], in_=raw[:, on_vector:])
             quantize(codes[:], plane[:], rounded[:])
             accumulate(e, s, codes, plane, range(PACK))
-
-        def split_pass(e, s, first_copy, second_copy=nc.scalar.copy):
-            codes, plane = turn("wb_codes", [P, H], U32), turn("wb_plane", [P, H], U8)
-            raw = wb_raw[e, s][:].rearrange("p d (m u v) -> p u m d v", u=2, v=2)
-            rounded = [turn("rounded_half%d" % u, [P, PACK * H // 2], BF16) for u in range(2)]
-            for u, copy in enumerate((first_copy, second_copy)):
-                copy(out=rounded[u][:].rearrange("p (v m d) -> p m d v", v=2, d=PACK), in_=raw[:, u])
-            for u in range(2):
-                cols = slice(u * H // 2, (u + 1) * H // 2)
-                quantize(codes[:, cols], plane[:, cols], rounded[u][:])
-                accumulate(e, s, codes, plane, range(2 * u, 2 * u + 2))
 
         def spent(tile):
             return tile[:].rearrange("p d i -> p (d i)")
@@ -188,8 +181,8 @@ def tile_moe_adb_relu2_kernel(
         def round_wa(e):
             rounded = turn("wa_rounded", [P, PACK * K], BF16)
             nc.scalar.copy(
-                out=rounded[:].rearrange("p (c r t) -> p c t r", r=2, t=PACK),
-                in_=wa_raw[e][:].rearrange("p t (c r) -> p c t r", r=2),
+                out=rounded[:].rearrange("p (c r t) -> p c t r", r=4, t=PACK),
+                in_=wa_raw[e][:].rearrange("p t (c r) -> p c t r", r=4),
             )
             return rounded
 
@@ -251,22 +244,22 @@ def tile_moe_adb_relu2_kernel(
 
         for e in range(E):
             if e == 0:
-                whole_pass(e, 0, nc.scalar.copy)
-                whole_pass(e, 1, nc.scalar.copy)
-                split_pass(e, 2, nc.vector.tensor_copy)
+                round_and_accumulate(e, 0, 0)
+                round_and_accumulate(e, 1, 0)
+                round_and_accumulate(e, 2, LAST_SHARE)
                 wa_rounded = round_wa(e)[:]
             elif e < LAST:
-                split_pass(e, 0, nc.vector.tensor_copy)
+                round_and_accumulate(e, 0, FIRST_SHARE)
                 wa_rounded = round_wa(e)[:]
                 empty_and_scatter(e - 1, 0, 0, C, spent(wa_raw[e]))
-                split_pass(e, 1, nc.vector.tensor_copy, nc.vector.tensor_copy)
-                split_pass(e, 2, nc.vector.tensor_copy)
+                round_and_accumulate(e, 1, P)
+                round_and_accumulate(e, 2, LAST_SHARE)
                 empty_and_scatter(e - 1, 1, 0, C, spent(wb_raw[e, 2]))
             else:
-                split_pass(e, 0, nc.vector.tensor_copy)
+                round_and_accumulate(e, 0, FIRST_SHARE)
                 empty_and_scatter(e - 1, 0, 0, C, spent(wb_raw[e, 0]))
-                split_pass(e, 1, nc.vector.tensor_copy, nc.vector.tensor_copy)
-                split_pass(e, 2, nc.vector.tensor_copy)
+                round_and_accumulate(e, 1, P)
+                round_and_accumulate(e, 2, LAST_SHARE)
                 wa_rounded = round_wa(e)[:]
                 empty_and_scatter(e - 1, 1, 0, C, spent(wa_raw[e]))
             factor = turn("factor", [P, PACK, C], F32)

@@ -29,7 +29,7 @@ QUADS = P // 32
 GATHER = T // 2
 LAST = E - 1
 FIRST_SHARE = 40
-LAST_SHARE = 88
+LAST_SHARE = 84
 
 
 def tile_moe_adb_relu2_kernel(
@@ -111,12 +111,13 @@ def tile_moe_adb_relu2_kernel(
                     load_wb(e, s)
                 if s == 0 and 0 < e < LAST:
                     load_wa(e)
+                if (e, s) == (LAST, 0):
+                    load_planes(wt_plane, wt_scales)
             load_a(e)
             if not (0 < e < LAST):
                 load_wa(e)
-        load_planes(dy_plane, dy_scales[1:])
-        load_planes(wt_plane, wt_scales)
         nc.sync.dma_start(out=wt_codes[:].bitcast(I32), in_=wt_words.rearrange("s p b -> p s b").bitcast(I32))
+        load_planes(dy_plane, dy_scales[1:])
 
         gate2 = keep("gate2", [P, T], F32)
         sums = [psum.tile([P, PACK, P], F32, name="sums%d" % half) for half in range(HALVES)]
@@ -185,6 +186,14 @@ def tile_moe_adb_relu2_kernel(
                 in_=wa_raw[e][:].rearrange("p t (c r) -> p c t r", r=4),
             )
             return rounded
+
+        def round_wa_tile(e, kt):
+            rounded = keep("wa_rounded%d" % kt, [P, PACK * P], BF16)
+            nc.scalar.copy(
+                out=rounded[:].rearrange("p (c r t) -> p c t r", r=4, t=PACK),
+                in_=wa_raw[e][:, :, kt * P : (kt + 1) * P].rearrange("p t (c r) -> p c t r", r=4),
+            )
+            return rounded[:]
 
         def make_factor(e, factor, first, count):
             nc.vector.scalar_tensor_tensor(
@@ -260,7 +269,7 @@ def tile_moe_adb_relu2_kernel(
                 empty_and_scatter(e - 1, 0, 0, C, spent(wb_raw[e, 0]))
                 round_and_accumulate(e, 1, P)
                 round_and_accumulate(e, 2, LAST_SHARE)
-                wa_rounded = round_wa(e)[:]
+                wa_tiles = [round_wa_tile(e, kt) for kt in range(K_TILES)]
                 empty_and_scatter(e - 1, 1, 0, C, spent(wa_raw[e]))
             factor = turn("factor", [P, PACK, C], F32)
             dh = turn("dh", [P, C, PACK], BF16)
@@ -273,7 +282,9 @@ def tile_moe_adb_relu2_kernel(
             for half in range(HALVES):
                 slots = slice(half * P, (half + 1) * P)
                 quantize(dh_codes[:, slots], dh_plane[:, slots], dh[:, slots, :].rearrange("p j t -> p (j t)"))
-                if half == 0:
+                if e == LAST:
+                    quantize(wa_codes[:, slots], wa_plane[:, slots], wa_tiles[half])
+                elif half == 0:
                     quantize(wa_codes[:], wa_plane[:], wa_rounded)
             if e < LAST:
                 banks = [dx_bank[e % 2][:, kt * C : (kt + 1) * C] for kt in range(K_TILES)]

@@ -28,8 +28,9 @@ HALVES = C // P
 QUADS = P // 32
 GATHER = T // 2
 LAST = E - 1
-FIRST_SHARE = 40
+FIRST_SHARE = 48
 LAST_SHARE = 84
+FINAL_SHARE = 84
 
 
 def tile_moe_adb_relu2_kernel(
@@ -96,30 +97,26 @@ def tile_moe_adb_relu2_kernel(
 
         nc.sync.dma_start(offsets[:], offs)
         load_dy(0)
-        nc.sync.dma_start(out=gate_rows[: T // P, :], in_=gate[0, :].rearrange("(m p) -> m p", p=P))
         load_dy(1)
         load_wb(0, 0)
+        load_dy(2)
+        nc.sync.dma_start(out=gate_rows[: T // P, :], in_=gate[0, :].rearrange("(m p) -> m p", p=P))
         for quad in range(QUADS):
             nc.sync.dma_start(
                 out=dy_packed[32 * quad : 32 * quad + 4 * PASSES, :].bitcast(I32),
                 in_=dy_scales[:, 4 * quad : 4 * quad + 4, :].bitcast(I32),
             )
-        load_dy(2)
         for e in range(E):
             for s in range(PASSES):
                 if (e, s) not in wb_raw:
                     load_wb(e, s)
-                if s == 0 and 0 < e < LAST:
-                    load_wa(e)
                 if (e, s) == (LAST, 0):
                     load_planes(wt_plane, wt_scales)
             load_a(e)
-            if not (0 < e < LAST):
-                load_wa(e)
+            load_wa(e)
         nc.sync.dma_start(out=wt_codes[:].bitcast(I32), in_=wt_words.rearrange("s p b -> p s b").bitcast(I32))
         load_planes(dy_plane, dy_scales[1:])
 
-        gate2 = keep("gate2", [P, T], F32)
         sums = [psum.tile([P, PACK, P], F32, name="sums%d" % half) for half in range(HALVES)]
         dx_bank = [psum.tile([P, BANK], F32, name="dx_bank%d" % b) for b in range(2)]
         pieces = [(kt, slice(h * BANK, (h + 1) * BANK)) for kt in range(K_TILES) for h in range(T // BANK)]
@@ -133,11 +130,10 @@ def tile_moe_adb_relu2_kernel(
                 for m in range(BANK // P):
                     column = h * (BANK // P) + m
                     nc.tensor.transpose(
-                        base[1 + h][:, m * P : (m + 1) * P],
+                        base[2 + h][:, m * P : (m + 1) * P],
                         gate_cols[:, column : column + 1].to_broadcast([P, P]),
                         identity[:],
                     )
-                nc.scalar.copy(out=gate2[:, h * BANK : (h + 1) * BANK], in_=base[1 + h][:])
 
         def gather(into, source):
             for first in range(0, E * C, GATHER):
@@ -171,6 +167,7 @@ def tile_moe_adb_relu2_kernel(
                 nc.scalar.copy(out=words[:, on_vector:], in_=raw[:, on_vector:])
             quantize(codes[:], plane[:], rounded[:])
             accumulate(e, s, codes, plane, range(PACK))
+            return rounded
 
         def spent(tile):
             return tile[:].rearrange("p d i -> p (d i)")
@@ -195,36 +192,51 @@ def tile_moe_adb_relu2_kernel(
             )
             return rounded[:]
 
+        def round_wa_on_gpsimd(e, quantized):
+            rounded = quantized[:, : PACK * K]
+            nc.gpsimd.tensor_scalar(
+                out=rounded.rearrange("p (k t) -> p k t", t=PACK),
+                in0=wa_raw[e][:].rearrange("p t k -> p k t"),
+                scalar1=1.0,
+                scalar2=0.0,
+                op0=ALU.mult,
+                op1=ALU.add,
+            )
+            return rounded
+
         def make_factor(e, factor, first, count):
             nc.vector.scalar_tensor_tensor(
                 out=factor[:, :, first : first + count],
                 in0=a_sb[e][:, :, first : first + count],
                 scalar=0.0,
-                in1=gate2[:, e * C + first : e * C + first + count].unsqueeze(1).to_broadcast([P, PACK, count]),
+                in1=base[2 + e // 2][:, e % 2 * C + first : e % 2 * C + first + count].unsqueeze(1).to_broadcast([P, PACK, count]),
                 op0=ALU.max,
                 op1=ALU.mult,
             )
 
-        def make_dh(half, factor, dh):
+        def make_dh(half, factor, values):
             slots = slice(half * P, (half + 1) * P)
             nc.vector.tensor_tensor(
-                out=dh[:, slots, :].rearrange("p (c r) t -> p c t r", r=2),
+                out=values.rearrange("p (c r t) -> p c t r", r=2, t=PACK),
                 in0=sums[half][:].rearrange("p t (c r) -> p c t r", r=2),
                 in1=factor[:, :, slots].rearrange("p t (c r) -> p c t r", r=2),
                 op=ALU.mult,
             )
 
-        def second_product(banks, wa_codes, wa_plane, dh_codes, dh_plane):
-            for kt in range(K_TILES):
-                nc.tensor.matmul_mx(
-                    out=banks[kt],
-                    lhsT=wa_codes[:, kt * P : (kt + 1) * P].bitcast(FP8X4),
-                    lhsT_scale=wa_plane[:, kt * P : (kt + 1) * P],
-                    rhs=dh_codes.bitcast(FP8X4),
-                    rhs_scale=dh_plane,
-                    start=True,
-                    stop=True,
-                )
+        def quantize_dh(half, values, dh_codes, dh_plane):
+            slots = slice(half * P, (half + 1) * P)
+            quantize(dh_codes[:, slots], dh_plane[:, slots], values)
+
+        def second_product(bank, wa_codes, wa_plane, dh_codes, dh_plane):
+            nc.tensor.matmul_mx(
+                out=bank,
+                lhsT=wa_codes.bitcast(FP8X4),
+                lhsT_scale=wa_plane,
+                rhs=dh_codes.bitcast(FP8X4),
+                rhs_scale=dh_plane,
+                start=True,
+                stop=True,
+            )
 
         def scatter_on_scalar(kt, first, values):
             nc.scalar.activation(window[kt][:].indirect(list_slice(first, values.shape[1])), values, COPY)
@@ -248,54 +260,69 @@ def tile_moe_adb_relu2_kernel(
         spread_gate()
         for s in range(PASSES):
             gather(slot_words[s][:].bitcast(U32), dy[s][:].bitcast(U32))
-            if s == 1:
-                gather(slot_scales[:], dy_packed[:])
+        gather(slot_scales[:], dy_packed[:])
 
         for e in range(E):
             if e == 0:
                 round_and_accumulate(e, 0, 0)
                 round_and_accumulate(e, 1, 0)
-                round_and_accumulate(e, 2, LAST_SHARE)
-                wa_rounded = round_wa(e)[:]
+                wa_rounded = round_wa_on_gpsimd(e, round_and_accumulate(e, 2, 64))
             elif e < LAST:
-                round_and_accumulate(e, 0, FIRST_SHARE)
-                wa_rounded = round_wa(e)[:]
-                empty_and_scatter(e - 1, 0, 0, C, spent(wa_raw[e]))
-                round_and_accumulate(e, 1, P)
-                round_and_accumulate(e, 2, LAST_SHARE)
-                empty_and_scatter(e - 1, 1, 0, C, spent(wb_raw[e, 2]))
+                round_and_accumulate(e, 0, 32)
+                empty_and_scatter(e - 1, 0, 0, C, wb_raw[e, 0][:, 0, H - C :])
+                round_and_accumulate(e, 1, 128)
+                wa_rounded = round_wa_on_gpsimd(e, round_and_accumulate(e, 2, 64))
+                empty_and_scatter(e - 1, 1, 0, C, wb_raw[e, 2][:, 0, H - C :])
             else:
-                round_and_accumulate(e, 0, FIRST_SHARE)
-                empty_and_scatter(e - 1, 0, 0, C, spent(wb_raw[e, 0]))
-                round_and_accumulate(e, 1, P)
-                round_and_accumulate(e, 2, LAST_SHARE)
+                round_and_accumulate(e, 0, 80)
+                early = spent(wb_raw[e, 0])[:, : C + P]
+                nc.scalar.copy(out=early, in_=dx_bank[(e - 1) % 2][:, : C + P])
+                scatter_on_scalar(0, (e - 1) * C, early[:, :C])
+                scatter_on_scalar(1, (e - 1) * C, early[:, C:])
+                round_and_accumulate(e, 1, 128)
+                round_and_accumulate(e, 2, 84)
+                empty_and_scatter(e - 1, 1, P, P, wb_raw[e, 2][:, 0, H - P :])
                 wa_tiles = [round_wa_tile(e, kt) for kt in range(K_TILES)]
-                empty_and_scatter(e - 1, 1, 0, C, spent(wa_raw[e]))
             factor = turn("factor", [P, PACK, C], F32)
-            dh = turn("dh", [P, C, PACK], BF16)
+            dh = turn("dh", [P, C * PACK], BF16)
             wa_codes, wa_plane = turn("wa_codes", [P, K], U32), turn("wa_plane", [P, K], U8)
             dh_codes, dh_plane = turn("dh_codes", [P, C], U32), turn("dh_plane", [P, C], U8)
             for half in range(HALVES):
                 make_factor(e, factor, half * P, P)
-            for half in range(HALVES):
-                make_dh(half, factor, dh)
-            for half in range(HALVES):
-                slots = slice(half * P, (half + 1) * P)
-                quantize(dh_codes[:, slots], dh_plane[:, slots], dh[:, slots, :].rearrange("p j t -> p (j t)"))
-                if e == LAST:
-                    quantize(wa_codes[:, slots], wa_plane[:, slots], wa_tiles[half])
-                elif half == 0:
-                    quantize(wa_codes[:], wa_plane[:], wa_rounded)
             if e < LAST:
-                banks = [dx_bank[e % 2][:, kt * C : (kt + 1) * C] for kt in range(K_TILES)]
-            else:
-                banks = [dx_bank[(e + kt) % 2][:, :C] for kt in range(K_TILES)]
-            second_product(banks, wa_codes, wa_plane, dh_codes[:], dh_plane[:])
-        last_steps = ((nc.vector.tensor_copy, scatter_on_vector), (nc.scalar.copy, scatter_on_scalar))
-        for kt, (copy, scatter) in enumerate(last_steps):
-            dx = keep("dx_last%d" % kt, [P, C], F32)
-            copy(out=dx[:], in_=banks[kt])
-            scatter(kt, LAST * C, dx[:])
+                halves = [dh[:, half * PASS : (half + 1) * PASS] for half in range(HALVES)]
+                for half in range(HALVES):
+                    make_dh(half, factor, halves[half])
+                for half in range(HALVES):
+                    quantize_dh(half, halves[half], dh_codes, dh_plane)
+                quantize(wa_codes[:], wa_plane[:], wa_rounded)
+                for kt in range(K_TILES):
+                    rows = slice(kt * P, (kt + 1) * P)
+                    bank = dx_bank[e % 2][:, kt * C : (kt + 1) * C]
+                    second_product(bank, wa_codes[:, rows], wa_plane[:, rows], dh_codes[:], dh_plane[:])
+
+        def last_product(kt, half):
+            rows, slots = slice(kt * P, (kt + 1) * P), slice(half * P, (half + 1) * P)
+            second_product(last[kt, half], wa_codes[:, rows], wa_plane[:, rows], dh_codes[:, slots], dh_plane[:, slots])
+
+        last = {(0, 0): dx_bank[1][:, :P], (0, 1): sums[0][:, 0, :], (1, 0): dx_bank[0][:, :P], (1, 1): dx_bank[0][:, P : 2 * P]}
+        dx = [keep("dx_last%d" % half, [P, P], F32) for half in range(HALVES)] + [keep("dx_last2", [P, C], F32)]
+        make_dh(0, factor, dh[:, :PASS])
+        quantize(wa_codes[:, :P], wa_plane[:, :P], wa_tiles[0])
+        quantize_dh(0, dh[:, :PASS], dh_codes, dh_plane)
+        last_product(0, 0)
+        nc.scalar.copy(out=dx[0][:], in_=last[0, 0])
+        scatter_on_scalar(0, LAST * C, dx[0][:])
+        make_dh(1, factor, wa_tiles[0])
+        quantize(wa_codes[:, P:], wa_plane[:, P:], wa_tiles[1])
+        quantize_dh(1, wa_tiles[0], dh_codes, dh_plane)
+        last_product(0, 1)
+        last_product(1, 0)
+        last_product(1, 1)
+        nc.vector.tensor_copy(out=dx[1][:], in_=last[0, 1])
+        scatter_on_vector(0, LAST * C + P, dx[1][:])
+        nc.scalar.copy(out=dx[2][:], in_=dx_bank[0][:, :C])
+        scatter_on_scalar(1, LAST * C, dx[2][:])
 
         frozen_layer()
         for piece, (kt, cols) in enumerate(pieces):

@@ -25,12 +25,15 @@ PASSES = N // PASS
 BANK = 512
 K_TILES = K // P
 HALVES = C // P
-QUADS = P // 32
+QUAD = 32
+ROWS = 4
+RUN = 4
 GATHER = T // 2
 LAST = E - 1
-FIRST_SHARE = 48
-LAST_SHARE = 84
-FINAL_SHARE = 84
+
+FIRST_SHARES = (0, 0, P // 2)
+MIDDLE_SHARES = (P // 4, P, P // 2)
+LAST_SHARES = (80, P, 84)
 
 
 def tile_moe_adb_relu2_kernel(
@@ -47,6 +50,9 @@ def tile_moe_adb_relu2_kernel(
 
         def turn(name, shape, dtype):
             return ring.tile(shape, dtype, name=name, align_bytes=64)
+
+        def part(index, width):
+            return slice(index * width, (index + 1) * width)
 
         def list_slice(first, count):
             return offsets[:, first // 16 : (first + count) // 16]
@@ -76,35 +82,33 @@ def tile_moe_adb_relu2_kernel(
 
         def load_wb(e, s):
             wb_raw[e, s] = keep("wb_raw%d_%d" % (e, s), [P, PACK, H], F32)
-            rows = wbt[e, s * PASS : (s + 1) * PASS, :].rearrange("(p d) i -> p d i", d=PACK)
-            nc.sync.dma_start(out=wb_raw[e, s][:], in_=rows)
+            nc.sync.dma_start(out=wb_raw[e, s][:], in_=wbt[e, part(s, PASS), :].rearrange("(p d) i -> p d i", d=PACK))
 
         def load_a(e):
             a_sb[e] = keep("a%d" % e, [P, PACK, C], F32)
-            rows = a.rearrange("(p t) j -> p t j", t=PACK)
-            nc.sync.dma_start(out=a_sb[e][:], in_=rows[:, :, e * C : (e + 1) * C])
+            nc.sync.dma_start(out=a_sb[e][:], in_=a.rearrange("(p t) j -> p t j", t=PACK)[:, :, part(e, C)])
 
         def load_wa(e):
             wa_raw[e] = keep("wa_raw%d" % e, [P, PACK, K], F32)
             nc.sync.dma_start(out=wa_raw[e][:], in_=wat[e].rearrange("(p t) k -> p t k", t=PACK))
 
         def load_planes(planes, scales):
-            for row in range(4):
+            for row in range(ROWS):
                 nc.sync.dma_start(
-                    out=planes[row:P:32, :, :].bitcast(I32),
-                    in_=scales[:, row::4, :].rearrange("s q t -> q s t").bitcast(I32),
+                    out=planes[row:P:QUAD, :, :].bitcast(I32),
+                    in_=scales[:, row::ROWS, :].rearrange("s q t -> q s t").bitcast(I32),
                 )
 
-        nc.sync.dma_start(offsets[:], offs)
         load_dy(0)
+        nc.sync.dma_start(offsets[:], offs)
         load_dy(1)
         load_wb(0, 0)
         load_dy(2)
         nc.sync.dma_start(out=gate_rows[: T // P, :], in_=gate[0, :].rearrange("(m p) -> m p", p=P))
-        for quad in range(QUADS):
+        for quad in range(P // QUAD):
             nc.sync.dma_start(
-                out=dy_packed[32 * quad : 32 * quad + 4 * PASSES, :].bitcast(I32),
-                in_=dy_scales[:, 4 * quad : 4 * quad + 4, :].bitcast(I32),
+                out=dy_packed[QUAD * quad : QUAD * quad + ROWS * PASSES, :].bitcast(I32),
+                in_=dy_scales[:, part(quad, ROWS), :].bitcast(I32),
             )
         for e in range(E):
             for s in range(PASSES):
@@ -119,21 +123,18 @@ def tile_moe_adb_relu2_kernel(
 
         sums = [psum.tile([P, PACK, P], F32, name="sums%d" % half) for half in range(HALVES)]
         dx_bank = [psum.tile([P, BANK], F32, name="dx_bank%d" % b) for b in range(2)]
-        pieces = [(kt, slice(h * BANK, (h + 1) * BANK)) for kt in range(K_TILES) for h in range(T // BANK)]
+        pieces = [(kt, part(h, BANK)) for kt in range(K_TILES) for h in range(T // BANK)]
         base = [psum.tile([P, BANK], F32, name="base%d" % piece) for piece in range(len(pieces))]
+        gate_banks = base[-(T // BANK) :]
 
         def spread_gate():
             gate_cols = keep("gate_cols", [P, T // P], F32)
             nc.tensor.transpose(base[0][:, :P], gate_rows[:], identity[:])
             nc.scalar.mul(gate_cols[:], base[0][:, : T // P], 2.0)
-            for h in range(T // BANK):
-                for m in range(BANK // P):
-                    column = h * (BANK // P) + m
-                    nc.tensor.transpose(
-                        base[2 + h][:, m * P : (m + 1) * P],
-                        gate_cols[:, column : column + 1].to_broadcast([P, P]),
-                        identity[:],
-                    )
+            for column in range(T // P):
+                h, m = divmod(column, BANK // P)
+                spread = gate_cols[:, column : column + 1].to_broadcast([P, P])
+                nc.tensor.transpose(gate_banks[h][:, part(m, P)], spread, identity[:])
 
         def gather(into, source):
             for first in range(0, E * C, GATHER):
@@ -142,21 +143,7 @@ def tile_moe_adb_relu2_kernel(
         def quantize(codes, plane, values):
             nc.vector.quantize_mx(out=codes.bitcast(FP8X4), scales=plane, in_=values)
 
-        def accumulate(e, s, codes, plane, tiles):
-            for half in range(HALVES):
-                cols = slice(e * C + half * P, e * C + (half + 1) * P)
-                for t in tiles:
-                    nc.tensor.matmul_mx(
-                        out=sums[half][:, t, :],
-                        lhsT=codes[:, t * P : (t + 1) * P].bitcast(FP8X4),
-                        lhsT_scale=plane[:, t * P : (t + 1) * P],
-                        rhs=slot_words[s][:, cols].bitcast(FP8X4),
-                        rhs_scale=slot_scales[4 * s :, cols],
-                        start=(s == 0 and t == 0),
-                        stop=(s == PASSES - 1 and t == PACK - 1),
-                    )
-
-        def round_and_accumulate(e, s, on_vector):
+        def first_product_pass(e, s, on_vector):
             rounded = turn("rounded", [P, PACK * H], BF16)
             codes, plane = turn("wb_codes", [P, H], U32), turn("wb_plane", [P, H], U8)
             words = rounded[:].rearrange("p (t m d) -> p m d t", t=PACK, d=PACK)
@@ -166,31 +153,19 @@ def tile_moe_adb_relu2_kernel(
             if on_vector < P:
                 nc.scalar.copy(out=words[:, on_vector:], in_=raw[:, on_vector:])
             quantize(codes[:], plane[:], rounded[:])
-            accumulate(e, s, codes, plane, range(PACK))
+            for half in range(HALVES):
+                cols = part(e * HALVES + half, P)
+                for t in range(PACK):
+                    nc.tensor.matmul_mx(
+                        out=sums[half][:, t, :],
+                        lhsT=codes[:, part(t, P)].bitcast(FP8X4),
+                        lhsT_scale=plane[:, part(t, P)],
+                        rhs=slot_words[s][:, cols].bitcast(FP8X4),
+                        rhs_scale=slot_scales[ROWS * s :, cols],
+                        start=(s == 0 and t == 0),
+                        stop=(s == PASSES - 1 and t == PACK - 1),
+                    )
             return rounded
-
-        def spent(tile):
-            return tile[:].rearrange("p d i -> p (d i)")
-
-        def empty_and_scatter(e, kt, first, count, through):
-            nc.scalar.copy(out=through[:, :count], in_=dx_bank[e % 2][:, kt * C + first : kt * C + first + count])
-            scatter_on_scalar(kt, e * C + first, through[:, :count])
-
-        def round_wa(e):
-            rounded = turn("wa_rounded", [P, PACK * K], BF16)
-            nc.scalar.copy(
-                out=rounded[:].rearrange("p (c r t) -> p c t r", r=4, t=PACK),
-                in_=wa_raw[e][:].rearrange("p t (c r) -> p c t r", r=4),
-            )
-            return rounded
-
-        def round_wa_tile(e, kt):
-            rounded = keep("wa_rounded%d" % kt, [P, PACK * P], BF16)
-            nc.scalar.copy(
-                out=rounded[:].rearrange("p (c r t) -> p c t r", r=4, t=PACK),
-                in_=wa_raw[e][:, :, kt * P : (kt + 1) * P].rearrange("p t (c r) -> p c t r", r=4),
-            )
-            return rounded[:]
 
         def round_wa_on_gpsimd(e, quantized):
             rounded = quantized[:, : PACK * K]
@@ -204,28 +179,35 @@ def tile_moe_adb_relu2_kernel(
             )
             return rounded
 
-        def make_factor(e, factor, first, count):
-            nc.vector.scalar_tensor_tensor(
-                out=factor[:, :, first : first + count],
-                in0=a_sb[e][:, :, first : first + count],
-                scalar=0.0,
-                in1=base[2 + e // 2][:, e % 2 * C + first : e % 2 * C + first + count].unsqueeze(1).to_broadcast([P, PACK, count]),
-                op0=ALU.max,
-                op1=ALU.mult,
+        def round_wa_on_scalar(e, kt):
+            rounded = keep("wa_rounded%d" % kt, [P, PACK * P], BF16)
+            nc.scalar.copy(
+                out=rounded[:].rearrange("p (c r t) -> p c t r", r=RUN, t=PACK),
+                in_=wa_raw[e][:, :, part(kt, P)].rearrange("p t (c r) -> p c t r", r=RUN),
             )
+            return rounded[:]
+
+        def make_factor(e):
+            factor = turn("factor", [P, PACK, C], F32)
+            for half in range(HALVES):
+                h, m = divmod(e * HALVES + half, BANK // P)
+                nc.vector.scalar_tensor_tensor(
+                    out=factor[:, :, part(half, P)],
+                    in0=a_sb[e][:, :, part(half, P)],
+                    scalar=0.0,
+                    in1=gate_banks[h][:, part(m, P)].unsqueeze(1).to_broadcast([P, PACK, P]),
+                    op0=ALU.max,
+                    op1=ALU.mult,
+                )
+            return factor
 
         def make_dh(half, factor, values):
-            slots = slice(half * P, (half + 1) * P)
             nc.vector.tensor_tensor(
                 out=values.rearrange("p (c r t) -> p c t r", r=2, t=PACK),
                 in0=sums[half][:].rearrange("p t (c r) -> p c t r", r=2),
-                in1=factor[:, :, slots].rearrange("p t (c r) -> p c t r", r=2),
+                in1=factor[:, :, part(half, P)].rearrange("p t (c r) -> p c t r", r=2),
                 op=ALU.mult,
             )
-
-        def quantize_dh(half, values, dh_codes, dh_plane):
-            slots = slice(half * P, (half + 1) * P)
-            quantize(dh_codes[:, slots], dh_plane[:, slots], values)
 
         def second_product(bank, wa_codes, wa_plane, dh_codes, dh_plane):
             nc.tensor.matmul_mx(
@@ -244,91 +226,91 @@ def tile_moe_adb_relu2_kernel(
         def scatter_on_vector(kt, first, values):
             nc.vector.tensor_copy(window[kt][:].indirect(list_slice(first, values.shape[1])), values)
 
-        def frozen_layer():
-            for piece, (kt, cols) in enumerate(pieces):
-                for s in range(PASSES):
-                    nc.tensor.matmul_mx(
-                        out=base[piece][:],
-                        lhsT=wt_codes[:, s, 2 * kt * P : 2 * (kt + 1) * P].bitcast(FP4X4),
-                        lhsT_scale=wt_plane[:, s, kt * P : (kt + 1) * P],
-                        rhs=dy[s][:, cols].bitcast(FP8X4),
-                        rhs_scale=dy_packed[:, cols] if s == 0 else dy_plane[:, s - 1, cols],
-                        start=(s == 0),
-                        stop=(s == PASSES - 1),
-                    )
+        def scatter_behind(raw, e, kt, first, count):
+            through = raw[:, 0, H - count :]
+            nc.scalar.copy(out=through, in_=dx_bank[e % 2][:, kt * C + first : kt * C + first + count])
+            scatter_on_scalar(kt, e * C + first, through)
+
+        def mx_tiles():
+            dh = turn("dh", [P, C * PACK], BF16)
+            wa_mx = turn("wa_codes", [P, K], U32), turn("wa_plane", [P, K], U8)
+            dh_mx = turn("dh_codes", [P, C], U32), turn("dh_plane", [P, C], U8)
+            return dh, wa_mx, dh_mx
+
+        def columns(mx, index):
+            return [tile[:, part(index, P)] for tile in mx]
 
         spread_gate()
         for s in range(PASSES):
             gather(slot_words[s][:].bitcast(U32), dy[s][:].bitcast(U32))
         gather(slot_scales[:], dy_packed[:])
 
-        for e in range(E):
-            if e == 0:
-                round_and_accumulate(e, 0, 0)
-                round_and_accumulate(e, 1, 0)
-                wa_rounded = round_wa_on_gpsimd(e, round_and_accumulate(e, 2, 64))
-            elif e < LAST:
-                round_and_accumulate(e, 0, 32)
-                empty_and_scatter(e - 1, 0, 0, C, wb_raw[e, 0][:, 0, H - C :])
-                round_and_accumulate(e, 1, 128)
-                wa_rounded = round_wa_on_gpsimd(e, round_and_accumulate(e, 2, 64))
-                empty_and_scatter(e - 1, 1, 0, C, wb_raw[e, 2][:, 0, H - C :])
-            else:
-                round_and_accumulate(e, 0, 80)
-                early = spent(wb_raw[e, 0])[:, : C + P]
-                nc.scalar.copy(out=early, in_=dx_bank[(e - 1) % 2][:, : C + P])
-                scatter_on_scalar(0, (e - 1) * C, early[:, :C])
-                scatter_on_scalar(1, (e - 1) * C, early[:, C:])
-                round_and_accumulate(e, 1, 128)
-                round_and_accumulate(e, 2, 84)
-                empty_and_scatter(e - 1, 1, P, P, wb_raw[e, 2][:, 0, H - P :])
-                wa_tiles = [round_wa_tile(e, kt) for kt in range(K_TILES)]
-            factor = turn("factor", [P, PACK, C], F32)
-            dh = turn("dh", [P, C * PACK], BF16)
-            wa_codes, wa_plane = turn("wa_codes", [P, K], U32), turn("wa_plane", [P, K], U8)
-            dh_codes, dh_plane = turn("dh_codes", [P, C], U32), turn("dh_plane", [P, C], U8)
+        for e in range(LAST):
+            shares = MIDDLE_SHARES if e > 0 else FIRST_SHARES
+            first_product_pass(e, 0, shares[0])
+            if e > 0:
+                scatter_behind(wb_raw[e, 0], e - 1, 0, 0, C)
+            first_product_pass(e, 1, shares[1])
+            wa_rounded = round_wa_on_gpsimd(e, first_product_pass(e, 2, shares[2]))
+            if e > 0:
+                scatter_behind(wb_raw[e, 2], e - 1, 1, 0, C)
+            factor = make_factor(e)
+            dh, wa_mx, dh_mx = mx_tiles()
             for half in range(HALVES):
-                make_factor(e, factor, half * P, P)
-            if e < LAST:
-                halves = [dh[:, half * PASS : (half + 1) * PASS] for half in range(HALVES)]
-                for half in range(HALVES):
-                    make_dh(half, factor, halves[half])
-                for half in range(HALVES):
-                    quantize_dh(half, halves[half], dh_codes, dh_plane)
-                quantize(wa_codes[:], wa_plane[:], wa_rounded)
-                for kt in range(K_TILES):
-                    rows = slice(kt * P, (kt + 1) * P)
-                    bank = dx_bank[e % 2][:, kt * C : (kt + 1) * C]
-                    second_product(bank, wa_codes[:, rows], wa_plane[:, rows], dh_codes[:], dh_plane[:])
+                make_dh(half, factor, dh[:, part(half, PASS)])
+            for half in range(HALVES):
+                quantize(*columns(dh_mx, half), dh[:, part(half, PASS)])
+            quantize(wa_mx[0][:], wa_mx[1][:], wa_rounded)
+            for kt in range(K_TILES):
+                second_product(dx_bank[e % 2][:, part(kt, C)], *columns(wa_mx, kt), dh_mx[0][:], dh_mx[1][:])
 
-        def last_product(kt, half):
-            rows, slots = slice(kt * P, (kt + 1) * P), slice(half * P, (half + 1) * P)
-            second_product(last[kt, half], wa_codes[:, rows], wa_plane[:, rows], dh_codes[:, slots], dh_plane[:, slots])
+        before = LAST - 1
+        first_product_pass(LAST, 0, LAST_SHARES[0])
+        early = wb_raw[LAST, 0][:, 0, : C + P]
+        nc.scalar.copy(out=early, in_=dx_bank[before % 2][:, : C + P])
+        scatter_on_scalar(0, before * C, early[:, :C])
+        scatter_on_scalar(1, before * C, early[:, C:])
+        first_product_pass(LAST, 1, LAST_SHARES[1])
+        first_product_pass(LAST, 2, LAST_SHARES[2])
+        scatter_behind(wb_raw[LAST, 2], before, 1, P, P)
+        wa_tiles = [round_wa_on_scalar(LAST, kt) for kt in range(K_TILES)]
+        factor = make_factor(LAST)
+        dh, wa_mx, dh_mx = mx_tiles()
 
-        last = {(0, 0): dx_bank[1][:, :P], (0, 1): sums[0][:, 0, :], (1, 0): dx_bank[0][:, :P], (1, 1): dx_bank[0][:, P : 2 * P]}
-        dx = [keep("dx_last%d" % half, [P, P], F32) for half in range(HALVES)] + [keep("dx_last2", [P, C], F32)]
+        tile0_banks = [dx_bank[LAST % 2][:, :P], sums[0][:, 0, :]]
+        tile1_bank = dx_bank[before % 2]
+        tile0_dx = [keep("tile0_dx%d" % half, [P, P], F32) for half in range(HALVES)]
+        tile1_dx = keep("tile1_dx", [P, C], F32)
+
         make_dh(0, factor, dh[:, :PASS])
-        quantize(wa_codes[:, :P], wa_plane[:, :P], wa_tiles[0])
-        quantize_dh(0, dh[:, :PASS], dh_codes, dh_plane)
-        last_product(0, 0)
-        nc.scalar.copy(out=dx[0][:], in_=last[0, 0])
-        scatter_on_scalar(0, LAST * C, dx[0][:])
-        make_dh(1, factor, wa_tiles[0])
-        quantize(wa_codes[:, P:], wa_plane[:, P:], wa_tiles[1])
-        quantize_dh(1, wa_tiles[0], dh_codes, dh_plane)
-        last_product(0, 1)
-        last_product(1, 0)
-        last_product(1, 1)
-        nc.vector.tensor_copy(out=dx[1][:], in_=last[0, 1])
-        scatter_on_vector(0, LAST * C + P, dx[1][:])
-        nc.scalar.copy(out=dx[2][:], in_=dx_bank[0][:, :C])
-        scatter_on_scalar(1, LAST * C, dx[2][:])
+        quantize(*columns(wa_mx, 0), wa_tiles[0])
+        quantize(*columns(dh_mx, 0), dh[:, :PASS])
+        second_product(tile0_banks[0], *columns(wa_mx, 0), *columns(dh_mx, 0))
+        nc.scalar.copy(out=tile0_dx[0][:], in_=tile0_banks[0])
+        scatter_on_scalar(0, LAST * C, tile0_dx[0][:])
 
-        frozen_layer()
+        make_dh(1, factor, wa_tiles[0])
+        quantize(*columns(wa_mx, 1), wa_tiles[1])
+        quantize(*columns(dh_mx, 1), wa_tiles[0])
+        second_product(tile0_banks[1], *columns(wa_mx, 0), *columns(dh_mx, 1))
+        for half in range(HALVES):
+            second_product(tile1_bank[:, part(half, P)], *columns(wa_mx, 1), *columns(dh_mx, half))
+        nc.vector.tensor_copy(out=tile0_dx[1][:], in_=tile0_banks[1])
+        scatter_on_vector(0, LAST * C + P, tile0_dx[1][:])
+        nc.scalar.copy(out=tile1_dx[:], in_=tile1_bank[:, :C])
+        scatter_on_scalar(1, LAST * C, tile1_dx[:])
+
         for piece, (kt, cols) in enumerate(pieces):
-            width = BANK // 2 if piece == 0 else BANK
-            for first in range(0, BANK, width):
-                tokens = slice(cols.start + first, cols.start + first + width)
-                sums_here = base[piece][:, first : first + width]
-                nc.vector.tensor_tensor(out=window[kt][:, tokens], in0=sums_here, in1=window[kt][:, tokens], op=ALU.add)
-                nc.sync.dma_start(out=out[kt * P : (kt + 1) * P, tokens], in_=window[kt][:, tokens])
+            for s in range(PASSES):
+                nc.tensor.matmul_mx(
+                    out=base[piece][:],
+                    lhsT=wt_codes[:, s, part(kt, 2 * P)].bitcast(FP4X4),
+                    lhsT_scale=wt_plane[:, s, part(kt, P)],
+                    rhs=dy[s][:, cols].bitcast(FP8X4),
+                    rhs_scale=dy_packed[:, cols] if s == 0 else dy_plane[:, s - 1, cols],
+                    start=(s == 0),
+                    stop=(s == PASSES - 1),
+                )
+        for piece, (kt, cols) in enumerate(pieces):
+            nc.vector.tensor_tensor(out=window[kt][:, cols], in0=base[piece][:], in1=window[kt][:, cols], op=ALU.add)
+            nc.sync.dma_start(out=out[part(kt, P), cols], in_=window[kt][:, cols])

@@ -31,9 +31,11 @@ RUN = 4
 GATHER = T // 2
 LAST = E - 1
 
-FIRST_SHARES = (0, 0, P // 2)
-MIDDLE_SHARES = (P // 4, P, P // 2)
-LAST_SHARES = (80, P, 84)
+FIRST_SHARES = ((0,), (0,), (64,))
+MIDDLE_SHARES = ((32,), (128,), (64,))
+LAST_SHARES = ((64,), (128,), (0, 32, 32))
+LAST_PIECES = (64, 32, 32)
+STORE_CUTS = ((0, 128, 512, 1024), (0, 512, 896, 1024))
 
 
 def tile_moe_adb_relu2_kernel(
@@ -80,21 +82,27 @@ def tile_moe_adb_relu2_kernel(
         def load_dy(s):
             nc.sync.dma_start(out=dy[s][:], in_=dy_words[s].rearrange("p t d -> p (t d)").bitcast(I32))
 
-        def load_wb(e, s):
-            wb_raw[e, s] = keep("wb_raw%d_%d" % (e, s), [P, PACK, H], F32)
-            nc.sync.dma_start(out=wb_raw[e, s][:], in_=wbt[e, part(s, PASS), :].rearrange("(p d) i -> p d i", d=PACK))
+        def load_wb(e, s, widths=(P,)):
+            rows = wbt[e, part(s, PASS), :].rearrange("(p d) i -> p d i", d=PACK)
+            wb_raw[e, s] = []
+            first = 0
+            for piece, width in enumerate(widths):
+                raw = keep("wb_raw%d_%d_%d" % (e, s, piece), [P, PACK, PACK * width], F32)
+                nc.sync.dma_start(out=raw[:], in_=rows[:, :, PACK * first : PACK * (first + width)])
+                wb_raw[e, s].append(raw)
+                first = first + width
 
         def load_a(e):
             a_sb[e] = keep("a%d" % e, [P, PACK, C], F32)
             nc.sync.dma_start(out=a_sb[e][:], in_=a.rearrange("(p t) j -> p t j", t=PACK)[:, :, part(e, C)])
 
-        def load_wa(e):
-            wa_raw[e] = keep("wa_raw%d" % e, [P, PACK, K], F32)
-            nc.sync.dma_start(out=wa_raw[e][:], in_=wat[e].rearrange("(p t) k -> p t k", t=PACK))
+        def load_wa(e, first, last):
+            wa_raw[e, first] = keep("wa_raw%d_%d" % (e, first), [P, PACK, last - first], F32)
+            nc.sync.dma_start(out=wa_raw[e, first][:], in_=wat[e].rearrange("(p t) k -> p t k", t=PACK)[:, :, first:last])
 
         def load_planes(planes, scales):
             for row in range(ROWS):
-                nc.sync.dma_start(
+                nc.gpsimd.dma_start(
                     out=planes[row:P:QUAD, :, :].bitcast(I32),
                     in_=scales[:, row::ROWS, :].rearrange("s q t -> q s t").bitcast(I32),
                 )
@@ -113,24 +121,25 @@ def tile_moe_adb_relu2_kernel(
         for e in range(E):
             for s in range(PASSES):
                 if (e, s) not in wb_raw:
-                    load_wb(e, s)
-                if (e, s) == (LAST, 0):
-                    load_planes(wt_plane, wt_scales)
+                    load_wb(e, s, LAST_PIECES if (e, s) == (LAST, PASSES - 1) else (P,))
             load_a(e)
-            load_wa(e)
+            load_wa(e, 0, K if e < LAST else P)
         nc.sync.dma_start(out=wt_codes[:].bitcast(I32), in_=wt_words.rearrange("s p b -> p s b").bitcast(I32))
+        load_wa(LAST, P, K)
+        load_planes(wt_plane, wt_scales)
         load_planes(dy_plane, dy_scales[1:])
 
         sums = [psum.tile([P, PACK, P], F32, name="sums%d" % half) for half in range(HALVES)]
-        dx_bank = [psum.tile([P, BANK], F32, name="dx_bank%d" % b) for b in range(2)]
-        pieces = [(kt, part(h, BANK)) for kt in range(K_TILES) for h in range(T // BANK)]
-        base = [psum.tile([P, BANK], F32, name="base%d" % piece) for piece in range(len(pieces))]
-        gate_banks = base[-(T // BANK) :]
+        dx_bank = [psum.tile([P, BANK], F32, name="dx_bank%d" % kt) for kt in range(K_TILES)]
+        halves = [(kt, h) for kt in range(K_TILES) for h in range(T // BANK)]
+        base = {(0, h): psum.tile([P, BANK], F32, name="base%d" % h)[:] for h in range(T // BANK)}
+        base[1, 0], base[1, 1] = [sums[half][:].rearrange("p t c -> p (t c)") for half in (1, 0)]
+        gate_banks = [psum.tile([P, BANK], F32, name="gate%d" % h) for h in range(T // BANK)]
 
         def spread_gate():
             gate_cols = keep("gate_cols", [P, T // P], F32)
-            nc.tensor.transpose(base[0][:, :P], gate_rows[:], identity[:])
-            nc.scalar.mul(gate_cols[:], base[0][:, : T // P], 2.0)
+            nc.tensor.transpose(base[0, 0][:, :P], gate_rows[:], identity[:])
+            nc.scalar.mul(gate_cols[:], base[0, 0][:, : T // P], 2.0)
             for column in range(T // P):
                 h, m = divmod(column, BANK // P)
                 spread = gate_cols[:, column : column + 1].to_broadcast([P, P])
@@ -143,15 +152,20 @@ def tile_moe_adb_relu2_kernel(
         def quantize(codes, plane, values):
             nc.vector.quantize_mx(out=codes.bitcast(FP8X4), scales=plane, in_=values)
 
-        def first_product_pass(e, s, on_vector):
+        def first_product_pass(e, s, shares):
             rounded = turn("rounded", [P, PACK * H], BF16)
             codes, plane = turn("wb_codes", [P, H], U32), turn("wb_plane", [P, H], U8)
             words = rounded[:].rearrange("p (t m d) -> p m d t", t=PACK, d=PACK)
-            raw = wb_raw[e, s][:].rearrange("p d (m t) -> p m d t", t=PACK)
-            if on_vector > 0:
-                nc.vector.tensor_copy(out=words[:, :on_vector], in_=raw[:, :on_vector])
-            if on_vector < P:
-                nc.scalar.copy(out=words[:, on_vector:], in_=raw[:, on_vector:])
+            first = 0
+            for piece, on_vector in enumerate(shares):
+                raw = wb_raw[e, s][piece][:].rearrange("p d (m t) -> p m d t", t=PACK)
+                width = raw.shape[1]
+                into = words[:, first : first + width]
+                first = first + width
+                if on_vector > 0:
+                    nc.vector.tensor_copy(out=into[:, :on_vector], in_=raw[:, :on_vector])
+                if on_vector < width:
+                    nc.scalar.copy(out=into[:, on_vector:], in_=raw[:, on_vector:])
             quantize(codes[:], plane[:], rounded[:])
             for half in range(HALVES):
                 cols = part(e * HALVES + half, P)
@@ -167,11 +181,10 @@ def tile_moe_adb_relu2_kernel(
                     )
             return rounded
 
-        def round_wa_on_gpsimd(e, quantized):
-            rounded = quantized[:, : PACK * K]
+        def round_wa_on_gpsimd(e, rounded):
             nc.gpsimd.tensor_scalar(
                 out=rounded.rearrange("p (k t) -> p k t", t=PACK),
-                in0=wa_raw[e][:].rearrange("p t k -> p k t"),
+                in0=wa_raw[e, 0][:].rearrange("p t k -> p k t"),
                 scalar1=1.0,
                 scalar2=0.0,
                 op0=ALU.mult,
@@ -180,10 +193,10 @@ def tile_moe_adb_relu2_kernel(
             return rounded
 
         def round_wa_on_scalar(e, kt):
-            rounded = keep("wa_rounded%d" % kt, [P, PACK * P], BF16)
+            rounded = turn("wa_rounded", [P, PACK * P], BF16)
             nc.scalar.copy(
                 out=rounded[:].rearrange("p (c r t) -> p c t r", r=RUN, t=PACK),
-                in_=wa_raw[e][:, :, part(kt, P)].rearrange("p t (c r) -> p c t r", r=RUN),
+                in_=wa_raw[e, kt * P][:].rearrange("p t (c r) -> p c t r", r=RUN),
             )
             return rounded[:]
 
@@ -220,22 +233,22 @@ def tile_moe_adb_relu2_kernel(
                 stop=True,
             )
 
-        def scatter_on_scalar(kt, first, values):
-            nc.scalar.activation(window[kt][:].indirect(list_slice(first, values.shape[1])), values, COPY)
+        def scatter_on_scalar(kt, first, bank, values=None):
+            count = bank.shape[1]
+            if values is None:
+                values = turn("dx%d" % count, [P, count], F32)[:]
+            nc.scalar.copy(out=values, in_=bank)
+            nc.scalar.activation(window[kt][:].indirect(list_slice(first, count)), values, COPY)
 
-        def scatter_on_vector(kt, first, values):
-            nc.vector.tensor_copy(window[kt][:].indirect(list_slice(first, values.shape[1])), values)
+        def scatter_on_vector(kt, first, bank):
+            count = bank.shape[1]
+            values = keep("dx_last", [P, count], F32)
+            nc.vector.tensor_copy(out=values[:], in_=bank)
+            nc.vector.tensor_copy(window[kt][:].indirect(list_slice(first, count)), values[:])
 
-        def scatter_behind(raw, e, kt, first, count):
-            through = raw[:, 0, H - count :]
-            nc.scalar.copy(out=through, in_=dx_bank[e % 2][:, kt * C + first : kt * C + first + count])
-            scatter_on_scalar(kt, e * C + first, through)
-
-        def mx_tiles():
-            dh = turn("dh", [P, C * PACK], BF16)
-            wa_mx = turn("wa_codes", [P, K], U32), turn("wa_plane", [P, K], U8)
-            dh_mx = turn("dh_codes", [P, C], U32), turn("dh_plane", [P, C], U8)
-            return dh, wa_mx, dh_mx
+        def spent_columns(e, s):
+            raw = wb_raw[e, s][0]
+            return raw[:, 0, raw.shape[2] - C :]
 
         def columns(mx, index):
             return [tile[:, part(index, P)] for tile in mx]
@@ -245,65 +258,50 @@ def tile_moe_adb_relu2_kernel(
             gather(slot_words[s][:].bitcast(U32), dy[s][:].bitcast(U32))
         gather(slot_scales[:], dy_packed[:])
 
-        for e in range(LAST):
-            shares = MIDDLE_SHARES if e > 0 else FIRST_SHARES
-            first_product_pass(e, 0, shares[0])
-            if e > 0:
-                scatter_behind(wb_raw[e, 0], e - 1, 0, 0, C)
-            first_product_pass(e, 1, shares[1])
-            wa_rounded = round_wa_on_gpsimd(e, first_product_pass(e, 2, shares[2]))
-            if e > 0:
-                scatter_behind(wb_raw[e, 2], e - 1, 1, 0, C)
+        for e in range(E):
+            shares = FIRST_SHARES if e == 0 else LAST_SHARES if e == LAST else MIDDLE_SHARES
+            for s in range(PASSES):
+                spent = first_product_pass(e, s, shares[s])
+                if e > 0 and s != 1:
+                    kt = s // 2
+                    scatter_on_scalar(kt, (e - 1) * C, dx_bank[kt][:, :C], spent_columns(e, s))
+            if e < LAST:
+                wa_rounded = round_wa_on_gpsimd(e, spent[:, : PACK * K])
+            else:
+                wa_tiles = [round_wa_on_gpsimd(e, spent[:, :PASS]), round_wa_on_scalar(e, 1)]
             factor = make_factor(e)
-            dh, wa_mx, dh_mx = mx_tiles()
-            for half in range(HALVES):
-                make_dh(half, factor, dh[:, part(half, PASS)])
-            for half in range(HALVES):
-                quantize(*columns(dh_mx, half), dh[:, part(half, PASS)])
-            quantize(wa_mx[0][:], wa_mx[1][:], wa_rounded)
-            for kt in range(K_TILES):
-                second_product(dx_bank[e % 2][:, part(kt, C)], *columns(wa_mx, kt), dh_mx[0][:], dh_mx[1][:])
+            dh = turn("dh", [P, C * PACK], BF16)
+            wa_mx = turn("wa_codes", [P, K], U32), turn("wa_plane", [P, K], U8)
+            dh_mx = turn("dh_codes", [P, C], U32), turn("dh_plane", [P, C], U8)
+            if e < LAST:
+                for half in range(HALVES):
+                    make_dh(half, factor, dh[:, part(half, PASS)])
+                for half in range(HALVES):
+                    quantize(*columns(dh_mx, half), dh[:, part(half, PASS)])
+                quantize(wa_mx[0][:], wa_mx[1][:], wa_rounded)
+                for kt in range(K_TILES):
+                    second_product(dx_bank[kt][:, :C], *columns(wa_mx, kt), dh_mx[0][:], dh_mx[1][:])
 
-        before = LAST - 1
-        first_product_pass(LAST, 0, LAST_SHARES[0])
-        early = wb_raw[LAST, 0][:, 0, : C + P]
-        nc.scalar.copy(out=early, in_=dx_bank[before % 2][:, : C + P])
-        scatter_on_scalar(0, before * C, early[:, :C])
-        scatter_on_scalar(1, before * C, early[:, C:])
-        first_product_pass(LAST, 1, LAST_SHARES[1])
-        first_product_pass(LAST, 2, LAST_SHARES[2])
-        scatter_behind(wb_raw[LAST, 2], before, 1, P, P)
-        wa_tiles = [round_wa_on_scalar(LAST, kt) for kt in range(K_TILES)]
-        factor = make_factor(LAST)
-        dh, wa_mx, dh_mx = mx_tiles()
-
-        tile0_banks = [dx_bank[LAST % 2][:, :P], sums[0][:, 0, :]]
-        tile1_bank = dx_bank[before % 2]
-        tile0_dx = [keep("tile0_dx%d" % half, [P, P], F32) for half in range(HALVES)]
-        tile1_dx = keep("tile1_dx", [P, C], F32)
-
+        tile0_banks = [dx_bank[0][:, :P], sums[0][:, 0, :]]
         make_dh(0, factor, dh[:, :PASS])
         quantize(*columns(wa_mx, 0), wa_tiles[0])
         quantize(*columns(dh_mx, 0), dh[:, :PASS])
         second_product(tile0_banks[0], *columns(wa_mx, 0), *columns(dh_mx, 0))
-        nc.scalar.copy(out=tile0_dx[0][:], in_=tile0_banks[0])
-        scatter_on_scalar(0, LAST * C, tile0_dx[0][:])
+        scatter_on_scalar(0, LAST * C, tile0_banks[0])
 
         make_dh(1, factor, wa_tiles[0])
         quantize(*columns(wa_mx, 1), wa_tiles[1])
         quantize(*columns(dh_mx, 1), wa_tiles[0])
         second_product(tile0_banks[1], *columns(wa_mx, 0), *columns(dh_mx, 1))
-        for half in range(HALVES):
-            second_product(tile1_bank[:, part(half, P)], *columns(wa_mx, 1), *columns(dh_mx, half))
-        nc.vector.tensor_copy(out=tile0_dx[1][:], in_=tile0_banks[1])
-        scatter_on_vector(0, LAST * C + P, tile0_dx[1][:])
-        nc.scalar.copy(out=tile1_dx[:], in_=tile1_bank[:, :C])
-        scatter_on_scalar(1, LAST * C, tile1_dx[:])
+        second_product(dx_bank[1][:, :C], *columns(wa_mx, 1), dh_mx[0][:], dh_mx[1][:])
+        scatter_on_vector(0, LAST * C + P, tile0_banks[1])
+        scatter_on_scalar(1, LAST * C, dx_bank[1][:, :C])
 
-        for piece, (kt, cols) in enumerate(pieces):
+        for kt, h in halves:
+            cols = part(h, BANK)
             for s in range(PASSES):
                 nc.tensor.matmul_mx(
-                    out=base[piece][:],
+                    out=base[kt, h],
                     lhsT=wt_codes[:, s, part(kt, 2 * P)].bitcast(FP4X4),
                     lhsT_scale=wt_plane[:, s, part(kt, P)],
                     rhs=dy[s][:, cols].bitcast(FP8X4),
@@ -311,6 +309,9 @@ def tile_moe_adb_relu2_kernel(
                     start=(s == 0),
                     stop=(s == PASSES - 1),
                 )
-        for piece, (kt, cols) in enumerate(pieces):
-            nc.vector.tensor_tensor(out=window[kt][:, cols], in0=base[piece][:], in1=window[kt][:, cols], op=ALU.add)
-            nc.sync.dma_start(out=out[part(kt, P), cols], in_=window[kt][:, cols])
+        for kt in range(K_TILES):
+            for first, last in zip(STORE_CUTS[kt], STORE_CUTS[kt][1:]):
+                h, cols = first // BANK, slice(first, last)
+                in_bank = base[kt, h][:, first - h * BANK : last - h * BANK]
+                nc.vector.tensor_tensor(out=window[kt][:, cols], in0=in_bank, in1=window[kt][:, cols], op=ALU.add)
+                nc.sync.dma_start(out=out[part(kt, P), cols], in_=window[kt][:, cols])

@@ -33,8 +33,8 @@ LAST = E - 1
 
 FIRST_SHARES = ((0,), (0,), (64,))
 MIDDLE_SHARES = ((32,), (128,), (64,))
-LAST_SHARES = ((64,), (128,), (0, 32, 32))
-LAST_PIECES = (64, 32, 32)
+LAST_SHARES = ((64,), (128,), (0, 64))
+LAST_PIECES = (64, 64)
 STORE_CUTS = ((0, 128, 512, 1024), (0, 512, 896, 1024))
 
 
@@ -123,9 +123,8 @@ def tile_moe_adb_relu2_kernel(
                 if (e, s) not in wb_raw:
                     load_wb(e, s, LAST_PIECES if (e, s) == (LAST, PASSES - 1) else (P,))
             load_a(e)
-            load_wa(e, 0, K if e < LAST else P)
+            load_wa(e, 0, K)
         nc.sync.dma_start(out=wt_codes[:].bitcast(I32), in_=wt_words.rearrange("s p b -> p s b").bitcast(I32))
-        load_wa(LAST, P, K)
         load_planes(wt_plane, wt_scales)
         load_planes(dy_plane, dy_scales[1:])
 
@@ -184,7 +183,7 @@ def tile_moe_adb_relu2_kernel(
         def round_wa_on_gpsimd(e, rounded):
             nc.gpsimd.tensor_scalar(
                 out=rounded.rearrange("p (k t) -> p k t", t=PACK),
-                in0=wa_raw[e, 0][:].rearrange("p t k -> p k t"),
+                in0=wa_raw[e, 0][:, :, : rounded.shape[1] // PACK].rearrange("p t k -> p k t"),
                 scalar1=1.0,
                 scalar2=0.0,
                 op0=ALU.mult,
@@ -196,7 +195,7 @@ def tile_moe_adb_relu2_kernel(
             rounded = turn("wa_rounded", [P, PACK * P], BF16)
             nc.scalar.copy(
                 out=rounded[:].rearrange("p (c r t) -> p c t r", r=RUN, t=PACK),
-                in_=wa_raw[e, kt * P][:].rearrange("p t (c r) -> p c t r", r=RUN),
+                in_=wa_raw[e, 0][:, :, part(kt, P)].rearrange("p t (c r) -> p c t r", r=RUN),
             )
             return rounded[:]
 

@@ -27,14 +27,13 @@ K_TILES = K // P
 HALVES = C // P
 QUAD = 32
 ROWS = 4
-RUN = 4
 GATHER = T // 2
 LAST = E - 1
 
-FIRST_SHARES = ((0,), (0,), (64,))
+FIRST_SHARES = ((0,), (0,), (16,))
 MIDDLE_SHARES = ((32,), (128,), (64,))
-LAST_SHARES = ((64,), (128,), (0, 64))
-LAST_PIECES = (64, 64)
+LAST_SHARES = ((40,), (128,), (84,))
+LAST_PIECES = (128,)
 STORE_CUTS = ((0, 128, 512, 1024), (0, 512, 896, 1024))
 
 
@@ -92,9 +91,13 @@ def tile_moe_adb_relu2_kernel(
                 wb_raw[e, s].append(raw)
                 first = first + width
 
-        def load_a(e):
-            a_sb[e] = keep("a%d" % e, [P, PACK, C], F32)
-            nc.sync.dma_start(out=a_sb[e][:], in_=a.rearrange("(p t) j -> p t j", t=PACK)[:, :, part(e, C)])
+        def load_a(e, count):
+            columns = keep("a%d" % e, [P, PACK, count * C], F32)
+            nc.sync.dma_start(
+                out=columns[:], in_=a.rearrange("(p t) j -> p t j", t=PACK)[:, :, e * C : (e + count) * C]
+            )
+            for index in range(count):
+                a_sb[e + index] = columns[:, :, part(index, C)]
 
         def load_wa(e, first, last):
             wa_raw[e, first] = keep("wa_raw%d_%d" % (e, first), [P, PACK, last - first], F32)
@@ -102,7 +105,7 @@ def tile_moe_adb_relu2_kernel(
 
         def load_planes(planes, scales):
             for row in range(ROWS):
-                nc.gpsimd.dma_start(
+                nc.sync.dma_start(
                     out=planes[row:P:QUAD, :, :].bitcast(I32),
                     in_=scales[:, row::ROWS, :].rearrange("s q t -> q s t").bitcast(I32),
                 )
@@ -122,18 +125,19 @@ def tile_moe_adb_relu2_kernel(
             for s in range(PASSES):
                 if (e, s) not in wb_raw:
                     load_wb(e, s, LAST_PIECES if (e, s) == (LAST, PASSES - 1) else (P,))
-            load_a(e)
+                if (e, s) == (LAST, 0):
+                    load_planes(wt_plane, wt_scales)
+            if e not in a_sb:
+                load_a(e, 2 if e == 0 else 1)
             load_wa(e, 0, K)
         nc.sync.dma_start(out=wt_codes[:].bitcast(I32), in_=wt_words.rearrange("s p b -> p s b").bitcast(I32))
-        load_planes(wt_plane, wt_scales)
         load_planes(dy_plane, dy_scales[1:])
 
         sums = [psum.tile([P, PACK, P], F32, name="sums%d" % half) for half in range(HALVES)]
         dx_bank = [psum.tile([P, BANK], F32, name="dx_bank%d" % kt) for kt in range(K_TILES)]
         halves = [(kt, h) for kt in range(K_TILES) for h in range(T // BANK)]
-        base = {(0, h): psum.tile([P, BANK], F32, name="base%d" % h)[:] for h in range(T // BANK)}
-        base[1, 0], base[1, 1] = [sums[half][:].rearrange("p t c -> p (t c)") for half in (1, 0)]
-        gate_banks = [psum.tile([P, BANK], F32, name="gate%d" % h) for h in range(T // BANK)]
+        base = {key: psum.tile([P, BANK], F32, name="base%d_%d" % key)[:] for key in halves}
+        gate_banks = [base[K_TILES - 1, h] for h in range(T // BANK)]
 
         def spread_gate():
             gate_cols = keep("gate_cols", [P, T // P], F32)
@@ -180,24 +184,16 @@ def tile_moe_adb_relu2_kernel(
                     )
             return rounded
 
-        def round_wa_on_gpsimd(e, rounded):
+        def round_wa_on_gpsimd(e, rounded, first=0):
             nc.gpsimd.tensor_scalar(
                 out=rounded.rearrange("p (k t) -> p k t", t=PACK),
-                in0=wa_raw[e, 0][:, :, : rounded.shape[1] // PACK].rearrange("p t k -> p k t"),
+                in0=wa_raw[e, 0][:, :, first : first + rounded.shape[1] // PACK].rearrange("p t k -> p k t"),
                 scalar1=1.0,
                 scalar2=0.0,
                 op0=ALU.mult,
                 op1=ALU.add,
             )
             return rounded
-
-        def round_wa_on_scalar(e, kt):
-            rounded = turn("wa_rounded", [P, PACK * P], BF16)
-            nc.scalar.copy(
-                out=rounded[:].rearrange("p (c r t) -> p c t r", r=RUN, t=PACK),
-                in_=wa_raw[e, 0][:, :, part(kt, P)].rearrange("p t (c r) -> p c t r", r=RUN),
-            )
-            return rounded[:]
 
         def make_factor(e):
             factor = turn("factor", [P, PACK, C], F32)
@@ -267,7 +263,7 @@ def tile_moe_adb_relu2_kernel(
             if e < LAST:
                 wa_rounded = round_wa_on_gpsimd(e, spent[:, : PACK * K])
             else:
-                wa_tiles = [round_wa_on_gpsimd(e, spent[:, :PASS]), round_wa_on_scalar(e, 1)]
+                wa_tiles = [round_wa_on_gpsimd(e, spent[:, part(kt, PASS)], kt * P) for kt in range(K_TILES)]
             factor = make_factor(e)
             dh = turn("dh", [P, C * PACK], BF16)
             wa_mx = turn("wa_codes", [P, K], U32), turn("wa_plane", [P, K], U8)

@@ -27,13 +27,14 @@ K_TILES = K // P
 HALVES = C // P
 QUAD = 32
 ROWS = 4
+RUN = 4
 GATHER = T // 2
 LAST = E - 1
 
 FIRST_SHARES = ((0,), (0,), (16,))
 MIDDLE_SHARES = ((32,), (128,), (64,))
-LAST_SHARES = ((40,), (128,), (84,))
-LAST_PIECES = (128,)
+LAST_SHARES = ((56,), (128,), (0, 64))
+LAST_PIECES = (64, 64)
 STORE_CUTS = ((0, 128, 512, 1024), (0, 512, 896, 1024))
 
 
@@ -195,6 +196,14 @@ def tile_moe_adb_relu2_kernel(
             )
             return rounded
 
+        def round_wa_on_scalar(e, kt):
+            rounded = keep("wa_rounded", [P, PACK * P], BF16)
+            nc.scalar.copy(
+                out=rounded[:].rearrange("p (c r t) -> p c t r", r=RUN, t=PACK),
+                in_=wa_raw[e, 0][:, :, part(kt, P)].rearrange("p t (c r) -> p c t r", r=RUN),
+            )
+            return rounded[:]
+
         def make_factor(e):
             factor = turn("factor", [P, PACK, C], F32)
             for half in range(HALVES):
@@ -263,7 +272,7 @@ def tile_moe_adb_relu2_kernel(
             if e < LAST:
                 wa_rounded = round_wa_on_gpsimd(e, spent[:, : PACK * K])
             else:
-                wa_tiles = [round_wa_on_gpsimd(e, spent[:, part(kt, PASS)], kt * P) for kt in range(K_TILES)]
+                wa_tiles = [round_wa_on_gpsimd(e, spent[:, :PASS]), round_wa_on_scalar(e, 1)]
             factor = make_factor(e)
             dh = turn("dh", [P, C * PACK], BF16)
             wa_mx = turn("wa_codes", [P, K], U32), turn("wa_plane", [P, K], U8)

@@ -33,8 +33,8 @@ LAST = E - 1
 
 FIRST_SHARES = ((0,), (0,), (16,))
 MIDDLE_SHARES = ((32,), (128,), (64,))
-LAST_SHARES = ((56,), (128,), (0, 64))
-LAST_PIECES = (64, 64)
+LAST_SHARES = ((56,), (128,), (0, 32, 32))
+LAST_PIECES = (64, 32, 32)
 STORE_CUTS = ((0, 128, 512, 1024), (0, 512, 896, 1024))
 
 
@@ -130,8 +130,9 @@ def tile_moe_adb_relu2_kernel(
                     load_planes(wt_plane, wt_scales)
             if e not in a_sb:
                 load_a(e, 2 if e == 0 else 1)
-            load_wa(e, 0, K)
+            load_wa(e, 0, K if e < LAST else P)
         nc.sync.dma_start(out=wt_codes[:].bitcast(I32), in_=wt_words.rearrange("s p b -> p s b").bitcast(I32))
+        load_wa(LAST, P, K)
         load_planes(dy_plane, dy_scales[1:])
 
         sums = [psum.tile([P, PACK, P], F32, name="sums%d" % half) for half in range(HALVES)]
@@ -200,7 +201,7 @@ def tile_moe_adb_relu2_kernel(
             rounded = keep("wa_rounded", [P, PACK * P], BF16)
             nc.scalar.copy(
                 out=rounded[:].rearrange("p (c r t) -> p c t r", r=RUN, t=PACK),
-                in_=wa_raw[e, 0][:, :, part(kt, P)].rearrange("p t (c r) -> p c t r", r=RUN),
+                in_=wa_raw[e, kt * P][:].rearrange("p t (c r) -> p c t r", r=RUN),
             )
             return rounded[:]
 

@@ -31,7 +31,7 @@ RUN = 4
 GATHER = T // 2
 LAST = E - 1
 
-FIRST_SHARES = ((0,), (0,), (16,))
+FIRST_SHARES = ((0,), (0,), (96,))
 MIDDLE_SHARES = ((32,), (128,), (64,))
 LAST_SHARES = ((56,), (128,), (0, 32, 32))
 LAST_PIECES = (64, 32, 32)
@@ -60,7 +60,9 @@ def tile_moe_adb_relu2_kernel(
             return offsets[:, first // 16 : (first + count) // 16]
 
         offsets = held.tile([P, T // 16], U16, name="offsets")
-        dy = [keep("dy%d" % s, [P, T], I32) for s in range(PASSES)]
+        dy_first = keep("dy_first", [P, T], I32)
+        dy_rest = keep("dy_rest", [P, PASSES - 1, T], I32)
+        dy = [dy_first[:]] + [dy_rest[:, s, :] for s in range(PASSES - 1)]
         dy_packed = keep("dy_packed", [P, T], U8)
         dy_plane = keep("dy_plane", [P, PASSES - 1, T], U8)
         wt_codes = keep("wt_codes", [P, PASSES, 2 * K], U8)
@@ -79,8 +81,12 @@ def tile_moe_adb_relu2_kernel(
 
         wb_raw, wa_raw, a_sb = {}, {}, {}
 
-        def load_dy(s):
-            nc.sync.dma_start(out=dy[s][:], in_=dy_words[s].rearrange("p t d -> p (t d)").bitcast(I32))
+        def load_passes(e, first, count):
+            raw = keep("wb_raw%d_%d" % (e, first), [P, count, PACK * H], F32)
+            rows = wbt[e, first * PASS : (first + count) * PASS, :]
+            nc.sync.dma_start(out=raw[:], in_=rows.rearrange("(s p d) i -> p s (d i)", p=P, d=PACK))
+            for index in range(count):
+                wb_raw[e, first + index] = [raw[:, index, :].rearrange("p (d i) -> p d i", d=PACK)]
 
         def load_wb(e, s, widths=(P,)):
             rows = wbt[e, part(s, PASS), :].rearrange("(p d) i -> p d i", d=PACK)
@@ -89,7 +95,7 @@ def tile_moe_adb_relu2_kernel(
             for piece, width in enumerate(widths):
                 raw = keep("wb_raw%d_%d_%d" % (e, s, piece), [P, PACK, PACK * width], F32)
                 nc.sync.dma_start(out=raw[:], in_=rows[:, :, PACK * first : PACK * (first + width)])
-                wb_raw[e, s].append(raw)
+                wb_raw[e, s].append(raw[:])
                 first = first + width
 
         def load_a(e, count):
@@ -111,17 +117,17 @@ def tile_moe_adb_relu2_kernel(
                     in_=scales[:, row::ROWS, :].rearrange("s q t -> q s t").bitcast(I32),
                 )
 
-        load_dy(0)
+        nc.sync.dma_start(out=dy_first[:], in_=dy_words[0].rearrange("p t d -> p (t d)").bitcast(I32))
         nc.sync.dma_start(offsets[:], offs)
-        load_dy(1)
+        nc.sync.dma_start(out=dy_rest[:], in_=dy_words[1:].rearrange("s p t d -> p s (t d)").bitcast(I32))
         load_wb(0, 0)
-        load_dy(2)
         nc.sync.dma_start(out=gate_rows[: T // P, :], in_=gate[0, :].rearrange("(m p) -> m p", p=P))
         for quad in range(P // QUAD):
             nc.sync.dma_start(
                 out=dy_packed[QUAD * quad : QUAD * quad + ROWS * PASSES, :].bitcast(I32),
                 in_=dy_scales[:, part(quad, ROWS), :].bitcast(I32),
             )
+        load_passes(0, 1, 2)
         for e in range(E):
             for s in range(PASSES):
                 if (e, s) not in wb_raw:
@@ -163,7 +169,7 @@ def tile_moe_adb_relu2_kernel(
             words = rounded[:].rearrange("p (t m d) -> p m d t", t=PACK, d=PACK)
             first = 0
             for piece, on_vector in enumerate(shares):
-                raw = wb_raw[e, s][piece][:].rearrange("p d (m t) -> p m d t", t=PACK)
+                raw = wb_raw[e, s][piece].rearrange("p d (m t) -> p m d t", t=PACK)
                 width = raw.shape[1]
                 into = words[:, first : first + width]
                 first = first + width
@@ -245,12 +251,6 @@ def tile_moe_adb_relu2_kernel(
             nc.scalar.copy(out=values, in_=bank)
             nc.scalar.activation(window[kt][:].indirect(list_slice(first, count)), values, COPY)
 
-        def scatter_on_vector(kt, first, bank):
-            count = bank.shape[1]
-            values = keep("dx_last", [P, count], F32)
-            nc.vector.tensor_copy(out=values[:], in_=bank)
-            nc.vector.tensor_copy(window[kt][:].indirect(list_slice(first, count)), values[:])
-
         def spent_columns(e, s):
             raw = wb_raw[e, s][0]
             return raw[:, 0, raw.shape[2] - C :]
@@ -260,7 +260,7 @@ def tile_moe_adb_relu2_kernel(
 
         spread_gate()
         for s in range(PASSES):
-            gather(slot_words[s][:].bitcast(U32), dy[s][:].bitcast(U32))
+            gather(slot_words[s][:].bitcast(U32), dy[s].bitcast(U32))
         gather(slot_scales[:], dy_packed[:])
 
         for e in range(E):
@@ -287,20 +287,32 @@ def tile_moe_adb_relu2_kernel(
                 for kt in range(K_TILES):
                     second_product(dx_bank[kt][:, :C], *columns(wa_mx, kt), dh_mx[0][:], dh_mx[1][:])
 
-        tile0_banks = [dx_bank[0][:, :P], sums[0][:, 0, :]]
+        last_bank = {(kt, 0): dx_bank[kt][:, :P] for kt in range(K_TILES)}
+        last_bank.update({(kt, 1): sums[kt][:, 0, :] for kt in range(K_TILES)})
+        last_dx = {key: keep("last_dx%d_%d" % key, [P, P], F32)[:] for key in last_bank}
+
+        def last_window(kt, half):
+            return window[kt][:].indirect(list_slice(LAST * C + half * P, P))
+
         make_dh(0, factor, dh[:, :PASS])
         quantize(*columns(wa_mx, 0), wa_tiles[0])
         quantize(*columns(dh_mx, 0), dh[:, :PASS])
-        second_product(tile0_banks[0], *columns(wa_mx, 0), *columns(dh_mx, 0))
-        scatter_on_scalar(0, LAST * C, tile0_banks[0])
+        second_product(last_bank[0, 0], *columns(wa_mx, 0), *columns(dh_mx, 0))
+        nc.scalar.copy(out=last_dx[0, 0], in_=last_bank[0, 0])
+        nc.scalar.activation(last_window(0, 0), last_dx[0, 0], COPY)
 
         make_dh(1, factor, wa_tiles[0])
         quantize(*columns(wa_mx, 1), wa_tiles[1])
         quantize(*columns(dh_mx, 1), wa_tiles[0])
-        second_product(tile0_banks[1], *columns(wa_mx, 0), *columns(dh_mx, 1))
-        second_product(dx_bank[1][:, :C], *columns(wa_mx, 1), dh_mx[0][:], dh_mx[1][:])
-        scatter_on_vector(0, LAST * C + P, tile0_banks[1])
-        scatter_on_scalar(1, LAST * C, dx_bank[1][:, :C])
+        second_product(last_bank[1, 0], *columns(wa_mx, 1), *columns(dh_mx, 0))
+        second_product(last_bank[0, 1], *columns(wa_mx, 0), *columns(dh_mx, 1))
+        second_product(last_bank[1, 1], *columns(wa_mx, 1), *columns(dh_mx, 1))
+        nc.vector.tensor_copy(out=last_dx[1, 0], in_=last_bank[1, 0])
+        nc.vector.tensor_copy(out=last_dx[0, 1], in_=last_bank[0, 1])
+        nc.vector.tensor_copy(last_window(1, 0), last_dx[1, 0])
+        nc.scalar.activation(last_window(0, 1), last_dx[0, 1], COPY)
+        nc.scalar.copy(out=last_dx[1, 1], in_=last_bank[1, 1])
+        nc.scalar.activation(last_window(1, 1), last_dx[1, 1], COPY)
 
         for kt, h in halves:
             cols = part(h, BANK)

@@ -190,6 +190,17 @@ def tile_moe_adb_relu2_kernel(
                         start=(s == 0 and t == 0),
                         stop=(s == PASSES - 1 and t == PACK - 1),
                     )
+            if e == LAST:
+                for h in range(PASSES - 1 - s):
+                    nc.tensor.matmul_mx(
+                        out=base[0, h],
+                        lhsT=codes[:, :P].bitcast(FP8X4),
+                        lhsT_scale=plane[:, :P],
+                        rhs=slot_words[s][:, part(h, BANK)].bitcast(FP8X4),
+                        rhs_scale=slot_scales[ROWS * s :, part(h, BANK)],
+                        start=True,
+                        stop=True,
+                    )
             return rounded
 
         def round_wa_on_gpsimd(e, rounded, first=0):

from contextlib import ExitStack

import concourse.mybir as mybir
from concourse.masks import make_identity

K, T, E, C, H, N = 256, 1024, 4, 256, 512, 1536
FLOPS = 2 * N * K * T + 2 * E * C * (N * H + H * K)
BYTES = N * T + N * T // 32 + N * K // 2 + N * K // 32 + 4 * (E * N * H + E * H * K + H * T + T + K * T) + 2 * 8 * T

F32 = mybir.dt.float32
BF16 = mybir.dt.bfloat16
I32 = mybir.dt.int32
U32 = mybir.dt.uint32
U16 = mybir.dt.uint16
U8 = mybir.dt.uint8
FP8X4 = mybir.dt.float8_e4m3fn_x4
FP4X4 = mybir.dt.float4_e2m1fn_x4
ALU = mybir.AluOpType
COPY = mybir.ActivationFunctionType.Copy

P = 128
PACK = 4
PASS = P * PACK
PASSES = N // PASS
BANK = 512
K_TILES = K // P
HALVES = C // P
QUAD = 32
ROWS = 4
RUN = 4
GATHER = T // 2
LAST = E - 1

FIRST_SHARES = ((0,), (0,), (96,))
MIDDLE_SHARES = ((32,), (128,), (64,))
LAST_SHARES = ((56,), (128,), (0, 32, 32))
LAST_PIECES = (64, 32, 32)
STORE_CUTS = ((0, 128, 512, 1024), (0, 512, 896, 1024))


def tile_moe_adb_relu2_kernel(
    tc, dy_words, dy_scales, wt_words, wt_scales, wbt, wat, a, gate, offs, out
):
    nc = tc.nc
    with ExitStack() as ctx:
        held = ctx.enter_context(tc.tile_pool(name="held", bufs=1))
        ring = ctx.enter_context(tc.tile_pool(name="ring", bufs=2))
        psum = ctx.enter_context(tc.psum_pool(name="psum", bufs=1))

        def keep(name, shape, dtype):
            return held.tile(shape, dtype, name=name, align_bytes=64)

        def turn(name, shape, dtype):
            return ring.tile(shape, dtype, name=name, align_bytes=64)

        def part(index, width):
            return slice(index * width, (index + 1) * width)

        def list_slice(first, count):
            return offsets[:, first // 16 : (first + count) // 16]

        offsets = held.tile([P, T // 16], U16, name="offsets")
        dy_first = keep("dy_first", [P, T], I32)
        dy_rest = keep("dy_rest", [P, PASSES - 1, T], I32)
        dy = [dy_first[:]] + [dy_rest[:, s, :] for s in range(PASSES - 1)]
        dy_packed = keep("dy_packed", [P, T], U8)
        dy_plane = keep("dy_plane", [P, PASSES - 1, T], U8)
        wt_codes = keep("wt_codes", [P, PASSES, 2 * K], U8)
        wt_plane = keep("wt_plane", [P, PASSES, K], U8)
        slot_words = [keep("slot_words%d" % s, [P, E * C], I32) for s in range(PASSES)]
        slot_scales = keep("slot_scales", [P, E * C], U8)
        window = [keep("window%d" % kt, [P, T], F32) for kt in range(K_TILES)]
        gate_rows = keep("gate_rows", [P, P], F32)
        identity = keep("identity", [P, P], F32)

        nc.vector.memset(dy_packed[:].bitcast(I32), 0)
        nc.vector.memset(gate_rows[:], 0.0)
        make_identity(nc, identity[:])
        nc.gpsimd.memset(dy_plane[:].rearrange("p s t -> p (s t)").bitcast(I32), 0)
        nc.gpsimd.memset(wt_plane[:].rearrange("p s k -> p (s k)").bitcast(I32), 0)

        wb_raw, wa_raw, a_sb = {}, {}, {}

        def load_passes(e, first, count):
            raw = keep("wb_raw%d_%d" % (e, first), [P, count, PACK * H], F32)
            rows = wbt[e, first * PASS : (first + count) * PASS, :]
            nc.sync.dma_start(out=raw[:], in_=rows.rearrange("(s p d) i -> p s (d i)", p=P, d=PACK))
            for index in range(count):
                wb_raw[e, first + index] = [raw[:, index, :].rearrange("p (d i) -> p d i", d=PACK)]

        def load_wb(e, s, widths=(P,)):
            rows = wbt[e, part(s, PASS), :].rearrange("(p d) i -> p d i", d=PACK)
            wb_raw[e, s] = []
            first = 0
            for piece, width in enumerate(widths):
                raw = keep("wb_raw%d_%d_%d" % (e, s, piece), [P, PACK, PACK * width], F32)
                nc.sync.dma_start(out=raw[:], in_=rows[:, :, PACK * first : PACK * (first + width)])
                wb_raw[e, s].append(raw[:])
                first = first + width

        def load_a(e, count):
            columns = keep("a%d" % e, [P, PACK, count * C], F32)
            nc.sync.dma_start(
                out=columns[:], in_=a.rearrange("(p t) j -> p t j", t=PACK)[:, :, e * C : (e + count) * C]
            )
            for index in range(count):
                a_sb[e + index] = columns[:, :, part(index, C)]

        def load_wa(e, first, last):
            wa_raw[e, first] = keep("wa_raw%d_%d" % (e, first), [P, PACK, last - first], F32)
            nc.sync.dma_start(out=wa_raw[e, first][:], in_=wat[e].rearrange("(p t) k -> p t k", t=PACK)[:, :, first:last])

        def load_planes(planes, scales):
            for row in range(ROWS):
                nc.sync.dma_start(
                    out=planes[row:P:QUAD, :, :].bitcast(I32),
                    in_=scales[:, row::ROWS, :].rearrange("s q t -> q s t").bitcast(I32),
                )

        nc.sync.dma_start(out=dy_first[:], in_=dy_words[0].rearrange("p t d -> p (t d)").bitcast(I32))
        nc.sync.dma_start(offsets[:], offs)
        nc.sync.dma_start(out=dy_rest[:], in_=dy_words[1:].rearrange("s p t d -> p s (t d)").bitcast(I32))
        load_wb(0, 0)
        nc.sync.dma_start(out=gate_rows[: T // P, :], in_=gate[0, :].rearrange("(m p) -> m p", p=P))
        for quad in range(P // QUAD):
            nc.sync.dma_start(
                out=dy_packed[QUAD * quad : QUAD * quad + ROWS * PASSES, :].bitcast(I32),
                in_=dy_scales[:, part(quad, ROWS), :].bitcast(I32),
            )
        load_passes(0, 1, 2)
        for e in range(E):
            for s in range(PASSES):
                if (e, s) not in wb_raw:
                    load_wb(e, s, LAST_PIECES if (e, s) == (LAST, PASSES - 1) else (P,))
                if (e, s) == (LAST, 0):
                    load_planes(wt_plane, wt_scales)
            if e not in a_sb:
                load_a(e, 2 if e == 0 else 1)
            load_wa(e, 0, K if e < LAST else P)
        nc.sync.dma_start(out=wt_codes[:].bitcast(I32), in_=wt_words.rearrange("s p b -> p s b").bitcast(I32))
        load_wa(LAST, P, K)
        load_planes(dy_plane, dy_scales[1:])

        sums = [psum.tile([P, PACK, P], F32, name="sums%d" % half) for half in range(HALVES)]
        dx_bank = [psum.tile([P, BANK], F32, name="dx_bank%d" % kt) for kt in range(K_TILES)]
        halves = [(kt, h) for kt in range(K_TILES) for h in range(T // BANK)]
        base = {key: psum.tile([P, BANK], F32, name="base%d_%d" % key)[:] for key in halves}
        gate_banks = [base[K_TILES - 1, h] for h in range(T // BANK)]

        def spread_gate():
            gate_cols = keep("gate_cols", [P, T // P], F32)
            nc.tensor.transpose(base[0, 0][:, :P], gate_rows[:], identity[:])
            nc.scalar.mul(gate_cols[:], base[0, 0][:, : T // P], 2.0)
            for column in range(T // P):
                h, m = divmod(column, BANK // P)
                spread = gate_cols[:, column : column + 1].to_broadcast([P, P])
                nc.tensor.transpose(gate_banks[h][:, part(m, P)], spread, identity[:])

        def gather(into, source):
            for first in range(0, E * C, GATHER):
                nc.vector.tensor_copy(into[:, first : first + GATHER], source.indirect(list_slice(first, GATHER)))

        def quantize(codes, plane, values):
            nc.vector.quantize_mx(out=codes.bitcast(FP8X4), scales=plane, in_=values)

        def first_product_pass(e, s, shares):
            rounded = turn("rounded", [P, PACK * H], BF16)
            codes, plane = turn("wb_codes", [P, H], U32), turn("wb_plane", [P, H], U8)
            words = rounded[:].rearrange("p (t m d) -> p m d t", t=PACK, d=PACK)
            first = 0
            for piece, on_vector in enumerate(shares):
                raw = wb_raw[e, s][piece].rearrange("p d (m t) -> p m d t", t=PACK)
                width = raw.shape[1]
                into = words[:, first : first + width]
                first = first + width
                if on_vector > 0:
                    nc.vector.tensor_copy(out=into[:, :on_vector], in_=raw[:, :on_vector])
                if on_vector < width:
                    nc.scalar.copy(out=into[:, on_vector:], in_=raw[:, on_vector:])
            quantize(codes[:], plane[:], rounded[:])
            for half in range(HALVES):
                cols = part(e * HALVES + half, P)
                for t in range(PACK):
                    nc.tensor.matmul_mx(
                        out=sums[half][:, t, :],
                        lhsT=codes[:, part(t, P)].bitcast(FP8X4),
                        lhsT_scale=plane[:, part(t, P)],
                        rhs=slot_words[s][:, cols].bitcast(FP8X4),
                        rhs_scale=slot_scales[ROWS * s :, cols],
                        start=(s == 0 and t == 0),
                        stop=(s == PASSES - 1 and t == PACK - 1),
                    )
            if e == LAST:
                for h in range(PASSES - 1 - s):
                    nc.tensor.matmul_mx(
                        out=base[0, h],
                        lhsT=codes[:, :P].bitcast(FP8X4),
                        lhsT_scale=plane[:, :P],
                        rhs=slot_words[s][:, part(h, BANK)].bitcast(FP8X4),
                        rhs_scale=slot_scales[ROWS * s :, part(h, BANK)],
                        start=True,
                        stop=True,
                    )
            return rounded

        def round_wa_on_gpsimd(e, rounded, first=0):
            nc.gpsimd.tensor_scalar(
                out=rounded.rearrange("p (k t) -> p k t", t=PACK),
                in0=wa_raw[e, 0][:, :, first : first + rounded.shape[1] // PACK].rearrange("p t k -> p k t"),
                scalar1=1.0,
                scalar2=0.0,
                op0=ALU.mult,
                op1=ALU.add,
            )
            return rounded

        def round_wa_on_scalar(e, kt):
            rounded = keep("wa_rounded", [P, PACK * P], BF16)
            nc.scalar.copy(
                out=rounded[:].rearrange("p (c r t) -> p c t r", r=RUN, t=PACK),
                in_=wa_raw[e, kt * P][:].rearrange("p t (c r) -> p c t r", r=RUN),
            )
            return rounded[:]

        def make_factor(e):
            factor = turn("factor", [P, PACK, C], F32)
            for half in range(HALVES):
                h, m = divmod(e * HALVES + half, BANK // P)
                nc.vector.scalar_tensor_tensor(
                    out=factor[:, :, part(half, P)],
                    in0=a_sb[e][:, :, part(half, P)],
                    scalar=0.0,
                    in1=gate_banks[h][:, part(m, P)].unsqueeze(1).to_broadcast([P, PACK, P]),
                    op0=ALU.max,
                    op1=ALU.mult,
                )
            return factor

        def make_dh(half, factor, values):
            nc.vector.tensor_tensor(
                out=values.rearrange("p (c r t) -> p c t r", r=2, t=PACK),
                in0=sums[half][:].rearrange("p t (c r) -> p c t r", r=2),
                in1=factor[:, :, part(half, P)].rearrange("p t (c r) -> p c t r", r=2),
                op=ALU.mult,
            )

        def second_product(bank, wa_codes, wa_plane, dh_codes, dh_plane):
            nc.tensor.matmul_mx(
                out=bank,
                lhsT=wa_codes.bitcast(FP8X4),
                lhsT_scale=wa_plane,
                rhs=dh_codes.bitcast(FP8X4),
                rhs_scale=dh_plane,
                start=True,
                stop=True,
            )

        def scatter_on_scalar(kt, first, bank, values=None):
            count = bank.shape[1]
            if values is None:
                values = turn("dx%d" % count, [P, count], F32)[:]
            nc.scalar.copy(out=values, in_=bank)
            nc.scalar.activation(window[kt][:].indirect(list_slice(first, count)), values, COPY)

        def spent_columns(e, s):
            raw = wb_raw[e, s][0]
            return raw[:, 0, raw.shape[2] - C :]

        def columns(mx, index):
            return [tile[:, part(index, P)] for tile in mx]

        spread_gate()
        for s in range(PASSES):
            gather(slot_words[s][:].bitcast(U32), dy[s].bitcast(U32))
        gather(slot_scales[:], dy_packed[:])

        for e in range(E):
            shares = FIRST_SHARES if e == 0 else LAST_SHARES if e == LAST else MIDDLE_SHARES
            for s in range(PASSES):
                spent = first_product_pass(e, s, shares[s])
                if e > 0 and s != 1:
                    kt = s // 2
                    scatter_on_scalar(kt, (e - 1) * C, dx_bank[kt][:, :C], spent_columns(e, s))
            if e < LAST:
                wa_rounded = round_wa_on_gpsimd(e, spent[:, : PACK * K])
            else:
                wa_tiles = [round_wa_on_gpsimd(e, spent[:, :PASS]), round_wa_on_scalar(e, 1)]
            factor = make_factor(e)
            dh = turn("dh", [P, C * PACK], BF16)
            wa_mx = turn("wa_codes", [P, K], U32), turn("wa_plane", [P, K], U8)
            dh_mx = turn("dh_codes", [P, C], U32), turn("dh_plane", [P, C], U8)
            if e < LAST:
                for half in range(HALVES):
                    make_dh(half, factor, dh[:, part(half, PASS)])
                for half in range(HALVES):
                    quantize(*columns(dh_mx, half), dh[:, part(half, PASS)])
                quantize(wa_mx[0][:], wa_mx[1][:], wa_rounded)
                for kt in range(K_TILES):
                    second_product(dx_bank[kt][:, :C], *columns(wa_mx, kt), dh_mx[0][:], dh_mx[1][:])

        last_bank = {(kt, 0): dx_bank[kt][:, :P] for kt in range(K_TILES)}
        last_bank.update({(kt, 1): sums[kt][:, 0, :] for kt in range(K_TILES)})
        last_dx = {key: keep("last_dx%d_%d" % key, [P, P], F32)[:] for key in last_bank}

        def last_window(kt, half):
            return window[kt][:].indirect(list_slice(LAST * C + half * P, P))

        make_dh(0, factor, dh[:, :PASS])
        quantize(*columns(wa_mx, 0), wa_tiles[0])
        quantize(*columns(dh_mx, 0), dh[:, :PASS])
        second_product(last_bank[0, 0], *columns(wa_mx, 0), *columns(dh_mx, 0))
        nc.scalar.copy(out=last_dx[0, 0], in_=last_bank[0, 0])
        nc.scalar.activation(last_window(0, 0), last_dx[0, 0], COPY)

        make_dh(1, factor, wa_tiles[0])
        quantize(*columns(wa_mx, 1), wa_tiles[1])
        quantize(*columns(dh_mx, 1), wa_tiles[0])
        second_product(last_bank[1, 0], *columns(wa_mx, 1), *columns(dh_mx, 0))
        second_product(last_bank[0, 1], *columns(wa_mx, 0), *columns(dh_mx, 1))
        second_product(last_bank[1, 1], *columns(wa_mx, 1), *columns(dh_mx, 1))
        nc.vector.tensor_copy(out=last_dx[1, 0], in_=last_bank[1, 0])
        nc.vector.tensor_copy(out=last_dx[0, 1], in_=last_bank[0, 1])
        nc.vector.tensor_copy(last_window(1, 0), last_dx[1, 0])
        nc.scalar.activation(last_window(0, 1), last_dx[0, 1], COPY)
        nc.scalar.copy(out=last_dx[1, 1], in_=last_bank[1, 1])
        nc.scalar.activation(last_window(1, 1), last_dx[1, 1], COPY)

        for kt, h in halves:
            cols = part(h, BANK)
            for s in range(PASSES):
                nc.tensor.matmul_mx(
                    out=base[kt, h],
                    lhsT=wt_codes[:, s, part(kt, 2 * P)].bitcast(FP4X4),
                    lhsT_scale=wt_plane[:, s, part(kt, P)],
                    rhs=dy[s][:, cols].bitcast(FP8X4),
                    rhs_scale=dy_packed[:, cols] if s == 0 else dy_plane[:, s - 1, cols],
                    start=(s == 0),
                    stop=(s == PASSES - 1),
                )
        for kt in range(K_TILES):
            for first, last in zip(STORE_CUTS[kt], STORE_CUTS[kt][1:]):
                h, cols = first // BANK, slice(first, last)
                in_bank = base[kt, h][:, first - h * BANK : last - h * BANK]
                nc.vector.tensor_tensor(out=window[kt][:, cols], in0=in_bank, in1=window[kt][:, cols], op=ALU.add)
                nc.sync.dma_start(out=out[part(kt, P), cols], in_=window[kt][:, cols])
